import numpy as np
import ml_dtypes


def mxq(x, axis, fmt="e4m3"):
    dtype, down = {"e4m3": (ml_dtypes.float8_e4m3fn, 7), "e5m2": (ml_dtypes.float8_e5m2, 14)}[fmt]
    v = np.moveaxis(np.asarray(x, np.float32).astype(ml_dtypes.bfloat16).astype(np.float64), axis, -1)
    blocks = v.reshape(v.shape[:-1] + (-1, 32))
    amax = np.abs(blocks).max(-1, keepdims=True)
    byte = np.maximum(np.where(amax > 0, np.frexp(amax)[1] - 1 + 127, 0) - down, 1)
    scale = np.exp2(byte - 127.0)
    codes = (blocks / scale).astype(np.float32).astype(dtype).astype(np.float64)
    return np.moveaxis((codes * scale).reshape(v.shape), -1, axis)


WIDE = False


def mx_kscale(k):
    if not WIDE:
        return np.ones(k)
    levels = np.array([30, -30])
    if k % 512:
        return np.exp2(np.random.permutation(np.resize(levels, k // 32))).repeat(32)
    a = np.empty((k // 512, 16))
    for p in range(k // 512):
        a[p, :8] = np.random.permutation(np.resize(levels, 8))
        for g in range(8):
            far = levels[np.abs(levels - a[p, g]) >= 10]
            a[p, g + 8] = far[np.random.randint(len(far))]
    return np.exp2(a.ravel()).repeat(32)


def f64(x):
    return np.asarray(x).astype(np.float64)


E2M1 = np.array([0.0, 0.5, 1.0, 1.5, 2.0, 3.0, 4.0, 6.0, -0.0, -0.5, -1.0, -1.5, -2.0, -3.0, -4.0, -6.0])


def pack_weight(w, fmt):
    k, n = w.shape
    w = f64(np.asarray(w, np.float32).astype(ml_dtypes.bfloat16)).reshape(k // 32, 32, n)
    amax = np.abs(w).max(1)
    if fmt == "e4m3":
        byte = np.frexp(amax)[1] - 1 + 127 - 7
    else:
        mant, ex = np.frexp(amax / 6.0)
        byte = np.where(mant > 0.5, ex, ex - 1) + 127
    byte = np.clip(np.where(amax > 0, byte, 1), 1, 254)
    scaled = (w * np.exp2(127.0 - byte)[:, None, :]).reshape(k, n).astype(np.float32)
    by_word = np.ascontiguousarray(scaled.reshape(k // 512, 128, 4, n).transpose(0, 1, 3, 2))
    if fmt == "e4m3":
        words = by_word.astype(ml_dtypes.float8_e4m3fn).view(np.uint8)
    else:
        c = by_word.astype(ml_dtypes.float4_e2m1fn).view(np.uint8) & 0xF
        words = (c[..., 0::2] | (c[..., 1::2] << 4)).reshape(k // 512, 128, 2 * n)
    return np.ascontiguousarray(words), np.ascontiguousarray(byte.astype(np.uint8).reshape(k // 512, 16, n))


def unpack_weight(words, scales, fmt):
    g, _, n = scales.shape
    words = np.ascontiguousarray(words).reshape(g, 128, n, -1)
    if fmt == "e4m3":
        vals = words.view(ml_dtypes.float8_e4m3fn).astype(np.float64)
    else:
        nib = np.empty((g, 128, n, 4), np.uint8)
        nib[..., 0::2] = words & 0xF
        nib[..., 1::2] = words >> 4
        vals = E2M1[nib]
    vals = vals * np.repeat(np.exp2(scales.astype(np.float64) - 127.0), 8, axis=1)[..., None]
    return vals.transpose(0, 1, 3, 2).reshape(g * 512, n)


def planes(y):
    n, m = y.shape
    v = y.astype(np.float32).astype(ml_dtypes.bfloat16).astype(np.float64).reshape(n // 32, 32, m)
    top = np.abs(v).max(1)
    byte = np.clip(np.where(top > 0, np.frexp(top)[1] - 1 + 127 - 7, 1), 1, 254)
    codes = (v * np.exp2(127.0 - byte)[:, None, :]).reshape(n, m).astype(np.float32).astype(ml_dtypes.float8_e4m3fn).view(np.uint8)
    words = codes.reshape(n // 512, 128, 4, m).transpose(0, 1, 3, 2)
    return np.ascontiguousarray(words), np.ascontiguousarray(byte.astype(np.uint8).reshape(n // 512, 16, m))


O, K, M, T = 512, 1024, 1536, 1536


def setup_inputs():
    n = np.random.standard_normal
    s = mx_kscale(K)[:, None]
    dy = np.exp(0.5 * n((1, T))) * n((K, T))
    w = n((K, M)) / np.sqrt(K) / s
    p_w8 = pack_weight(w[:O], "e4m3")
    p_w4 = pack_weight(w[O:], "e2m1")
    return {
        "dy": (dy * s).astype(np.float32),
        "w8_words": p_w8[0],
        "w8_scales": p_w8[1],
        "w4_words": p_w4[0],
        "w4_scales": p_w4[1],
    }


def reference(dy, w8_words, w8_scales, w4_words, w4_scales):
    dy_ = mxq(f64(dy), 0, "e5m2")
    w8_ = unpack_weight(w8_words, w8_scales, "e4m3")
    w4_ = unpack_weight(w4_words, w4_scales, "e2m1")
    y = w8_.T @ dy_[:O] + w4_.T @ dy_[O:]
    out_0 = y
    return (out_0,) + planes(out_0)

@@ -1,0 +1,190 @@
+from contextlib import ExitStack
+
+import concourse.mybir as mybir
+
+K, D, T = 1024, 1536, 1536
+FLOPS = 2 * K * D * T
+
+F32 = mybir.dt.float32
+BF16 = mybir.dt.bfloat16
+I32 = mybir.dt.int32
+U8 = mybir.dt.uint8
+E4M3 = mybir.dt.float8_e4m3fn_x4
+E5M2 = mybir.dt.float8_e5m2_x4
+E2M1 = mybir.dt.float4_e2m1fn_x4
+
+P = 128
+PACK = 4
+SPAN = P * PACK
+N = 512
+N_A = D // SPAN
+N_C = T // N
+RUN = 4
+
+
+def tile_mix_dyq_fm_pl_none_kernel(tc, dy, w8_words, w8_scales, w4_words, w4_scales, out_0, out_1, out_2):
+    nc = tc.nc
+    with ExitStack() as ctx:
+        keep = ctx.enter_context(tc.tile_pool(name="keep", bufs=1))
+        stage = ctx.enter_context(tc.tile_pool(name="stage", bufs=4))
+        psum = ctx.enter_context(tc.psum_pool(name="psum", bufs=8))
+        ctx.enter_context(tc.manual_schedule())
+
+        w8_raw = keep.tile([P, D], I32, align_bytes=64)
+        w4_raw = keep.tile([P, 2 * D], U8, align_bytes=64)
+        ws_raw = keep.tile([P, 2, D], U8, align_bytes=64)
+        w8 = keep.tile([P, D], I32, align_bytes=64)
+        w4 = keep.tile([P, 2 * D], U8, align_bytes=64)
+        ws = keep.tile([P, 2, D], U8, align_bytes=64)
+        dy_raw, dy_codes, dy_scales, result, out_codes = {}, {}, {}, {}, {}
+        for c in range(N_C):
+            for g in range(2):
+                dy_raw[c, g] = keep.tile([P, PACK, N], F32, name="dy_raw_%d_%d" % (c, g), align_bytes=64)
+                dy_codes[c, g] = keep.tile([P, N], I32, name="dy_codes_%d_%d" % (c, g), align_bytes=64)
+                dy_scales[c, g] = keep.tile([P, N], U8, name="dy_scales_%d_%d" % (c, g), align_bytes=64)
+            for a in range(N_A):
+                result[c, a] = keep.tile([P, PACK, N], F32, name="result_%d_%d" % (c, a), align_bytes=64)
+            out_codes[c] = keep.tile([P, N_A, N], I32, name="out_codes_%d" % c, align_bytes=64)
+        out_scales = keep.tile([P, N_A, T], U8, align_bytes=64)
+
+        def load_dy(c, g):
+            rows = dy[g * SPAN : (g + 1) * SPAN, c * N : (c + 1) * N]
+            nc.sync.dma_start(out=dy_raw[c, g][:], in_=rows.rearrange("(p j) t -> p j t", j=PACK))
+
+        def load_scales(engine, s, scales):
+            for q in range(4):
+                engine.dma_start(
+                    out=ws_raw[32 * q : 32 * q + 4, s, :].bitcast(I32),
+                    in_=scales[0, 4 * q : 4 * q + 4, :].bitcast(I32),
+                )
+
+        nc.vector.memset(ws_raw[:].rearrange("p s d -> p (s d)").bitcast(I32), 0)
+        nc.sync.dma_start(out=w8_raw[:], in_=w8_words[0].rearrange("p d i -> p (d i)").bitcast(I32))
+        nc.sync.dma_start(out=w4_raw[:].bitcast(I32), in_=w4_words[0].bitcast(I32))
+        load_dy(0, 0)
+        load_dy(0, 1)
+        load_scales(nc.scalar, 0, w8_scales)
+        load_scales(nc.gpsimd, 1, w4_scales)
+        for c in range(1, N_C):
+            load_dy(c, 0)
+            load_dy(c, 1)
+
+        nc.vector.tensor_copy(
+            out=w8[:].rearrange("p (a r c i) -> p a c r i", a=N_A, r=PACK, i=4),
+            in_=w8_raw[:].rearrange("p (a c i r) -> p a c r i", a=N_A, r=PACK, i=4),
+        )
+        for a in range(N_A):
+            cols = slice(2 * a * SPAN, 2 * (a + 1) * SPAN)
+            nc.vector.tensor_copy(
+                out=w4[:, cols].rearrange("p (r c i b) -> p c r i b", r=PACK, i=8, b=2),
+                in_=w4_raw[:, cols].rearrange("p (c i r b) -> p c r i b", r=PACK, i=8, b=2),
+            )
+        for a in range(N_A):
+            cols = slice(a * SPAN, (a + 1) * SPAN)
+            nc.vector.tensor_copy(
+                out=ws[:, :, cols].rearrange("p s (r c i) -> p s c r i", r=PACK, i=16),
+                in_=ws_raw[:, :, cols].rearrange("p s (c i r) -> p s c r i", r=PACK, i=16),
+            )
+
+        grouped = {}
+
+        def interleave(key, src, on_scalar=False):
+            tile = stage.tile([P, N, PACK], BF16, name="grouped", align_bytes=64)
+            grouped[key] = tile
+            dst_v = tile[:].rearrange("p (c i) j -> p c j i", i=RUN)
+            src_v = src[:].rearrange("p j (c i) -> p c j i", i=RUN)
+            if on_scalar:
+                nc.scalar.copy(out=dst_v, in_=src_v)
+            else:
+                nc.vector.tensor_copy(out=dst_v, in_=src_v)
+
+        def group_dy(c, g, on_scalar=False):
+            interleave(("dy", c, g), dy_raw[c, g], on_scalar)
+
+        def quant_dy(c, g):
+            nc.vector.quantize_mx(
+                out=dy_codes[c, g][:].bitcast(E5M2),
+                scales=dy_scales[c, g][:],
+                in_=grouped["dy", c, g][:].rearrange("p t j -> p (t j)"),
+            )
+
+        def multiply(c, a):
+            for r in range(PACK):
+                m0 = a * SPAN + r * P
+                acc = psum.tile([P, N], F32, name="acc")
+                nc.tensor.matmul_mx(
+                    out=acc[:],
+                    lhsT=w8[:, m0 : m0 + P].bitcast(E4M3),
+                    lhsT_scale=ws[:, 0, m0 : m0 + P],
+                    rhs=dy_codes[c, 0][:].bitcast(E5M2),
+                    rhs_scale=dy_scales[c, 0][:],
+                    start=True,
+                    stop=False,
+                )
+                nc.tensor.matmul_mx(
+                    out=acc[:],
+                    lhsT=w4[:, 2 * m0 : 2 * (m0 + P)].bitcast(E2M1),
+                    lhsT_scale=ws[:, 1, m0 : m0 + P],
+                    rhs=dy_codes[c, 1][:].bitcast(E5M2),
+                    rhs_scale=dy_scales[c, 1][:],
+                    start=False,
+                    stop=True,
+                )
+                nc.scalar.copy(out=result[c, a][:, r, :], in_=acc[:])
+
+        def group_out(c, a):
+            interleave(("out", c, a), result[c, a])
+
+        def quant_out(c, a):
+            nc.vector.quantize_mx(
+                out=out_codes[c][:, a, :].bitcast(E4M3),
+                scales=out_scales[:, a, c * N : (c + 1) * N],
+                in_=grouped["out", c, a][:].rearrange("p t j -> p (t j)"),
+            )
+
+        def store_result(c, a):
+            rows = out_0[a * SPAN : (a + 1) * SPAN, c * N : (c + 1) * N]
+            nc.sync.dma_start(out=rows.rearrange("(p r) t -> p r t", r=PACK), in_=result[c, a][:])
+
+        def store_codes(c):
+            words = out_1[:, :, c * N : (c + 1) * N, :].rearrange("a p t i -> p a (t i)")
+            nc.sync.dma_start(out=words.bitcast(I32), in_=out_codes[c][:])
+
+        def store_scales():
+            for q in range(4):
+                nc.scalar.dma_start(
+                    out=out_2[:, 4 * q : 4 * q + 4, :].rearrange("a r t -> r a t").bitcast(I32),
+                    in_=out_scales[32 * q : 32 * q + 4, :, :].bitcast(I32),
+                )
+
+        group_dy(0, 0, on_scalar=True)
+        group_dy(0, 1)
+        quant_dy(0, 0)
+        quant_dy(0, 1)
+        multiply(0, 0)
+        group_dy(1, 0)
+        group_dy(1, 1)
+        quant_dy(1, 0)
+        quant_dy(1, 1)
+        multiply(0, 1)
+        group_out(0, 0)
+        group_dy(2, 0)
+        quant_out(0, 0)
+        group_dy(2, 1)
+        quant_dy(2, 0)
+        group_out(0, 1)
+        quant_dy(2, 1)
+        store_result(0, 0)
+        store_result(0, 1)
+        groups = [(c, a) for c in range(N_C) for a in range(N_A)]
+        for i in range(2, len(groups)):
+            multiply(*groups[i])
+            group_out(*groups[i])
+            quant_out(*groups[i - 1])
+            if i == len(groups) - 1:
+                quant_out(*groups[i])
+                store_codes(N_C - 1)
+            store_result(*groups[i])
+            if i in (4, 6):
+                store_codes(i // 2 - 2)
+        store_scales()

@@ -20,86 +20,99 @@ N = 512
 N_A = D // SPAN
 N_C = T // N
 RUN = 4
+DY_PARTS = (((0, 1), (1, 2), (2, 3)), ((0, 1), (1, 2), (2, 3)))
+OUT_PARTS = (((0, 1), (1, 3)), ((0, 2), (2, 3)), ((0, 3),))
 
 
 def tile_mix_dyq_fm_pl_none_kernel(tc, dy, w8_words, w8_scales, w4_words, w4_scales, out_0, out_1, out_2):
     nc = tc.nc
     with ExitStack() as ctx:
         keep = ctx.enter_context(tc.tile_pool(name="keep", bufs=1))
-        stage = ctx.enter_context(tc.tile_pool(name="stage", bufs=4))
+        stage = ctx.enter_context(tc.tile_pool(name="stage", bufs=5))
         psum = ctx.enter_context(tc.psum_pool(name="psum", bufs=8))
         ctx.enter_context(tc.manual_schedule())
 
-        w8_raw = keep.tile([P, D], I32, align_bytes=64)
-        w4_raw = keep.tile([P, 2 * D], U8, align_bytes=64)
-        ws_raw = keep.tile([P, 2, D], U8, align_bytes=64)
-        w8 = keep.tile([P, D], I32, align_bytes=64)
-        w4 = keep.tile([P, 2 * D], U8, align_bytes=64)
-        ws = keep.tile([P, 2, D], U8, align_bytes=64)
-        dy_raw, dy_codes, dy_scales, result, out_codes = {}, {}, {}, {}, {}
-        for c in range(N_C):
-            for g in range(2):
-                dy_raw[c, g] = keep.tile([P, PACK, N], F32, name="dy_raw_%d_%d" % (c, g), align_bytes=64)
+        w8_raw = keep.tile([P, D], I32, name="w8_raw", align_bytes=64)
+        w4_raw = keep.tile([P, 2 * D], U8, name="w4_raw", align_bytes=64)
+        ws_raw = keep.tile([P, 2, D], U8, name="ws_raw", align_bytes=64)
+        w8 = keep.tile([P, D], I32, name="w8", align_bytes=64)
+        w4 = keep.tile([P, 2 * D], U8, name="w4", align_bytes=64)
+        ws = keep.tile([P, 2, D], U8, name="ws", align_bytes=64)
+        dy_raw, dy_codes, dy_scales, result, out_codes, out_scales = {}, {}, {}, {}, {}, {}
+        for g in range(2):
+            for c0, c1 in DY_PARTS[g]:
+                dy_raw[g, c0] = keep.tile([P, PACK, (c1 - c0) * N], F32, name="dy_raw_%d_%d" % (g, c0), align_bytes=64)
+            for c in range(N_C):
                 dy_codes[c, g] = keep.tile([P, N], I32, name="dy_codes_%d_%d" % (c, g), align_bytes=64)
                 dy_scales[c, g] = keep.tile([P, N], U8, name="dy_scales_%d_%d" % (c, g), align_bytes=64)
-            for a in range(N_A):
-                result[c, a] = keep.tile([P, PACK, N], F32, name="result_%d_%d" % (c, a), align_bytes=64)
-            out_codes[c] = keep.tile([P, N_A, N], I32, name="out_codes_%d" % c, align_bytes=64)
-        out_scales = keep.tile([P, N_A, T], U8, align_bytes=64)
+        for a in range(N_A):
+            for c0, c1 in OUT_PARTS[a]:
+                result[a, c0] = keep.tile([P, PACK, (c1 - c0) * N], F32, name="result_%d_%d" % (a, c0), align_bytes=64)
+            out_codes[a] = keep.tile([P, T], I32, name="out_codes_%d" % a, align_bytes=64)
+            out_scales[a] = keep.tile([P, T], U8, name="out_scales_%d" % a, align_bytes=64)
 
-        def load_dy(c, g):
-            rows = dy[g * SPAN : (g + 1) * SPAN, c * N : (c + 1) * N]
-            nc.sync.dma_start(out=dy_raw[c, g][:], in_=rows.rearrange("(p j) t -> p j t", j=PACK))
+        def chunk_of(tiles, parts, index, c):
+            c0 = max(lo for lo, hi in parts[index] if lo <= c)
+            return tiles[index, c0][:, :, (c - c0) * N : (c - c0 + 1) * N]
 
-        def load_scales(engine, s, scales):
-            for q in range(4):
-                engine.dma_start(
-                    out=ws_raw[32 * q : 32 * q + 4, s, :].bitcast(I32),
-                    in_=scales[0, 4 * q : 4 * q + 4, :].bitcast(I32),
+        def load_dy(g, part):
+            c0, c1 = DY_PARTS[g][part]
+            rows = dy[g * SPAN : (g + 1) * SPAN, c0 * N : c1 * N]
+            nc.sync.dma_start(out=dy_raw[g, c0][:], in_=rows.rearrange("(p j) t -> p j t", j=PACK))
+
+        def load_scales(s):
+            scales = (w8_scales, w4_scales)[s]
+            for r in range(4):
+                nc.sync.dma_start(
+                    out=ws_raw[r:P:32, s, :].bitcast(I32),
+                    in_=scales[0, r:16:4, :].bitcast(I32),
                 )
 
-        nc.vector.memset(ws_raw[:].rearrange("p s d -> p (s d)").bitcast(I32), 0)
-        nc.sync.dma_start(out=w8_raw[:], in_=w8_words[0].rearrange("p d i -> p (d i)").bitcast(I32))
-        nc.sync.dma_start(out=w4_raw[:].bitcast(I32), in_=w4_words[0].bitcast(I32))
-        load_dy(0, 0)
-        load_dy(0, 1)
-        load_scales(nc.scalar, 0, w8_scales)
-        load_scales(nc.gpsimd, 1, w4_scales)
-        for c in range(1, N_C):
-            load_dy(c, 0)
-            load_dy(c, 1)
+        def load_w8():
+            nc.sync.dma_start(out=w8_raw[:], in_=w8_words[0].rearrange("p d i -> p (d i)").bitcast(I32))
 
-        nc.vector.tensor_copy(
-            out=w8[:].rearrange("p (a r c i) -> p a c r i", a=N_A, r=PACK, i=4),
-            in_=w8_raw[:].rearrange("p (a c i r) -> p a c r i", a=N_A, r=PACK, i=4),
-        )
-        for a in range(N_A):
+        def load_w4():
+            nc.sync.dma_start(out=w4_raw[:].bitcast(I32), in_=w4_words[0].bitcast(I32))
+
+        def deal_w8(a0, a1):
+            cols = slice(a0 * SPAN, a1 * SPAN)
+            nc.vector.tensor_copy(
+                out=w8[:, cols].rearrange("p (a r c i) -> p a c r i", a=a1 - a0, r=PACK, i=4),
+                in_=w8_raw[:, cols].rearrange("p (a c i r) -> p a c r i", a=a1 - a0, r=PACK, i=4),
+            )
+
+        def deal_w4(a):
             cols = slice(2 * a * SPAN, 2 * (a + 1) * SPAN)
             nc.vector.tensor_copy(
                 out=w4[:, cols].rearrange("p (r c i b) -> p c r i b", r=PACK, i=8, b=2),
                 in_=w4_raw[:, cols].rearrange("p (c i r b) -> p c r i b", r=PACK, i=8, b=2),
             )
-        for a in range(N_A):
-            cols = slice(a * SPAN, (a + 1) * SPAN)
+
+        def deal_scales(s, a0, a1):
+            cols = slice(a0 * SPAN, a1 * SPAN)
             nc.vector.tensor_copy(
-                out=ws[:, :, cols].rearrange("p s (r c i) -> p s c r i", r=PACK, i=16),
-                in_=ws_raw[:, :, cols].rearrange("p s (c i r) -> p s c r i", r=PACK, i=16),
+                out=ws[:, s, cols].rearrange("p (a r c i) -> p a c r i", a=a1 - a0, r=PACK, i=16),
+                in_=ws_raw[:, s, cols].rearrange("p (a c i r) -> p a c r i", a=a1 - a0, r=PACK, i=16),
             )
 
         grouped = {}
 
-        def interleave(key, src, on_scalar=False):
+        def interleave(key, src, on_vector):
             tile = stage.tile([P, N, PACK], BF16, name="grouped", align_bytes=64)
             grouped[key] = tile
-            dst_v = tile[:].rearrange("p (c i) j -> p c j i", i=RUN)
-            src_v = src[:].rearrange("p j (c i) -> p c j i", i=RUN)
-            if on_scalar:
-                nc.scalar.copy(out=dst_v, in_=src_v)
-            else:
-                nc.vector.tensor_copy(out=dst_v, in_=src_v)
+            if on_vector > 0:
+                nc.vector.tensor_copy(
+                    out=tile[:, :on_vector, :].rearrange("p (c i) j -> p c j i", i=RUN),
+                    in_=src[:, :, :on_vector].rearrange("p j (c i) -> p c j i", i=RUN),
+                )
+            if on_vector < N:
+                nc.scalar.copy(
+                    out=tile[:, on_vector:, :].rearrange("p (c i) j -> p c j i", i=RUN),
+                    in_=src[:, :, on_vector:].rearrange("p j (c i) -> p c j i", i=RUN),
+                )
 
-        def group_dy(c, g, on_scalar=False):
-            interleave(("dy", c, g), dy_raw[c, g], on_scalar)
+        def group_dy(c, g, on_vector=N):
+            interleave(("dy", c, g), chunk_of(dy_raw, DY_PARTS, g, c), on_vector)
 
         def quant_dy(c, g):
             nc.vector.quantize_mx(
@@ -108,83 +121,126 @@ def tile_mix_dyq_fm_pl_none_kernel(tc, dy, w8_words, w8_scales, w4_words, w4_sca
                 in_=grouped["dy", c, g][:].rearrange("p t j -> p (t j)"),
             )
 
-        def multiply(c, a):
-            for r in range(PACK):
-                m0 = a * SPAN + r * P
-                acc = psum.tile([P, N], F32, name="acc")
-                nc.tensor.matmul_mx(
-                    out=acc[:],
-                    lhsT=w8[:, m0 : m0 + P].bitcast(E4M3),
-                    lhsT_scale=ws[:, 0, m0 : m0 + P],
-                    rhs=dy_codes[c, 0][:].bitcast(E5M2),
-                    rhs_scale=dy_scales[c, 0][:],
-                    start=True,
-                    stop=False,
-                )
-                nc.tensor.matmul_mx(
-                    out=acc[:],
-                    lhsT=w4[:, 2 * m0 : 2 * (m0 + P)].bitcast(E2M1),
-                    lhsT_scale=ws[:, 1, m0 : m0 + P],
-                    rhs=dy_codes[c, 1][:].bitcast(E5M2),
-                    rhs_scale=dy_scales[c, 1][:],
-                    start=False,
-                    stop=True,
-                )
-                nc.scalar.copy(out=result[c, a][:, r, :], in_=acc[:])
+        def multiply(c, a, r):
+            m0 = a * SPAN + r * P
+            acc = psum.tile([P, N], F32, name="acc")
+            nc.tensor.matmul_mx(
+                out=acc[:],
+                lhsT=w4[:, 2 * m0 : 2 * (m0 + P)].bitcast(E2M1),
+                lhsT_scale=ws[:, 1, m0 : m0 + P],
+                rhs=dy_codes[c, 1][:].bitcast(E5M2),
+                rhs_scale=dy_scales[c, 1][:],
+                start=True,
+                stop=False,
+            )
+            nc.tensor.matmul_mx(
+                out=acc[:],
+                lhsT=w8[:, m0 : m0 + P].bitcast(E4M3),
+                lhsT_scale=ws[:, 0, m0 : m0 + P],
+                rhs=dy_codes[c, 0][:].bitcast(E5M2),
+                rhs_scale=dy_scales[c, 0][:],
+                start=False,
+                stop=True,
+            )
+            nc.scalar.copy(out=chunk_of(result, OUT_PARTS, a, c)[:, r, :], in_=acc[:])
 
-        def group_out(c, a):
-            interleave(("out", c, a), result[c, a])
+        def multiply_rows(a, chunks, r0, r1):
+            for c in chunks:
+                for r in range(r0, r1):
+                    multiply(c, a, r)
+
+        def group_out(c, a, on_vector=N):
+            interleave(("out", c, a), chunk_of(result, OUT_PARTS, a, c), on_vector)
 
         def quant_out(c, a):
             nc.vector.quantize_mx(
-                out=out_codes[c][:, a, :].bitcast(E4M3),
-                scales=out_scales[:, a, c * N : (c + 1) * N],
+                out=out_codes[a][:, c * N : (c + 1) * N].bitcast(E4M3),
+                scales=out_scales[a][4 * (a + 1) : P, c * N : (c + 1) * N],
                 in_=grouped["out", c, a][:].rearrange("p t j -> p (t j)"),
             )
 
-        def store_result(c, a):
-            rows = out_0[a * SPAN : (a + 1) * SPAN, c * N : (c + 1) * N]
-            nc.sync.dma_start(out=rows.rearrange("(p r) t -> p r t", r=PACK), in_=result[c, a][:])
+        def store_result(a, part, r0, r1):
+            c0, c1 = OUT_PARTS[a][part]
+            rows = out_0[a * SPAN : (a + 1) * SPAN, c0 * N : c1 * N].rearrange("(p r) t -> p r t", r=PACK)
+            nc.sync.dma_start(out=rows[:, r0:r1, :], in_=result[a, c0][:, r0:r1, :])
 
-        def store_codes(c):
-            words = out_1[:, :, c * N : (c + 1) * N, :].rearrange("a p t i -> p a (t i)")
-            nc.sync.dma_start(out=words.bitcast(I32), in_=out_codes[c][:])
-
-        def store_scales():
-            for q in range(4):
-                nc.scalar.dma_start(
-                    out=out_2[:, 4 * q : 4 * q + 4, :].rearrange("a r t -> r a t").bitcast(I32),
-                    in_=out_scales[32 * q : 32 * q + 4, :, :].bitcast(I32),
+        def store_scales(a):
+            for r in range(4):
+                nc.sync.dma_start(
+                    out=out_2[a, r:16:4, :].bitcast(I32),
+                    in_=out_scales[a][4 * (a + 1) + r : P : 32, :].bitcast(I32),
                 )
 
-        group_dy(0, 0, on_scalar=True)
-        group_dy(0, 1)
+        def store_codes(a):
+            nc.sync.dma_start(out=out_1[a].rearrange("p t i -> p (t i)").bitcast(I32), in_=out_codes[a][:])
+
+        nc.vector.memset(ws_raw[:].rearrange("p s d -> p (s d)").bitcast(I32), 0)
+        load_w4()
+        load_dy(0, 0)
+        load_scales(1)
+        load_dy(1, 0)
+        load_scales(0)
+        load_w8()
+        load_dy(0, 1)
+        load_dy(1, 1)
+        load_dy(0, 2)
+        load_dy(1, 2)
+        deal_w4(0)
+        deal_w4(1)
+        deal_w4(2)
+        group_dy(0, 0, 0)
+        deal_scales(1, 0, 3)
+        group_dy(0, 1, 320)
         quant_dy(0, 0)
+        deal_scales(0, 0, 1)
         quant_dy(0, 1)
-        multiply(0, 0)
+        deal_w8(0, 1)
+        deal_scales(0, 1, 3)
+        deal_w8(1, 3)
         group_dy(1, 0)
-        group_dy(1, 1)
+        multiply_rows(0, (0,), 0, 4)
+        store_result(0, 0, 0, 4)
         quant_dy(1, 0)
-        quant_dy(1, 1)
-        multiply(0, 1)
         group_out(0, 0)
+        group_dy(1, 1)
+        quant_dy(1, 1)
+        multiply_rows(1, (0,), 0, 4)
+        multiply_rows(2, (0,), 0, 4)
         group_dy(2, 0)
         quant_out(0, 0)
         group_dy(2, 1)
         quant_dy(2, 0)
-        group_out(0, 1)
         quant_dy(2, 1)
-        store_result(0, 0)
-        store_result(0, 1)
-        groups = [(c, a) for c in range(N_C) for a in range(N_A)]
-        for i in range(2, len(groups)):
-            multiply(*groups[i])
-            group_out(*groups[i])
-            quant_out(*groups[i - 1])
-            if i == len(groups) - 1:
-                quant_out(*groups[i])
-                store_codes(N_C - 1)
-            store_result(*groups[i])
-            if i in (4, 6):
-                store_codes(i // 2 - 2)
-        store_scales()
+        multiply_rows(1, (1,), 0, 4)
+        store_result(1, 0, 0, 2)
+        store_result(1, 0, 2, 4)
+        multiply_rows(2, (1, 2), 0, 4)
+        store_result(2, 0, 0, 2)
+        store_result(2, 0, 2, 4)
+        group_out(0, 2)
+        group_out(1, 2)
+        quant_out(0, 2)
+        group_out(2, 2)
+        quant_out(1, 2)
+        group_out(0, 1)
+        quant_out(2, 2)
+        multiply_rows(0, (1, 2), 0, 4)
+        store_scales(2)
+        store_codes(2)
+        store_result(0, 1, 0, 2)
+        store_result(0, 1, 2, 4)
+        group_out(1, 0)
+        quant_out(0, 1)
+        group_out(2, 0)
+        quant_out(1, 0)
+        group_out(1, 1)
+        quant_out(2, 0)
+        multiply_rows(1, (2,), 0, 4)
+        store_scales(0)
+        store_codes(0)
+        store_result(1, 1, 0, 4)
+        group_out(2, 1)
+        quant_out(1, 1)
+        quant_out(2, 1)
+        store_scales(1)
+        store_codes(1)

@@ -38,7 +38,7 @@ def tile_mix_dyq_fm_pl_none_kernel(tc, dy, w8_words, w8_scales, w4_words, w4_sca
         w8 = keep.tile([P, D], I32, name="w8", align_bytes=64)
         w4 = keep.tile([P, 2 * D], U8, name="w4", align_bytes=64)
         ws = keep.tile([P, 2, D], U8, name="ws", align_bytes=64)
-        dy_raw, dy_codes, dy_scales, result, out_codes, out_scales = {}, {}, {}, {}, {}, {}
+        dy_raw, dy_codes, dy_scales, result, out_codes = {}, {}, {}, {}, {}
         for g in range(2):
             for c0, c1 in DY_PARTS[g]:
                 dy_raw[g, c0] = keep.tile([P, PACK, (c1 - c0) * N], F32, name="dy_raw_%d_%d" % (g, c0), align_bytes=64)
@@ -49,7 +49,7 @@ def tile_mix_dyq_fm_pl_none_kernel(tc, dy, w8_words, w8_scales, w4_words, w4_sca
             for c0, c1 in OUT_PARTS[a]:
                 result[a, c0] = keep.tile([P, PACK, (c1 - c0) * N], F32, name="result_%d_%d" % (a, c0), align_bytes=64)
             out_codes[a] = keep.tile([P, T], I32, name="out_codes_%d" % a, align_bytes=64)
-            out_scales[a] = keep.tile([P, T], U8, name="out_scales_%d" % a, align_bytes=64)
+        out_scales = keep.tile([P, T], U8, name="out_scales", align_bytes=64)
 
         def chunk_of(tiles, parts, index, c):
             c0 = max(lo for lo, hi in parts[index] if lo <= c)
@@ -155,7 +155,7 @@ def tile_mix_dyq_fm_pl_none_kernel(tc, dy, w8_words, w8_scales, w4_words, w4_sca
         def quant_out(c, a):
             nc.vector.quantize_mx(
                 out=out_codes[a][:, c * N : (c + 1) * N].bitcast(E4M3),
-                scales=out_scales[a][4 * (a + 1) : P, c * N : (c + 1) * N],
+                scales=out_scales[4 * (a + 1) : P, c * N : (c + 1) * N],
                 in_=grouped["out", c, a][:].rearrange("p t j -> p (t j)"),
             )
 
@@ -164,11 +164,11 @@ def tile_mix_dyq_fm_pl_none_kernel(tc, dy, w8_words, w8_scales, w4_words, w4_sca
             rows = out_0[a * SPAN : (a + 1) * SPAN, c0 * N : c1 * N].rearrange("(p r) t -> p r t", r=PACK)
             nc.sync.dma_start(out=rows[:, r0:r1, :], in_=result[a, c0][:, r0:r1, :])
 
-        def store_scales(a):
-            for r in range(4):
-                nc.sync.dma_start(
-                    out=out_2[a, r:16:4, :].bitcast(I32),
-                    in_=out_scales[a][4 * (a + 1) + r : P : 32, :].bitcast(I32),
+        def store_scales():
+            for q in range(4):
+                nc.gpsimd.dma_start(
+                    out=out_2[:, 4 * q : 4 * q + 4, :].bitcast(I32),
+                    in_=out_scales[32 * q + 4 : 32 * q + 16, :].bitcast(I32),
                 )
 
         def store_codes(a):
@@ -201,15 +201,13 @@ def tile_mix_dyq_fm_pl_none_kernel(tc, dy, w8_words, w8_scales, w4_words, w4_sca
         multiply_rows(0, (0,), 0, 4)
         store_result(0, 0, 0, 4)
         quant_dy(1, 0)
-        group_out(0, 0)
         group_dy(1, 1)
         quant_dy(1, 1)
         multiply_rows(1, (0,), 0, 4)
         multiply_rows(2, (0,), 0, 4)
         group_dy(2, 0)
-        quant_out(0, 0)
-        group_dy(2, 1)
         quant_dy(2, 0)
+        group_dy(2, 1)
         quant_dy(2, 1)
         multiply_rows(1, (1,), 0, 4)
         store_result(1, 0, 0, 2)
@@ -217,30 +215,30 @@ def tile_mix_dyq_fm_pl_none_kernel(tc, dy, w8_words, w8_scales, w4_words, w4_sca
         multiply_rows(2, (1, 2), 0, 4)
         store_result(2, 0, 0, 2)
         store_result(2, 0, 2, 4)
+        group_out(0, 0)
         group_out(0, 2)
+        quant_out(0, 0)
         group_out(1, 2)
         quant_out(0, 2)
         group_out(2, 2)
         quant_out(1, 2)
-        group_out(0, 1)
-        quant_out(2, 2)
         multiply_rows(0, (1, 2), 0, 4)
-        store_scales(2)
-        store_codes(2)
         store_result(0, 1, 0, 2)
         store_result(0, 1, 2, 4)
         group_out(1, 0)
-        quant_out(0, 1)
+        quant_out(2, 2)
+        store_codes(2)
         group_out(2, 0)
         quant_out(1, 0)
-        group_out(1, 1)
-        quant_out(2, 0)
         multiply_rows(1, (2,), 0, 4)
-        store_scales(0)
-        store_codes(0)
         store_result(1, 1, 0, 4)
-        group_out(2, 1)
+        group_out(1, 1, 0)
+        group_out(0, 1)
+        quant_out(2, 0)
+        store_codes(0)
+        group_out(2, 1, 256)
+        quant_out(0, 1)
         quant_out(1, 1)
         quant_out(2, 1)
-        store_scales(1)
+        store_scales()
         store_codes(1)

@@ -8,6 +8,7 @@ FLOPS = 2 * K * D * T
 F32 = mybir.dt.float32
 BF16 = mybir.dt.bfloat16
 I32 = mybir.dt.int32
+U16 = mybir.dt.uint16
 U8 = mybir.dt.uint8
 E4M3 = mybir.dt.float8_e4m3fn_x4
 E5M2 = mybir.dt.float8_e5m2_x4
@@ -20,24 +21,23 @@ N = 512
 N_A = D // SPAN
 N_C = T // N
 RUN = 4
-DY_PARTS = (((0, 1), (1, 2), (2, 3)), ((0, 1), (1, 2), (2, 3)))
-OUT_PARTS = (((0, 1), (1, 3)), ((0, 2), (2, 3)), ((0, 3),))
+DY_PARTS = (((0, 3),), ((0, 1), (1, 2), (2, 3)))
+W_PARTS = ((0, 1), (1, 3))
 
 
 def tile_mix_dyq_fm_pl_none_kernel(tc, dy, w8_words, w8_scales, w4_words, w4_scales, out_0, out_1, out_2):
     nc = tc.nc
     with ExitStack() as ctx:
         keep = ctx.enter_context(tc.tile_pool(name="keep", bufs=1))
-        stage = ctx.enter_context(tc.tile_pool(name="stage", bufs=5))
+        stage = ctx.enter_context(tc.tile_pool(name="stage", bufs=6))
         psum = ctx.enter_context(tc.psum_pool(name="psum", bufs=8))
         ctx.enter_context(tc.manual_schedule())
 
-        w8_raw = keep.tile([P, D], I32, name="w8_raw", align_bytes=64)
-        w4_raw = keep.tile([P, 2 * D], U8, name="w4_raw", align_bytes=64)
-        ws_raw = keep.tile([P, 2, D], U8, name="ws_raw", align_bytes=64)
-        w8 = keep.tile([P, D], I32, name="w8", align_bytes=64)
-        w4 = keep.tile([P, 2 * D], U8, name="w4", align_bytes=64)
-        ws = keep.tile([P, 2, D], U8, name="ws", align_bytes=64)
+        ws_raw = [keep.tile([P, D], U8, name="ws_raw_%d" % s, align_bytes=64) for s in range(2)]
+        w8_raw, w4_raw, w8, w4, ws = {}, {}, {}, {}, {}
+        for a0, a1 in W_PARTS:
+            w8_raw[a0] = keep.tile([P, (a1 - a0) * SPAN], I32, name="w8_raw_%d" % a0, align_bytes=64)
+            w4_raw[a0] = keep.tile([P, 2 * (a1 - a0) * SPAN], U8, name="w4_raw_%d" % a0, align_bytes=64)
         dy_raw, dy_codes, dy_scales, result, out_codes = {}, {}, {}, {}, {}
         for g in range(2):
             for c0, c1 in DY_PARTS[g]:
@@ -46,14 +46,13 @@ def tile_mix_dyq_fm_pl_none_kernel(tc, dy, w8_words, w8_scales, w4_words, w4_sca
                 dy_codes[c, g] = keep.tile([P, N], I32, name="dy_codes_%d_%d" % (c, g), align_bytes=64)
                 dy_scales[c, g] = keep.tile([P, N], U8, name="dy_scales_%d_%d" % (c, g), align_bytes=64)
         for a in range(N_A):
-            for c0, c1 in OUT_PARTS[a]:
-                result[a, c0] = keep.tile([P, PACK, (c1 - c0) * N], F32, name="result_%d_%d" % (a, c0), align_bytes=64)
+            w8[a] = keep.tile([P, SPAN], I32, name="w8_%d" % a, align_bytes=64)
+            w4[a] = keep.tile([P, 2 * SPAN], U8, name="w4_%d" % a, align_bytes=64)
+            for s in range(2):
+                ws[s, a] = keep.tile([P, SPAN], U8, name="ws_%d_%d" % (s, a), align_bytes=64)
+            result[a] = keep.tile([P, PACK, T], F32, name="result_%d" % a, align_bytes=64)
             out_codes[a] = keep.tile([P, T], I32, name="out_codes_%d" % a, align_bytes=64)
         out_scales = keep.tile([P, T], U8, name="out_scales", align_bytes=64)
-
-        def chunk_of(tiles, parts, index, c):
-            c0 = max(lo for lo, hi in parts[index] if lo <= c)
-            return tiles[index, c0][:, :, (c - c0) * N : (c - c0 + 1) * N]
 
         def load_dy(g, part):
             c0, c1 = DY_PARTS[g][part]
@@ -63,106 +62,104 @@ def tile_mix_dyq_fm_pl_none_kernel(tc, dy, w8_words, w8_scales, w4_words, w4_sca
         def load_scales(s):
             scales = (w8_scales, w4_scales)[s]
             for r in range(4):
-                nc.sync.dma_start(
-                    out=ws_raw[r:P:32, s, :].bitcast(I32),
-                    in_=scales[0, r:16:4, :].bitcast(I32),
-                )
+                nc.sync.dma_start(out=ws_raw[s][r:P:32, :].bitcast(I32), in_=scales[0, r:16:4, :].bitcast(I32))
 
-        def load_w8():
-            nc.sync.dma_start(out=w8_raw[:], in_=w8_words[0].rearrange("p d i -> p (d i)").bitcast(I32))
+        def load_w8(part):
+            a0, a1 = W_PARTS[part]
+            words = w8_words[0].rearrange("p d i -> p (d i)").bitcast(I32)
+            nc.sync.dma_start(out=w8_raw[a0][:], in_=words[:, a0 * SPAN : a1 * SPAN])
 
-        def load_w4():
-            nc.sync.dma_start(out=w4_raw[:].bitcast(I32), in_=w4_words[0].bitcast(I32))
+        def load_w4(part):
+            a0, a1 = W_PARTS[part]
+            nc.sync.dma_start(out=w4_raw[a0][:].bitcast(I32), in_=w4_words[0][:, 2 * a0 * SPAN : 2 * a1 * SPAN].bitcast(I32))
 
-        def deal_w8(a0, a1):
-            cols = slice(a0 * SPAN, a1 * SPAN)
+        def deal(out, in_, line):
             nc.vector.tensor_copy(
-                out=w8[:, cols].rearrange("p (a r c i) -> p a c r i", a=a1 - a0, r=PACK, i=4),
-                in_=w8_raw[:, cols].rearrange("p (a c i r) -> p a c r i", a=a1 - a0, r=PACK, i=4),
+                out=out.rearrange("p (r c i) -> p c r i", r=PACK, i=line),
+                in_=in_.rearrange("p (c i r) -> p c r i", r=PACK, i=line),
             )
+
+        def deal_w8(a):
+            a0 = max(lo for lo, hi in W_PARTS if lo <= a)
+            deal(w8[a][:], w8_raw[a0][:, (a - a0) * SPAN : (a - a0 + 1) * SPAN], 4)
 
         def deal_w4(a):
-            cols = slice(2 * a * SPAN, 2 * (a + 1) * SPAN)
-            nc.vector.tensor_copy(
-                out=w4[:, cols].rearrange("p (r c i b) -> p c r i b", r=PACK, i=8, b=2),
-                in_=w4_raw[:, cols].rearrange("p (c i r b) -> p c r i b", r=PACK, i=8, b=2),
-            )
+            a0 = max(lo for lo, hi in W_PARTS if lo <= a)
+            deal(w4[a][:].bitcast(U16), w4_raw[a0][:, 2 * (a - a0) * SPAN : 2 * (a - a0 + 1) * SPAN].bitcast(U16), 8)
 
-        def deal_scales(s, a0, a1):
-            cols = slice(a0 * SPAN, a1 * SPAN)
-            nc.vector.tensor_copy(
-                out=ws[:, s, cols].rearrange("p (a r c i) -> p a c r i", a=a1 - a0, r=PACK, i=16),
-                in_=ws_raw[:, s, cols].rearrange("p (a c i r) -> p a c r i", a=a1 - a0, r=PACK, i=16),
-            )
+        def deal_scales(s, a):
+            deal(ws[s, a][:], ws_raw[s][:, a * SPAN : (a + 1) * SPAN], 16)
 
         grouped = {}
 
-        def interleave(key, src, on_vector):
+        def interleave(key, src, on_vector, run):
             tile = stage.tile([P, N, PACK], BF16, name="grouped", align_bytes=64)
             grouped[key] = tile
-            if on_vector > 0:
-                nc.vector.tensor_copy(
-                    out=tile[:, :on_vector, :].rearrange("p (c i) j -> p c j i", i=RUN),
-                    in_=src[:, :, :on_vector].rearrange("p j (c i) -> p c j i", i=RUN),
-                )
-            if on_vector < N:
-                nc.scalar.copy(
-                    out=tile[:, on_vector:, :].rearrange("p (c i) j -> p c j i", i=RUN),
-                    in_=src[:, :, on_vector:].rearrange("p j (c i) -> p c j i", i=RUN),
-                )
+            for copy, lo, hi in ((nc.vector.tensor_copy, 0, on_vector), (nc.scalar.copy, on_vector, N)):
+                if lo == hi:
+                    continue
+                if run:
+                    copy(
+                        out=tile[:, lo:hi, :].rearrange("p (c i) j -> p c j i", i=RUN),
+                        in_=src[:, :, lo:hi].rearrange("p j (c i) -> p c j i", i=RUN),
+                    )
+                else:
+                    copy(out=tile[:, lo:hi, :], in_=src[:, :, lo:hi].rearrange("p j t -> p t j"))
 
-        def group_dy(c, g, on_vector=N):
-            interleave(("dy", c, g), chunk_of(dy_raw, DY_PARTS, g, c), on_vector)
+        def group_dy(g, c, on_vector=N):
+            c0 = max(lo for lo, hi in DY_PARTS[g] if lo <= c)
+            interleave(("dy", g, c), dy_raw[g, c0][:, :, (c - c0) * N : (c - c0 + 1) * N], on_vector, True)
 
-        def quant_dy(c, g):
+        def quant_dy(g, c):
             nc.vector.quantize_mx(
                 out=dy_codes[c, g][:].bitcast(E5M2),
                 scales=dy_scales[c, g][:],
-                in_=grouped["dy", c, g][:].rearrange("p t j -> p (t j)"),
+                in_=grouped["dy", g, c][:].rearrange("p t j -> p (t j)"),
             )
 
-        def multiply(c, a, r):
-            m0 = a * SPAN + r * P
-            acc = psum.tile([P, N], F32, name="acc")
+        banks = {}
+
+        def one_pass(g, a, c, r, first):
+            if first:
+                banks[a, c, r] = psum.tile([P, N], F32, name="acc")
+            lhsT = w8[a][:, r * P : (r + 1) * P].bitcast(E4M3) if g == 0 else w4[a][:, 2 * r * P : 2 * (r + 1) * P].bitcast(E2M1)
             nc.tensor.matmul_mx(
-                out=acc[:],
-                lhsT=w4[:, 2 * m0 : 2 * (m0 + P)].bitcast(E2M1),
-                lhsT_scale=ws[:, 1, m0 : m0 + P],
-                rhs=dy_codes[c, 1][:].bitcast(E5M2),
-                rhs_scale=dy_scales[c, 1][:],
-                start=True,
-                stop=False,
+                out=banks[a, c, r][:],
+                lhsT=lhsT,
+                lhsT_scale=ws[g, a][:, r * P : (r + 1) * P],
+                rhs=dy_codes[c, g][:].bitcast(E5M2),
+                rhs_scale=dy_scales[c, g][:],
+                start=first,
+                stop=not first,
             )
-            nc.tensor.matmul_mx(
-                out=acc[:],
-                lhsT=w8[:, m0 : m0 + P].bitcast(E4M3),
-                lhsT_scale=ws[:, 0, m0 : m0 + P],
-                rhs=dy_codes[c, 0][:].bitcast(E5M2),
-                rhs_scale=dy_scales[c, 0][:],
-                start=False,
-                stop=True,
-            )
-            nc.scalar.copy(out=chunk_of(result, OUT_PARTS, a, c)[:, r, :], in_=acc[:])
 
-        def multiply_rows(a, chunks, r0, r1):
-            for c in chunks:
-                for r in range(r0, r1):
-                    multiply(c, a, r)
+        def open_banks(a, c, rows):
+            for r in rows:
+                one_pass(0, a, c, r, True)
 
-        def group_out(c, a, on_vector=N):
-            interleave(("out", c, a), chunk_of(result, OUT_PARTS, a, c), on_vector)
+        def close_banks(a, c, rows):
+            for r in rows:
+                one_pass(1, a, c, r, False)
+                nc.scalar.copy(out=result[a][:, r, c * N : (c + 1) * N], in_=banks[a, c, r][:])
 
-        def quant_out(c, a):
+        def multiply(a, c, rows):
+            for r in rows:
+                open_banks(a, c, (r,))
+                close_banks(a, c, (r,))
+
+        def group_out(a, c, on_vector=N):
+            interleave(("out", a, c), result[a][:, :, c * N : (c + 1) * N], on_vector, c == N_C - 1)
+
+        def quant_out(a, c):
             nc.vector.quantize_mx(
                 out=out_codes[a][:, c * N : (c + 1) * N].bitcast(E4M3),
                 scales=out_scales[4 * (a + 1) : P, c * N : (c + 1) * N],
-                in_=grouped["out", c, a][:].rearrange("p t j -> p (t j)"),
+                in_=grouped["out", a, c][:].rearrange("p t j -> p (t j)"),
             )
 
-        def store_result(a, part, r0, r1):
-            c0, c1 = OUT_PARTS[a][part]
-            rows = out_0[a * SPAN : (a + 1) * SPAN, c0 * N : c1 * N].rearrange("(p r) t -> p r t", r=PACK)
-            nc.sync.dma_start(out=rows[:, r0:r1, :], in_=result[a, c0][:, r0:r1, :])
+        def store_result(a, r0, r1, c0, c1):
+            rows = out_0[a * SPAN : (a + 1) * SPAN, :].rearrange("(p r) t -> p r t", r=PACK)
+            nc.sync.dma_start(out=rows[:, r0:r1, c0 * N : c1 * N], in_=result[a][:, r0:r1, c0 * N : c1 * N])
 
         def store_scales():
             for q in range(4):
@@ -174,71 +171,95 @@ def tile_mix_dyq_fm_pl_none_kernel(tc, dy, w8_words, w8_scales, w4_words, w4_sca
         def store_codes(a):
             nc.sync.dma_start(out=out_1[a].rearrange("p t i -> p (t i)").bitcast(I32), in_=out_codes[a][:])
 
-        nc.vector.memset(ws_raw[:].rearrange("p s d -> p (s d)").bitcast(I32), 0)
-        load_w4()
-        load_dy(0, 0)
+        nc.vector.memset(ws_raw[1][:].bitcast(I32), 0)
+        nc.vector.memset(ws_raw[0][:].bitcast(I32), 0)
+        load_w4(0)
+        load_w8(0)
         load_scales(1)
-        load_dy(1, 0)
+        load_dy(0, 0)
         load_scales(0)
-        load_w8()
-        load_dy(0, 1)
+        load_dy(1, 0)
         load_dy(1, 1)
-        load_dy(0, 2)
         load_dy(1, 2)
+        load_w4(1)
+        load_w8(1)
         deal_w4(0)
-        deal_w4(1)
-        deal_w4(2)
-        group_dy(0, 0, 0)
-        deal_scales(1, 0, 3)
-        group_dy(0, 1, 320)
+        deal_scales(1, 0)
+        deal_w8(0)
+        deal_scales(1, 1)
+        deal_scales(1, 2)
+        group_dy(0, 0)
+        group_dy(0, 2, 0)
+        deal_scales(0, 0)
         quant_dy(0, 0)
-        deal_scales(0, 0, 1)
+        group_dy(0, 1)
+        open_banks(0, 0, range(4))
+        group_dy(1, 0, 256)
         quant_dy(0, 1)
-        deal_w8(0, 1)
-        deal_scales(0, 1, 3)
-        deal_w8(1, 3)
-        group_dy(1, 0)
-        multiply_rows(0, (0,), 0, 4)
-        store_result(0, 0, 0, 4)
         quant_dy(1, 0)
-        group_dy(1, 1)
+        group_dy(1, 1, 384)
+        close_banks(0, 0, range(4))
+        open_banks(0, 1, (2, 3, 0, 1))
+        store_result(0, 0, 2, 0, 1)
+        deal_scales(0, 1)
         quant_dy(1, 1)
-        multiply_rows(1, (0,), 0, 4)
-        multiply_rows(2, (0,), 0, 4)
-        group_dy(2, 0)
-        quant_dy(2, 0)
-        group_dy(2, 1)
-        quant_dy(2, 1)
-        multiply_rows(1, (1,), 0, 4)
-        store_result(1, 0, 0, 2)
-        store_result(1, 0, 2, 4)
-        multiply_rows(2, (1, 2), 0, 4)
-        store_result(2, 0, 0, 2)
-        store_result(2, 0, 2, 4)
+        quant_dy(0, 2)
+        close_banks(0, 1, (2,))
+        store_result(0, 2, 3, 0, 2)
+        close_banks(0, 1, (3,))
+        store_result(0, 3, 4, 0, 2)
+        close_banks(0, 1, (0, 1))
+        open_banks(0, 2, range(4))
+        group_dy(1, 2)
+        deal_scales(0, 2)
+        quant_dy(1, 2)
+        close_banks(0, 2, (0,))
+        store_result(0, 0, 1, 1, 3)
+        close_banks(0, 2, (1,))
+        store_result(0, 1, 2, 1, 3)
+        close_banks(0, 2, (2, 3))
+        store_result(0, 2, 4, 2, 3)
+        deal_w4(1)
+        deal_w8(1)
+        multiply(1, 0, (0,))
+        multiply(1, 1, (0,))
+        multiply(1, 2, (0,))
+        store_result(1, 0, 1, 0, 3)
+        multiply(1, 0, (1,))
+        multiply(1, 1, (1,))
+        multiply(1, 2, (1,))
+        store_result(1, 1, 2, 0, 3)
         group_out(0, 0)
-        group_out(0, 2)
-        quant_out(0, 0)
-        group_out(1, 2)
-        quant_out(0, 2)
-        group_out(2, 2)
-        quant_out(1, 2)
-        multiply_rows(0, (1, 2), 0, 4)
-        store_result(0, 1, 0, 2)
-        store_result(0, 1, 2, 4)
-        group_out(1, 0)
-        quant_out(2, 2)
-        store_codes(2)
-        group_out(2, 0)
-        quant_out(1, 0)
-        multiply_rows(1, (2,), 0, 4)
-        store_result(1, 1, 0, 4)
-        group_out(1, 1, 0)
         group_out(0, 1)
-        quant_out(2, 0)
-        store_codes(0)
-        group_out(2, 1, 256)
+        quant_out(0, 0)
+        group_out(0, 2)
         quant_out(0, 1)
+        deal_w4(2)
+        quant_out(0, 2)
+        deal_w8(2)
+        multiply(1, 0, (2, 3))
+        multiply(1, 1, (2, 3))
+        multiply(1, 2, (2, 3))
+        store_codes(0)
+        store_result(1, 2, 4, 0, 3)
+        group_out(1, 0)
+        group_out(1, 1)
+        quant_out(1, 0)
+        group_out(1, 2)
         quant_out(1, 1)
-        quant_out(2, 1)
-        store_scales()
+        multiply(2, 0, range(4))
+        quant_out(1, 2)
         store_codes(1)
+        group_out(2, 0)
+        multiply(2, 1, range(4))
+        group_out(2, 1)
+        quant_out(2, 0)
+        quant_out(2, 1)
+        multiply(2, 2, (0, 1))
+        store_result(2, 0, 2, 0, 3)
+        multiply(2, 2, (2, 3))
+        store_result(2, 2, 4, 0, 3)
+        group_out(2, 2, 192)
+        quant_out(2, 2)
+        store_scales()
+        store_codes(2)

@@ -18,87 +18,97 @@ P = 128
 PACK = 4
 SPAN = P * PACK
 N = 512
-N_A = D // SPAN
-N_C = T // N
+N_SPANS = D // SPAN
+N_CHUNKS = T // N
+QUADRANT = 32
+LINE = 16
 RUN = 4
-DY_PARTS = (((0, 3),), ((0, 1), (1, 2), (2, 3)))
-W_PARTS = ((0, 1), (1, 3))
+STAGED = 6
+DY_LOADS = (((0, 3),), ((0, 1), (1, 2), (2, 3)))
+W_LOADS = ((0, 1), (1, 3))
+SHARE_FIRST = 256
+SHARE_SECOND = 384
+SHARE_LAST = 192
 
 
 def tile_mix_dyq_fm_pl_none_kernel(tc, dy, w8_words, w8_scales, w4_words, w4_scales, out_0, out_1, out_2):
     nc = tc.nc
     with ExitStack() as ctx:
         keep = ctx.enter_context(tc.tile_pool(name="keep", bufs=1))
-        stage = ctx.enter_context(tc.tile_pool(name="stage", bufs=6))
+        stage = ctx.enter_context(tc.tile_pool(name="stage", bufs=STAGED))
         psum = ctx.enter_context(tc.psum_pool(name="psum", bufs=8))
         ctx.enter_context(tc.manual_schedule())
 
-        ws_raw = [keep.tile([P, D], U8, name="ws_raw_%d" % s, align_bytes=64) for s in range(2)]
+        ws_raw = [keep.tile([P, D], U8, name="ws_raw_%d" % g, align_bytes=64) for g in range(2)]
         w8_raw, w4_raw, w8, w4, ws = {}, {}, {}, {}, {}
-        for a0, a1 in W_PARTS:
+        for a0, a1 in W_LOADS:
             w8_raw[a0] = keep.tile([P, (a1 - a0) * SPAN], I32, name="w8_raw_%d" % a0, align_bytes=64)
             w4_raw[a0] = keep.tile([P, 2 * (a1 - a0) * SPAN], U8, name="w4_raw_%d" % a0, align_bytes=64)
         dy_raw, dy_codes, dy_scales, result, out_codes = {}, {}, {}, {}, {}
         for g in range(2):
-            for c0, c1 in DY_PARTS[g]:
+            for c0, c1 in DY_LOADS[g]:
                 dy_raw[g, c0] = keep.tile([P, PACK, (c1 - c0) * N], F32, name="dy_raw_%d_%d" % (g, c0), align_bytes=64)
-            for c in range(N_C):
+            for c in range(N_CHUNKS):
                 dy_codes[c, g] = keep.tile([P, N], I32, name="dy_codes_%d_%d" % (c, g), align_bytes=64)
                 dy_scales[c, g] = keep.tile([P, N], U8, name="dy_scales_%d_%d" % (c, g), align_bytes=64)
-        for a in range(N_A):
+        for a in range(N_SPANS):
             w8[a] = keep.tile([P, SPAN], I32, name="w8_%d" % a, align_bytes=64)
             w4[a] = keep.tile([P, 2 * SPAN], U8, name="w4_%d" % a, align_bytes=64)
-            for s in range(2):
-                ws[s, a] = keep.tile([P, SPAN], U8, name="ws_%d_%d" % (s, a), align_bytes=64)
+            for g in range(2):
+                ws[g, a] = keep.tile([P, SPAN], U8, name="ws_%d_%d" % (g, a), align_bytes=64)
             result[a] = keep.tile([P, PACK, T], F32, name="result_%d" % a, align_bytes=64)
             out_codes[a] = keep.tile([P, T], I32, name="out_codes_%d" % a, align_bytes=64)
         out_scales = keep.tile([P, T], U8, name="out_scales", align_bytes=64)
 
+        def first_of(ranges, index):
+            return max(lo for lo, hi in ranges if lo <= index)
+
         def load_dy(g, part):
-            c0, c1 = DY_PARTS[g][part]
+            c0, c1 = DY_LOADS[g][part]
             rows = dy[g * SPAN : (g + 1) * SPAN, c0 * N : c1 * N]
             nc.sync.dma_start(out=dy_raw[g, c0][:], in_=rows.rearrange("(p j) t -> p j t", j=PACK))
 
-        def load_scales(s):
-            scales = (w8_scales, w4_scales)[s]
+        def load_scales(g, a0=0, a1=N_SPANS):
+            scales = (w8_scales, w4_scales)[g]
             for r in range(4):
-                nc.sync.dma_start(out=ws_raw[s][r:P:32, :].bitcast(I32), in_=scales[0, r:16:4, :].bitcast(I32))
+                cols = slice(a0 * SPAN, a1 * SPAN)
+                nc.sync.dma_start(out=ws_raw[g][r:P:QUADRANT, cols].bitcast(I32), in_=scales[0, r:16:4, cols].bitcast(I32))
 
         def load_w8(part):
-            a0, a1 = W_PARTS[part]
+            a0, a1 = W_LOADS[part]
             words = w8_words[0].rearrange("p d i -> p (d i)").bitcast(I32)
             nc.sync.dma_start(out=w8_raw[a0][:], in_=words[:, a0 * SPAN : a1 * SPAN])
 
         def load_w4(part):
-            a0, a1 = W_PARTS[part]
+            a0, a1 = W_LOADS[part]
             nc.sync.dma_start(out=w4_raw[a0][:].bitcast(I32), in_=w4_words[0][:, 2 * a0 * SPAN : 2 * a1 * SPAN].bitcast(I32))
 
-        def deal(out, in_, line):
+        def deal(out, in_, per_line):
             nc.vector.tensor_copy(
-                out=out.rearrange("p (r c i) -> p c r i", r=PACK, i=line),
-                in_=in_.rearrange("p (c i r) -> p c r i", r=PACK, i=line),
+                out=out.rearrange("p (r c i) -> p c r i", r=PACK, i=per_line),
+                in_=in_.rearrange("p (c i r) -> p c r i", r=PACK, i=per_line),
             )
 
         def deal_w8(a):
-            a0 = max(lo for lo, hi in W_PARTS if lo <= a)
-            deal(w8[a][:], w8_raw[a0][:, (a - a0) * SPAN : (a - a0 + 1) * SPAN], 4)
+            a0 = first_of(W_LOADS, a)
+            deal(w8[a][:], w8_raw[a0][:, (a - a0) * SPAN : (a - a0 + 1) * SPAN], LINE // 4)
 
         def deal_w4(a):
-            a0 = max(lo for lo, hi in W_PARTS if lo <= a)
-            deal(w4[a][:].bitcast(U16), w4_raw[a0][:, 2 * (a - a0) * SPAN : 2 * (a - a0 + 1) * SPAN].bitcast(U16), 8)
+            a0 = first_of(W_LOADS, a)
+            deal(w4[a][:].bitcast(U16), w4_raw[a0][:, 2 * (a - a0) * SPAN : 2 * (a - a0 + 1) * SPAN].bitcast(U16), LINE // 2)
 
-        def deal_scales(s, a):
-            deal(ws[s, a][:], ws_raw[s][:, a * SPAN : (a + 1) * SPAN], 16)
+        def deal_scales(g, a):
+            deal(ws[g, a][:], ws_raw[g][:, a * SPAN : (a + 1) * SPAN], LINE)
 
         grouped = {}
 
-        def interleave(key, src, on_vector, run):
+        def interleave(key, src, on_vector, in_runs):
             tile = stage.tile([P, N, PACK], BF16, name="grouped", align_bytes=64)
             grouped[key] = tile
             for copy, lo, hi in ((nc.vector.tensor_copy, 0, on_vector), (nc.scalar.copy, on_vector, N)):
                 if lo == hi:
                     continue
-                if run:
+                if in_runs:
                     copy(
                         out=tile[:, lo:hi, :].rearrange("p (c i) j -> p c j i", i=RUN),
                         in_=src[:, :, lo:hi].rearrange("p j (c i) -> p c j i", i=RUN),
@@ -107,7 +117,7 @@ def tile_mix_dyq_fm_pl_none_kernel(tc, dy, w8_words, w8_scales, w4_words, w4_sca
                     copy(out=tile[:, lo:hi, :], in_=src[:, :, lo:hi].rearrange("p j t -> p t j"))
 
         def group_dy(g, c, on_vector=N):
-            c0 = max(lo for lo, hi in DY_PARTS[g] if lo <= c)
+            c0 = first_of(DY_LOADS[g], c)
             interleave(("dy", g, c), dy_raw[g, c0][:, :, (c - c0) * N : (c - c0 + 1) * N], on_vector, True)
 
         def quant_dy(g, c):
@@ -119,36 +129,39 @@ def tile_mix_dyq_fm_pl_none_kernel(tc, dy, w8_words, w8_scales, w4_words, w4_sca
 
         banks = {}
 
-        def one_pass(g, a, c, r, first):
-            if first:
+        def open_banks(a, c, slots):
+            for r in slots:
                 banks[a, c, r] = psum.tile([P, N], F32, name="acc")
-            lhsT = w8[a][:, r * P : (r + 1) * P].bitcast(E4M3) if g == 0 else w4[a][:, 2 * r * P : 2 * (r + 1) * P].bitcast(E2M1)
-            nc.tensor.matmul_mx(
-                out=banks[a, c, r][:],
-                lhsT=lhsT,
-                lhsT_scale=ws[g, a][:, r * P : (r + 1) * P],
-                rhs=dy_codes[c, g][:].bitcast(E5M2),
-                rhs_scale=dy_scales[c, g][:],
-                start=first,
-                stop=not first,
-            )
+                nc.tensor.matmul_mx(
+                    out=banks[a, c, r][:],
+                    lhsT=w8[a][:, r * P : (r + 1) * P].bitcast(E4M3),
+                    lhsT_scale=ws[0, a][:, r * P : (r + 1) * P],
+                    rhs=dy_codes[c, 0][:].bitcast(E5M2),
+                    rhs_scale=dy_scales[c, 0][:],
+                    start=True,
+                    stop=False,
+                )
 
-        def open_banks(a, c, rows):
-            for r in rows:
-                one_pass(0, a, c, r, True)
-
-        def close_banks(a, c, rows):
-            for r in rows:
-                one_pass(1, a, c, r, False)
+        def close_banks(a, c, slots):
+            for r in slots:
+                nc.tensor.matmul_mx(
+                    out=banks[a, c, r][:],
+                    lhsT=w4[a][:, 2 * r * P : 2 * (r + 1) * P].bitcast(E2M1),
+                    lhsT_scale=ws[1, a][:, r * P : (r + 1) * P],
+                    rhs=dy_codes[c, 1][:].bitcast(E5M2),
+                    rhs_scale=dy_scales[c, 1][:],
+                    start=False,
+                    stop=True,
+                )
                 nc.scalar.copy(out=result[a][:, r, c * N : (c + 1) * N], in_=banks[a, c, r][:])
 
-        def multiply(a, c, rows):
-            for r in rows:
+        def multiply(a, c, slots):
+            for r in slots:
                 open_banks(a, c, (r,))
                 close_banks(a, c, (r,))
 
         def group_out(a, c, on_vector=N):
-            interleave(("out", a, c), result[a][:, :, c * N : (c + 1) * N], on_vector, c == N_C - 1)
+            interleave(("out", a, c), result[a][:, :, c * N : (c + 1) * N], on_vector, c == N_CHUNKS - 1)
 
         def quant_out(a, c):
             nc.vector.quantize_mx(
@@ -157,78 +170,78 @@ def tile_mix_dyq_fm_pl_none_kernel(tc, dy, w8_words, w8_scales, w4_words, w4_sca
                 in_=grouped["out", a, c][:].rearrange("p t j -> p (t j)"),
             )
 
-        def store_result(a, r0, r1, c0, c1):
+        def store_result(a, r0, r1, c0=0, c1=N_CHUNKS):
             rows = out_0[a * SPAN : (a + 1) * SPAN, :].rearrange("(p r) t -> p r t", r=PACK)
             nc.sync.dma_start(out=rows[:, r0:r1, c0 * N : c1 * N], in_=result[a][:, r0:r1, c0 * N : c1 * N])
 
-        def store_scales():
-            for q in range(4):
-                nc.gpsimd.dma_start(
-                    out=out_2[:, 4 * q : 4 * q + 4, :].bitcast(I32),
-                    in_=out_scales[32 * q + 4 : 32 * q + 16, :].bitcast(I32),
-                )
+        def multiply_and_store_slot(a, r):
+            for c in range(N_CHUNKS):
+                multiply(a, c, (r,))
+            store_result(a, r, r + 1)
 
         def store_codes(a):
             nc.sync.dma_start(out=out_1[a].rearrange("p t i -> p (t i)").bitcast(I32), in_=out_codes[a][:])
 
+        def store_scales():
+            for q in range(P // QUADRANT):
+                nc.gpsimd.dma_start(
+                    out=out_2[:, 4 * q : 4 * q + 4, :].bitcast(I32),
+                    in_=out_scales[QUADRANT * q + 4 : QUADRANT * q + 16, :].bitcast(I32),
+                )
+
         nc.vector.memset(ws_raw[1][:].bitcast(I32), 0)
         nc.vector.memset(ws_raw[0][:].bitcast(I32), 0)
+
         load_w4(0)
         load_w8(0)
         load_scales(1)
         load_dy(0, 0)
-        load_scales(0)
-        load_dy(1, 0)
-        load_dy(1, 1)
-        load_dy(1, 2)
+        load_scales(0, 0, 1)
+        for part in range(N_CHUNKS):
+            load_dy(1, part)
+        load_scales(0, 1, 3)
         load_w4(1)
         load_w8(1)
+
         deal_w4(0)
         deal_scales(1, 0)
         deal_w8(0)
-        deal_scales(1, 1)
         deal_scales(1, 2)
+
         group_dy(0, 0)
-        group_dy(0, 2, 0)
+        group_dy(0, 2, on_vector=0)
         deal_scales(0, 0)
         quant_dy(0, 0)
         group_dy(0, 1)
-        open_banks(0, 0, range(4))
-        group_dy(1, 0, 256)
+        open_banks(0, 0, range(PACK))
+        group_dy(1, 0, SHARE_FIRST)
         quant_dy(0, 1)
         quant_dy(1, 0)
-        group_dy(1, 1, 384)
-        close_banks(0, 0, range(4))
+        group_dy(1, 1, SHARE_SECOND)
+        close_banks(0, 0, range(PACK))
         open_banks(0, 1, (2, 3, 0, 1))
         store_result(0, 0, 2, 0, 1)
-        deal_scales(0, 1)
+        deal_scales(1, 1)
         quant_dy(1, 1)
         quant_dy(0, 2)
-        close_banks(0, 1, (2,))
-        store_result(0, 2, 3, 0, 2)
-        close_banks(0, 1, (3,))
-        store_result(0, 3, 4, 0, 2)
+        for r in (2, 3):
+            close_banks(0, 1, (r,))
+            store_result(0, r, r + 1, 0, 2)
         close_banks(0, 1, (0, 1))
-        open_banks(0, 2, range(4))
+        open_banks(0, 2, range(PACK))
         group_dy(1, 2)
-        deal_scales(0, 2)
+        deal_scales(0, 1)
         quant_dy(1, 2)
-        close_banks(0, 2, (0,))
-        store_result(0, 0, 1, 1, 3)
-        close_banks(0, 2, (1,))
-        store_result(0, 1, 2, 1, 3)
+        for r in (0, 1):
+            close_banks(0, 2, (r,))
+            store_result(0, r, r + 1, 1, 3)
         close_banks(0, 2, (2, 3))
         store_result(0, 2, 4, 2, 3)
+
         deal_w4(1)
         deal_w8(1)
-        multiply(1, 0, (0,))
-        multiply(1, 1, (0,))
-        multiply(1, 2, (0,))
-        store_result(1, 0, 1, 0, 3)
-        multiply(1, 0, (1,))
-        multiply(1, 1, (1,))
-        multiply(1, 2, (1,))
-        store_result(1, 1, 2, 0, 3)
+        multiply_and_store_slot(1, 0)
+        multiply_and_store_slot(1, 1)
         group_out(0, 0)
         group_out(0, 1)
         quant_out(0, 0)
@@ -237,29 +250,29 @@ def tile_mix_dyq_fm_pl_none_kernel(tc, dy, w8_words, w8_scales, w4_words, w4_sca
         deal_w4(2)
         quant_out(0, 2)
         deal_w8(2)
-        multiply(1, 0, (2, 3))
-        multiply(1, 1, (2, 3))
-        multiply(1, 2, (2, 3))
+        deal_scales(0, 2)
+        for c in range(N_CHUNKS):
+            multiply(1, c, (2, 3))
         store_codes(0)
-        store_result(1, 2, 4, 0, 3)
+        store_result(1, 2, 4)
+
         group_out(1, 0)
         group_out(1, 1)
         quant_out(1, 0)
         group_out(1, 2)
         quant_out(1, 1)
-        multiply(2, 0, range(4))
+        multiply_and_store_slot(2, 0)
+        multiply(2, 0, (1, 2, 3))
         quant_out(1, 2)
         store_codes(1)
         group_out(2, 0)
-        multiply(2, 1, range(4))
+        multiply(2, 1, (1, 2, 3))
         group_out(2, 1)
         quant_out(2, 0)
         quant_out(2, 1)
-        multiply(2, 2, (0, 1))
-        store_result(2, 0, 2, 0, 3)
-        multiply(2, 2, (2, 3))
-        store_result(2, 2, 4, 0, 3)
-        group_out(2, 2, 192)
+        multiply(2, 2, (1, 2, 3))
+        store_result(2, 1, 4)
+        group_out(2, 2, SHARE_LAST)
         quant_out(2, 2)
         store_scales()
         store_codes(2)

@@ -184,7 +184,7 @@ def tile_mix_dyq_fm_pl_none_kernel(tc, dy, w8_words, w8_scales, w4_words, w4_sca
 
         def store_scales():
             for q in range(P // QUADRANT):
-                nc.gpsimd.dma_start(
+                (nc.gpsimd, nc.scalar)[q // 2].dma_start(
                     out=out_2[:, 4 * q : 4 * q + 4, :].bitcast(I32),
                     in_=out_scales[QUADRANT * q + 4 : QUADRANT * q + 16, :].bitcast(I32),
                 )

@@ -184,7 +184,7 @@ def tile_mix_dyq_fm_pl_none_kernel(tc, dy, w8_words, w8_scales, w4_words, w4_sca
 
         def store_scales():
             for q in range(P // QUADRANT):
-                (nc.gpsimd, nc.scalar)[q // 2].dma_start(
+                nc.scalar.dma_start(
                     out=out_2[:, 4 * q : 4 * q + 4, :].bitcast(I32),
                     in_=out_scales[QUADRANT * q + 4 : QUADRANT * q + 16, :].bitcast(I32),
                 )

@@ -24,11 +24,9 @@ QUADRANT = 32
 LINE = 16
 RUN = 4
 STAGED = 6
-DY_LOADS = (((0, 3),), ((0, 1), (1, 2), (2, 3)))
+DY_CUTS = ((0, T), (0, 768, 1280, T))
+EARLY_BANKS = ((0, 0), (0, 1), (0, 2), (1, 2), (0, 3), (1, 3), (1, 0), (1, 1))
 W_LOADS = ((0, 1), (1, 3))
-SHARE_FIRST = 256
-SHARE_SECOND = 384
-SHARE_LAST = 192
 
 
 def tile_mix_dyq_fm_pl_none_kernel(tc, dy, w8_words, w8_scales, w4_words, w4_scales, out_0, out_1, out_2):
@@ -46,8 +44,8 @@ def tile_mix_dyq_fm_pl_none_kernel(tc, dy, w8_words, w8_scales, w4_words, w4_sca
             w4_raw[a0] = keep.tile([P, 2 * (a1 - a0) * SPAN], U8, name="w4_raw_%d" % a0, align_bytes=64)
         dy_raw, dy_codes, dy_scales, result, out_codes = {}, {}, {}, {}, {}
         for g in range(2):
-            for c0, c1 in DY_LOADS[g]:
-                dy_raw[g, c0] = keep.tile([P, PACK, (c1 - c0) * N], F32, name="dy_raw_%d_%d" % (g, c0), align_bytes=64)
+            for t0, t1 in zip(DY_CUTS[g], DY_CUTS[g][1:]):
+                dy_raw[g, t0] = keep.tile([P, PACK, t1 - t0], F32, name="dy_raw_%d_%d" % (g, t0), align_bytes=64)
             for c in range(N_CHUNKS):
                 dy_codes[c, g] = keep.tile([P, N], I32, name="dy_codes_%d_%d" % (c, g), align_bytes=64)
                 dy_scales[c, g] = keep.tile([P, N], U8, name="dy_scales_%d_%d" % (c, g), align_bytes=64)
@@ -64,9 +62,9 @@ def tile_mix_dyq_fm_pl_none_kernel(tc, dy, w8_words, w8_scales, w4_words, w4_sca
             return max(lo for lo, hi in ranges if lo <= index)
 
         def load_dy(g, part):
-            c0, c1 = DY_LOADS[g][part]
-            rows = dy[g * SPAN : (g + 1) * SPAN, c0 * N : c1 * N]
-            nc.sync.dma_start(out=dy_raw[g, c0][:], in_=rows.rearrange("(p j) t -> p j t", j=PACK))
+            t0, t1 = DY_CUTS[g][part : part + 2]
+            rows = dy[g * SPAN : (g + 1) * SPAN, t0:t1]
+            nc.sync.dma_start(out=dy_raw[g, t0][:], in_=rows.rearrange("(p j) t -> p j t", j=PACK))
 
         def load_scales(g, a0=0, a1=N_SPANS):
             scales = (w8_scales, w4_scales)[g]
@@ -101,30 +99,29 @@ def tile_mix_dyq_fm_pl_none_kernel(tc, dy, w8_words, w8_scales, w4_words, w4_sca
             deal(ws[g, a][:], ws_raw[g][:, a * SPAN : (a + 1) * SPAN], LINE)
 
         grouped = {}
+        on_vector, on_scalar = nc.vector.tensor_copy, nc.scalar.copy
 
-        def interleave(key, src, on_vector, in_runs):
-            tile = stage.tile([P, N, PACK], BF16, name="grouped", align_bytes=64)
-            grouped[key] = tile
-            for copy, lo, hi in ((nc.vector.tensor_copy, 0, on_vector), (nc.scalar.copy, on_vector, N)):
-                if lo == hi:
-                    continue
-                if in_runs:
-                    copy(
-                        out=tile[:, lo:hi, :].rearrange("p (c i) j -> p c j i", i=RUN),
-                        in_=src[:, :, lo:hi].rearrange("p j (c i) -> p c j i", i=RUN),
-                    )
-                else:
-                    copy(out=tile[:, lo:hi, :], in_=src[:, :, lo:hi].rearrange("p j t -> p t j"))
+        def interleave(key, src, copy, lo, hi, in_runs):
+            if key not in grouped:
+                grouped[key] = stage.tile([P, N, PACK], BF16, name="grouped", align_bytes=64)
+            out = grouped[key][:, lo:hi, :]
+            if in_runs:
+                copy(
+                    out=out.rearrange("p (c i) j -> p c j i", i=RUN),
+                    in_=src.rearrange("p j (c i) -> p c j i", i=RUN),
+                )
+            else:
+                copy(out=out, in_=src.rearrange("p j t -> p t j"))
 
-        def group_dy(g, c, on_vector=N):
-            c0 = first_of(DY_LOADS[g], c)
-            interleave(("dy", g, c), dy_raw[g, c0][:, :, (c - c0) * N : (c - c0 + 1) * N], on_vector, True)
+        def group_dy(g, c, copy, lo=0, hi=N):
+            t0 = max(t for t in DY_CUTS[g] if t <= c * N + lo)
+            interleave(("dy", g, c), dy_raw[g, t0][:, :, c * N + lo - t0 : c * N + hi - t0], copy, lo, hi, True)
 
-        def quant_dy(g, c):
+        def quant_dy(g, c, lo=0, hi=N):
             nc.vector.quantize_mx(
-                out=dy_codes[c, g][:].bitcast(E5M2),
-                scales=dy_scales[c, g][:],
-                in_=grouped["dy", g, c][:].rearrange("p t j -> p (t j)"),
+                out=dy_codes[c, g][:, lo:hi].bitcast(E5M2),
+                scales=dy_scales[c, g][:, lo:hi],
+                in_=grouped["dy", g, c][:, lo:hi, :].rearrange("p t j -> p (t j)"),
             )
 
         banks = {}
@@ -142,7 +139,7 @@ def tile_mix_dyq_fm_pl_none_kernel(tc, dy, w8_words, w8_scales, w4_words, w4_sca
                     stop=False,
                 )
 
-        def close_banks(a, c, slots):
+        def end_sums(a, c, slots):
             for r in slots:
                 nc.tensor.matmul_mx(
                     out=banks[a, c, r][:],
@@ -153,15 +150,23 @@ def tile_mix_dyq_fm_pl_none_kernel(tc, dy, w8_words, w8_scales, w4_words, w4_sca
                     start=False,
                     stop=True,
                 )
-                nc.scalar.copy(out=result[a][:, r, c * N : (c + 1) * N], in_=banks[a, c, r][:])
 
-        def multiply(a, c, slots):
+        def drain(a, c, slots, copy=on_scalar):
+            for r in slots:
+                copy(out=result[a][:, r, c * N : (c + 1) * N], in_=banks[a, c, r][:])
+
+        def close_banks(a, c, slots, copy=on_scalar):
+            for r in slots:
+                end_sums(a, c, (r,))
+                drain(a, c, (r,), copy)
+
+        def multiply(a, c, slots, copy=nc.scalar.copy):
             for r in slots:
                 open_banks(a, c, (r,))
-                close_banks(a, c, (r,))
+                close_banks(a, c, (r,), copy)
 
-        def group_out(a, c, on_vector=N):
-            interleave(("out", a, c), result[a][:, :, c * N : (c + 1) * N], on_vector, c == N_CHUNKS - 1)
+        def group_out(a, c, copy, in_runs, lo=0, hi=N):
+            interleave(("out", a, c), result[a][:, :, c * N + lo : c * N + hi], copy, lo, hi, in_runs)
 
         def quant_out(a, c):
             nc.vector.quantize_mx(
@@ -170,14 +175,13 @@ def tile_mix_dyq_fm_pl_none_kernel(tc, dy, w8_words, w8_scales, w4_words, w4_sca
                 in_=grouped["out", a, c][:].rearrange("p t j -> p (t j)"),
             )
 
-        def store_result(a, r0, r1, c0=0, c1=N_CHUNKS):
-            rows = out_0[a * SPAN : (a + 1) * SPAN, :].rearrange("(p r) t -> p r t", r=PACK)
-            nc.sync.dma_start(out=rows[:, r0:r1, c0 * N : c1 * N], in_=result[a][:, r0:r1, c0 * N : c1 * N])
+        def store_result(a, lo, hi):
+            rows = out_0[a * SPAN : (a + 1) * SPAN, :].rearrange("(p r) t -> p (r t)", r=PACK)
+            nc.sync.dma_start(out=rows[:, lo * N : hi * N], in_=result[a][:].rearrange("p r t -> p (r t)")[:, lo * N : hi * N])
 
-        def multiply_and_store_slot(a, r):
-            for c in range(N_CHUNKS):
-                multiply(a, c, (r,))
-            store_result(a, r, r + 1)
+        def store_chunk(a, r0, r1, c):
+            rows = out_0[a * SPAN : (a + 1) * SPAN, :].rearrange("(p r) t -> p r t", r=PACK)
+            nc.sync.dma_start(out=rows[:, r0:r1, c * N : (c + 1) * N], in_=result[a][:, r0:r1, c * N : (c + 1) * N])
 
         def store_codes(a):
             nc.sync.dma_start(out=out_1[a].rearrange("p t i -> p (t i)").bitcast(I32), in_=out_codes[a][:])
@@ -200,79 +204,102 @@ def tile_mix_dyq_fm_pl_none_kernel(tc, dy, w8_words, w8_scales, w4_words, w4_sca
         for part in range(N_CHUNKS):
             load_dy(1, part)
         load_scales(0, 1, 3)
-        load_w4(1)
         load_w8(1)
+        load_w4(1)
 
         deal_w4(0)
-        deal_scales(1, 0)
         deal_w8(0)
-        deal_scales(1, 2)
+        for a in range(N_SPANS):
+            deal_scales(1, a)
 
-        group_dy(0, 0)
-        group_dy(0, 2, on_vector=0)
+        group_dy(0, 0, on_vector)
+        group_dy(0, 1, on_scalar)
         deal_scales(0, 0)
         quant_dy(0, 0)
-        group_dy(0, 1)
-        open_banks(0, 0, range(PACK))
-        group_dy(1, 0, SHARE_FIRST)
+        group_dy(0, 2, on_vector, 0, 320)
+        group_dy(0, 2, on_scalar, 320, N)
         quant_dy(0, 1)
+        for c, r in EARLY_BANKS[:6]:
+            open_banks(0, c, (r,))
+        group_dy(1, 0, on_vector, 0, 340)
+        group_dy(1, 0, on_scalar, 340, N)
+        group_dy(1, 1, on_scalar, 64, 256)
+        group_dy(1, 1, on_vector, 0, 64)
         quant_dy(1, 0)
-        group_dy(1, 1, SHARE_SECOND)
-        close_banks(0, 0, range(PACK))
-        open_banks(0, 1, (2, 3, 0, 1))
-        store_result(0, 0, 2, 0, 1)
-        deal_scales(1, 1)
-        quant_dy(1, 1)
         quant_dy(0, 2)
-        for r in (2, 3):
-            close_banks(0, 1, (r,))
-            store_result(0, r, r + 1, 0, 2)
-        close_banks(0, 1, (0, 1))
-        open_banks(0, 2, range(PACK))
-        group_dy(1, 2)
+        quant_dy(1, 1, 0, 256)
+        group_dy(1, 1, on_vector, 256, N)
+        group_dy(1, 2, on_vector, 0, 128)
+        quant_dy(1, 1, 256, N)
+        group_dy(1, 2, on_vector, 128, 256)
+        group_dy(1, 2, on_vector, 256, N)
+        quant_dy(1, 2, 0, 256)
+        quant_dy(1, 2, 256, N)
         deal_scales(0, 1)
-        quant_dy(1, 2)
-        for r in (0, 1):
-            close_banks(0, 2, (r,))
-            store_result(0, r, r + 1, 1, 3)
-        close_banks(0, 2, (2, 3))
-        store_result(0, 2, 4, 2, 3)
-
-        deal_w4(1)
         deal_w8(1)
-        multiply_and_store_slot(1, 0)
-        multiply_and_store_slot(1, 1)
-        group_out(0, 0)
-        group_out(0, 1)
-        quant_out(0, 0)
-        group_out(0, 2)
-        quant_out(0, 1)
-        deal_w4(2)
-        quant_out(0, 2)
-        deal_w8(2)
-        deal_scales(0, 2)
-        for c in range(N_CHUNKS):
-            multiply(1, c, (2, 3))
-        store_codes(0)
-        store_result(1, 2, 4)
+        deal_w4(1)
+        end_sums(0, 0, range(PACK))
+        for c, r in EARLY_BANKS[6:]:
+            open_banks(0, c, (r,))
+        end_sums(0, 1, (2, 3, 0, 1))
+        drain(0, 0, (0, 1))
+        store_chunk(0, 0, 2, 0)
+        drain(0, 0, (2,))
+        drain(0, 1, (2,))
+        store_result(0, 6, 8)
+        drain(0, 0, (3,))
+        drain(0, 1, (3,))
+        store_result(0, 9, 11)
+        drain(0, 1, (0,))
+        drain(0, 1, (1,), on_vector)
+        open_banks(0, 2, range(PACK))
+        close_banks(0, 2, (0,))
+        store_result(0, 1, 3)
+        close_banks(0, 2, (1,))
+        store_result(0, 4, 6)
+        close_banks(0, 2, (2,))
+        close_banks(0, 2, (3,), on_scalar)
+        store_chunk(0, 2, 4, 2)
 
-        group_out(1, 0)
-        group_out(1, 1)
+        for r in (0, 1):
+            for c in range(N_CHUNKS):
+                multiply(1, c, (r,))
+            store_result(1, 3 * r, 3 * r + 3)
+        group_out(0, 0, on_vector, False)
+        deal_scales(0, 2)
+        deal_w8(2)
+        quant_out(0, 0)
+        group_out(0, 1, on_vector, True)
+        deal_w4(2)
+        group_out(0, 2, on_vector, True)
+        quant_out(0, 1)
+        quant_out(0, 2)
+        store_codes(0)
+        multiply(1, 0, (2, 3))
+        group_out(1, 0, on_vector, False)
+        multiply(1, 1, (2, 3))
+        multiply(1, 2, (2, 3))
+        store_result(1, 6, 12)
+        group_out(1, 1, on_vector, True)
         quant_out(1, 0)
-        group_out(1, 2)
+        group_out(1, 2, on_vector, True)
         quant_out(1, 1)
-        multiply_and_store_slot(2, 0)
-        multiply(2, 0, (1, 2, 3))
         quant_out(1, 2)
+        for r in range(1):
+            for c in range(N_CHUNKS):
+                multiply(2, c, (r,))
+        store_result(2, 0, 3)
         store_codes(1)
-        group_out(2, 0)
-        multiply(2, 1, (1, 2, 3))
-        group_out(2, 1)
+        multiply(2, 0, range(1, PACK))
+        group_out(2, 0, on_vector, False)
+        multiply(2, 1, range(1, PACK))
+        group_out(2, 1, on_vector, False)
         quant_out(2, 0)
         quant_out(2, 1)
-        multiply(2, 2, (1, 2, 3))
-        store_result(2, 1, 4)
-        group_out(2, 2, SHARE_LAST)
+        multiply(2, 2, range(1, PACK))
+        store_result(2, 3, 12)
+        group_out(2, 2, on_vector, True, 0, 192)
+        group_out(2, 2, on_scalar, True, 192, N)
         quant_out(2, 2)
         store_scales()
         store_codes(2)

@@ -24,9 +24,14 @@ QUADRANT = 32
 LINE = 16
 RUN = 4
 STAGED = 6
-DY_CUTS = ((0, T), (0, 768, 1280, T))
-EARLY_BANKS = ((0, 0), (0, 1), (0, 2), (1, 2), (0, 3), (1, 3), (1, 0), (1, 1))
+HALF = N // 2
+DY_CUTS = ((0, T), (0, 768, 1152, T))
 W_LOADS = ((0, 1), (1, 3))
+EARLY_BANKS = [(0, r) for r in range(PACK)] + [(1, r) for r in (2, 3, 0, 1)]
+OPEN_AHEAD = 5
+SHARE_HALF_0 = 320
+SHARE_HALF_1 = 344
+SHARE_LAST = 192
 
 
 def tile_mix_dyq_fm_pl_none_kernel(tc, dy, w8_words, w8_scales, w4_words, w4_scales, out_0, out_1, out_2):
@@ -155,15 +160,15 @@ def tile_mix_dyq_fm_pl_none_kernel(tc, dy, w8_words, w8_scales, w4_words, w4_sca
             for r in slots:
                 copy(out=result[a][:, r, c * N : (c + 1) * N], in_=banks[a, c, r][:])
 
-        def close_banks(a, c, slots, copy=on_scalar):
+        def close_banks(a, c, slots):
             for r in slots:
                 end_sums(a, c, (r,))
-                drain(a, c, (r,), copy)
+                drain(a, c, (r,))
 
-        def multiply(a, c, slots, copy=nc.scalar.copy):
+        def multiply(a, c, slots):
             for r in slots:
                 open_banks(a, c, (r,))
-                close_banks(a, c, (r,), copy)
+                close_banks(a, c, (r,))
 
         def group_out(a, c, copy, in_runs, lo=0, hi=N):
             interleave(("out", a, c), result[a][:, :, c * N + lo : c * N + hi], copy, lo, hi, in_runs)
@@ -175,13 +180,14 @@ def tile_mix_dyq_fm_pl_none_kernel(tc, dy, w8_words, w8_scales, w4_words, w4_sca
                 in_=grouped["out", a, c][:].rearrange("p t j -> p (t j)"),
             )
 
-        def store_result(a, lo, hi):
-            rows = out_0[a * SPAN : (a + 1) * SPAN, :].rearrange("(p r) t -> p (r t)", r=PACK)
-            nc.sync.dma_start(out=rows[:, lo * N : hi * N], in_=result[a][:].rearrange("p r t -> p (r t)")[:, lo * N : hi * N])
-
-        def store_chunk(a, r0, r1, c):
+        def store_result(a, r0, r1, c0=0, c1=N_CHUNKS):
             rows = out_0[a * SPAN : (a + 1) * SPAN, :].rearrange("(p r) t -> p r t", r=PACK)
-            nc.sync.dma_start(out=rows[:, r0:r1, c * N : (c + 1) * N], in_=result[a][:, r0:r1, c * N : (c + 1) * N])
+            nc.sync.dma_start(out=rows[:, r0:r1, c0 * N : c1 * N], in_=result[a][:, r0:r1, c0 * N : c1 * N])
+
+        def multiply_and_store_slot(a, r):
+            for c in range(N_CHUNKS):
+                multiply(a, c, (r,))
+            store_result(a, r, r + 1)
 
         def store_codes(a):
             nc.sync.dma_start(out=out_1[a].rearrange("p t i -> p (t i)").bitcast(I32), in_=out_codes[a][:])
@@ -201,7 +207,7 @@ def tile_mix_dyq_fm_pl_none_kernel(tc, dy, w8_words, w8_scales, w4_words, w4_sca
         load_scales(1)
         load_dy(0, 0)
         load_scales(0, 0, 1)
-        for part in range(N_CHUNKS):
+        for part in range(len(DY_CUTS[1]) - 1):
             load_dy(1, part)
         load_scales(0, 1, 3)
         load_w8(1)
@@ -216,90 +222,92 @@ def tile_mix_dyq_fm_pl_none_kernel(tc, dy, w8_words, w8_scales, w4_words, w4_sca
         group_dy(0, 1, on_scalar)
         deal_scales(0, 0)
         quant_dy(0, 0)
-        group_dy(0, 2, on_vector, 0, 320)
-        group_dy(0, 2, on_scalar, 320, N)
+        group_dy(0, 2, on_vector, 0, SHARE_HALF_0)
+        group_dy(0, 2, on_scalar, SHARE_HALF_0, N)
         quant_dy(0, 1)
-        for c, r in EARLY_BANKS[:6]:
+        for c, r in EARLY_BANKS[:OPEN_AHEAD]:
             open_banks(0, c, (r,))
-        group_dy(1, 0, on_vector, 0, 340)
-        group_dy(1, 0, on_scalar, 340, N)
-        group_dy(1, 1, on_scalar, 64, 256)
-        group_dy(1, 1, on_vector, 0, 64)
-        quant_dy(1, 0)
+
+        group_dy(1, 0, on_vector, 0, HALF)
+        group_dy(1, 0, on_vector, HALF, SHARE_HALF_1)
+        group_dy(1, 0, on_scalar, SHARE_HALF_1, N)
+        group_dy(1, 1, on_scalar, 0, HALF)
+        quant_dy(1, 0, 0, HALF)
+        quant_dy(1, 0, HALF, N)
         quant_dy(0, 2)
-        quant_dy(1, 1, 0, 256)
-        group_dy(1, 1, on_vector, 256, N)
-        group_dy(1, 2, on_vector, 0, 128)
-        quant_dy(1, 1, 256, N)
-        group_dy(1, 2, on_vector, 128, 256)
-        group_dy(1, 2, on_vector, 256, N)
-        quant_dy(1, 2, 0, 256)
-        quant_dy(1, 2, 256, N)
+        second_end = DY_CUTS[1][2] - 2 * N
+        group_dy(1, 1, on_vector, HALF, N)
+        quant_dy(1, 1, 0, HALF)
+        quant_dy(1, 1, HALF, N)
+        group_dy(1, 2, on_vector, 0, second_end)
+
+        end_sums(0, 0, range(PACK))
+        for c, r in EARLY_BANKS[OPEN_AHEAD:-1]:
+            open_banks(0, c, (r,))
+        end_sums(0, 1, (2,))
+        open_banks(0, 1, (1,))
+        end_sums(0, 1, (3, 0, 1))
+        for r in (0, 1):
+            drain(0, 0, (r,))
+            store_result(0, r, r + 1, 0, 1)
+        drain(0, 0, (2,), on_vector)
+        group_dy(1, 2, on_vector, second_end, HALF)
+        group_dy(1, 2, on_vector, HALF, N)
+        quant_dy(1, 2, 0, HALF)
+        quant_dy(1, 2, HALF, N)
         deal_scales(0, 1)
         deal_w8(1)
         deal_w4(1)
-        end_sums(0, 0, range(PACK))
-        for c, r in EARLY_BANKS[6:]:
-            open_banks(0, c, (r,))
-        end_sums(0, 1, (2, 3, 0, 1))
-        drain(0, 0, (0, 1))
-        store_chunk(0, 0, 2, 0)
-        drain(0, 0, (2,))
-        drain(0, 1, (2,))
-        store_result(0, 6, 8)
         drain(0, 0, (3,))
-        drain(0, 1, (3,))
-        store_result(0, 9, 11)
-        drain(0, 1, (0,))
-        drain(0, 1, (1,), on_vector)
-        open_banks(0, 2, range(PACK))
-        close_banks(0, 2, (0,))
-        store_result(0, 1, 3)
-        close_banks(0, 2, (1,))
-        store_result(0, 4, 6)
-        close_banks(0, 2, (2,))
-        close_banks(0, 2, (3,), on_scalar)
-        store_chunk(0, 2, 4, 2)
+        for r in (2, 3):
+            drain(0, 1, (r,))
+            store_result(0, r, r + 1, 0, 2)
+        drain(0, 1, (0, 1))
 
-        for r in (0, 1):
-            for c in range(N_CHUNKS):
-                multiply(1, c, (r,))
-            store_result(1, 3 * r, 3 * r + 3)
+        open_banks(0, 2, (0, 1, 2))
+        close_banks(0, 2, (0,))
+        store_result(0, 0, 1, 1, 3)
+        open_banks(0, 2, (3,))
+        close_banks(0, 2, (1,))
+        store_result(0, 1, 2, 1, 3)
+        close_banks(0, 2, (2, 3))
+        store_result(0, 2, 4, 2, 3)
+
+        multiply_and_store_slot(1, 0)
+        multiply_and_store_slot(1, 1)
         group_out(0, 0, on_vector, False)
         deal_scales(0, 2)
-        deal_w8(2)
         quant_out(0, 0)
         group_out(0, 1, on_vector, True)
-        deal_w4(2)
         group_out(0, 2, on_vector, True)
         quant_out(0, 1)
         quant_out(0, 2)
+        deal_w8(2)
+        deal_w4(2)
         store_codes(0)
         multiply(1, 0, (2, 3))
         group_out(1, 0, on_vector, False)
         multiply(1, 1, (2, 3))
         multiply(1, 2, (2, 3))
-        store_result(1, 6, 12)
+        store_result(1, 2, 4)
+
         group_out(1, 1, on_vector, True)
         quant_out(1, 0)
         group_out(1, 2, on_vector, True)
         quant_out(1, 1)
         quant_out(1, 2)
-        for r in range(1):
-            for c in range(N_CHUNKS):
-                multiply(2, c, (r,))
-        store_result(2, 0, 3)
+        multiply_and_store_slot(2, 0)
         store_codes(1)
-        multiply(2, 0, range(1, PACK))
+        multiply(2, 0, (1, 2, 3))
         group_out(2, 0, on_vector, False)
-        multiply(2, 1, range(1, PACK))
+        multiply(2, 1, (1, 2, 3))
         group_out(2, 1, on_vector, False)
         quant_out(2, 0)
         quant_out(2, 1)
-        multiply(2, 2, range(1, PACK))
-        store_result(2, 3, 12)
-        group_out(2, 2, on_vector, True, 0, 192)
-        group_out(2, 2, on_scalar, True, 192, N)
+        multiply(2, 2, (1, 2, 3))
+        store_result(2, 1, 4)
+        group_out(2, 2, on_vector, True, 0, SHARE_LAST)
+        group_out(2, 2, on_scalar, True, SHARE_LAST, N)
         quant_out(2, 2)
         store_scales()
         store_codes(2)

@@ -194,7 +194,7 @@ def tile_mix_dyq_fm_pl_none_kernel(tc, dy, w8_words, w8_scales, w4_words, w4_sca
 
         def store_scales():
             for q in range(P // QUADRANT):
-                nc.scalar.dma_start(
+                nc.sync.dma_start(
                     out=out_2[:, 4 * q : 4 * q + 4, :].bitcast(I32),
                     in_=out_scales[QUADRANT * q + 4 : QUADRANT * q + 16, :].bitcast(I32),
                 )
@@ -309,5 +309,5 @@ def tile_mix_dyq_fm_pl_none_kernel(tc, dy, w8_words, w8_scales, w4_words, w4_sca
         group_out(2, 2, on_vector, True, 0, SHARE_LAST)
         group_out(2, 2, on_scalar, True, SHARE_LAST, N)
         quant_out(2, 2)
-        store_scales()
         store_codes(2)
+        store_scales()

@@ -20,6 +20,7 @@ SPAN = P * PACK
 N = 512
 N_SPANS = D // SPAN
 N_CHUNKS = T // N
+ALIGN = 256
 QUADRANT = 32
 LINE = 16
 RUN = 4
@@ -42,26 +43,26 @@ def tile_mix_dyq_fm_pl_none_kernel(tc, dy, w8_words, w8_scales, w4_words, w4_sca
         psum = ctx.enter_context(tc.psum_pool(name="psum", bufs=8))
         ctx.enter_context(tc.manual_schedule())
 
-        ws_raw = [keep.tile([P, D], U8, name="ws_raw_%d" % g, align_bytes=64) for g in range(2)]
+        ws_raw = [keep.tile([P, D], U8, name="ws_raw_%d" % g, align_bytes=ALIGN) for g in range(2)]
         w8_raw, w4_raw, w8, w4, ws = {}, {}, {}, {}, {}
         for a0, a1 in W_LOADS:
-            w8_raw[a0] = keep.tile([P, (a1 - a0) * SPAN], I32, name="w8_raw_%d" % a0, align_bytes=64)
-            w4_raw[a0] = keep.tile([P, 2 * (a1 - a0) * SPAN], U8, name="w4_raw_%d" % a0, align_bytes=64)
+            w8_raw[a0] = keep.tile([P, (a1 - a0) * SPAN], I32, name="w8_raw_%d" % a0, align_bytes=ALIGN)
+            w4_raw[a0] = keep.tile([P, 2 * (a1 - a0) * SPAN], U8, name="w4_raw_%d" % a0, align_bytes=ALIGN)
         dy_raw, dy_codes, dy_scales, result, out_codes = {}, {}, {}, {}, {}
         for g in range(2):
             for t0, t1 in zip(DY_CUTS[g], DY_CUTS[g][1:]):
-                dy_raw[g, t0] = keep.tile([P, PACK, t1 - t0], F32, name="dy_raw_%d_%d" % (g, t0), align_bytes=64)
+                dy_raw[g, t0] = keep.tile([P, PACK, t1 - t0], F32, name="dy_raw_%d_%d" % (g, t0), align_bytes=ALIGN)
             for c in range(N_CHUNKS):
-                dy_codes[c, g] = keep.tile([P, N], I32, name="dy_codes_%d_%d" % (c, g), align_bytes=64)
-                dy_scales[c, g] = keep.tile([P, N], U8, name="dy_scales_%d_%d" % (c, g), align_bytes=64)
+                dy_codes[c, g] = keep.tile([P, N], I32, name="dy_codes_%d_%d" % (c, g), align_bytes=ALIGN)
+                dy_scales[c, g] = keep.tile([P, N], U8, name="dy_scales_%d_%d" % (c, g), align_bytes=ALIGN)
         for a in range(N_SPANS):
-            w8[a] = keep.tile([P, SPAN], I32, name="w8_%d" % a, align_bytes=64)
-            w4[a] = keep.tile([P, 2 * SPAN], U8, name="w4_%d" % a, align_bytes=64)
+            w8[a] = keep.tile([P, SPAN], I32, name="w8_%d" % a, align_bytes=ALIGN)
+            w4[a] = keep.tile([P, 2 * SPAN], U8, name="w4_%d" % a, align_bytes=ALIGN)
             for g in range(2):
-                ws[g, a] = keep.tile([P, SPAN], U8, name="ws_%d_%d" % (g, a), align_bytes=64)
-            result[a] = keep.tile([P, PACK, T], F32, name="result_%d" % a, align_bytes=64)
-            out_codes[a] = keep.tile([P, T], I32, name="out_codes_%d" % a, align_bytes=64)
-        out_scales = keep.tile([P, T], U8, name="out_scales", align_bytes=64)
+                ws[g, a] = keep.tile([P, SPAN], U8, name="ws_%d_%d" % (g, a), align_bytes=ALIGN)
+            result[a] = keep.tile([P, PACK, T], F32, name="result_%d" % a, align_bytes=ALIGN)
+            out_codes[a] = keep.tile([P, T], I32, name="out_codes_%d" % a, align_bytes=ALIGN)
+        out_scales = keep.tile([P, T], U8, name="out_scales", align_bytes=ALIGN)
 
         def first_of(ranges, index):
             return max(lo for lo, hi in ranges if lo <= index)
@@ -108,7 +109,7 @@ def tile_mix_dyq_fm_pl_none_kernel(tc, dy, w8_words, w8_scales, w4_words, w4_sca
 
         def interleave(key, src, copy, lo, hi, in_runs):
             if key not in grouped:
-                grouped[key] = stage.tile([P, N, PACK], BF16, name="grouped", align_bytes=64)
+                grouped[key] = stage.tile([P, N, PACK], BF16, name="grouped", align_bytes=ALIGN)
             out = grouped[key][:, lo:hi, :]
             if in_runs:
                 copy(

@@ -26,11 +26,9 @@ LINE = 16
 RUN = 4
 STAGED = 6
 HALF = N // 2
-DY_CUTS = ((0, T), (0, 768, 1152, T))
-W_LOADS = ((0, 1), (1, 3))
-EARLY_BANKS = [(0, r) for r in range(PACK)] + [(1, r) for r in (2, 3, 0, 1)]
-OPEN_AHEAD = 5
-SHARE_HALF_0 = 320
+DY_CUTS = ((0, 2 * N, T), (0, N, 2 * N, T))
+OUT_CUTS = ((0, 1, 3), (0, 2, 3), (0, 3))
+W_LOADS = ((0, 3),)
 SHARE_HALF_1 = 344
 SHARE_LAST = 192
 
@@ -48,7 +46,7 @@ def tile_mix_dyq_fm_pl_none_kernel(tc, dy, w8_words, w8_scales, w4_words, w4_sca
         for a0, a1 in W_LOADS:
             w8_raw[a0] = keep.tile([P, (a1 - a0) * SPAN], I32, name="w8_raw_%d" % a0, align_bytes=ALIGN)
             w4_raw[a0] = keep.tile([P, 2 * (a1 - a0) * SPAN], U8, name="w4_raw_%d" % a0, align_bytes=ALIGN)
-        dy_raw, dy_codes, dy_scales, result, out_codes = {}, {}, {}, {}, {}
+        dy_raw, dy_codes, dy_scales, result = {}, {}, {}, {}
         for g in range(2):
             for t0, t1 in zip(DY_CUTS[g], DY_CUTS[g][1:]):
                 dy_raw[g, t0] = keep.tile([P, PACK, t1 - t0], F32, name="dy_raw_%d_%d" % (g, t0), align_bytes=ALIGN)
@@ -60,9 +58,14 @@ def tile_mix_dyq_fm_pl_none_kernel(tc, dy, w8_words, w8_scales, w4_words, w4_sca
             w4[a] = keep.tile([P, 2 * SPAN], U8, name="w4_%d" % a, align_bytes=ALIGN)
             for g in range(2):
                 ws[g, a] = keep.tile([P, SPAN], U8, name="ws_%d_%d" % (g, a), align_bytes=ALIGN)
-            result[a] = keep.tile([P, PACK, T], F32, name="result_%d" % a, align_bytes=ALIGN)
-            out_codes[a] = keep.tile([P, T], I32, name="out_codes_%d" % a, align_bytes=ALIGN)
+            for c0, c1 in zip(OUT_CUTS[a], OUT_CUTS[a][1:]):
+                result[a, c0] = keep.tile([P, PACK, (c1 - c0) * N], F32, name="result_%d_%d" % (a, c0), align_bytes=ALIGN)
+        out_codes = keep.tile([P, N_SPANS, T], I32, name="out_codes", align_bytes=ALIGN)
         out_scales = keep.tile([P, T], U8, name="out_scales", align_bytes=ALIGN)
+
+        def chunk_of_result(a, c):
+            c0 = max(cut for cut in OUT_CUTS[a] if cut <= c)
+            return result[a, c0][:, :, (c - c0) * N : (c - c0 + 1) * N]
 
         def first_of(ranges, index):
             return max(lo for lo, hi in ranges if lo <= index)
@@ -159,7 +162,7 @@ def tile_mix_dyq_fm_pl_none_kernel(tc, dy, w8_words, w8_scales, w4_words, w4_sca
 
         def drain(a, c, slots, copy=on_scalar):
             for r in slots:
-                copy(out=result[a][:, r, c * N : (c + 1) * N], in_=banks[a, c, r][:])
+                copy(out=chunk_of_result(a, c)[:, r, :], in_=banks[a, c, r][:])
 
         def close_banks(a, c, slots):
             for r in slots:
@@ -172,26 +175,23 @@ def tile_mix_dyq_fm_pl_none_kernel(tc, dy, w8_words, w8_scales, w4_words, w4_sca
                 close_banks(a, c, (r,))
 
         def group_out(a, c, copy, in_runs, lo=0, hi=N):
-            interleave(("out", a, c), result[a][:, :, c * N + lo : c * N + hi], copy, lo, hi, in_runs)
+            interleave(("out", a, c), chunk_of_result(a, c)[:, :, lo:hi], copy, lo, hi, in_runs)
 
         def quant_out(a, c):
             nc.vector.quantize_mx(
-                out=out_codes[a][:, c * N : (c + 1) * N].bitcast(E4M3),
+                out=out_codes[:, a, c * N : (c + 1) * N].bitcast(E4M3),
                 scales=out_scales[4 * (a + 1) : P, c * N : (c + 1) * N],
                 in_=grouped["out", a, c][:].rearrange("p t j -> p (t j)"),
             )
 
-        def store_result(a, r0, r1, c0=0, c1=N_CHUNKS):
+        def store_result(a, part, r0, r1):
+            c0, c1 = OUT_CUTS[a][part : part + 2]
             rows = out_0[a * SPAN : (a + 1) * SPAN, :].rearrange("(p r) t -> p r t", r=PACK)
-            nc.sync.dma_start(out=rows[:, r0:r1, c0 * N : c1 * N], in_=result[a][:, r0:r1, c0 * N : c1 * N])
+            nc.sync.dma_start(out=rows[:, r0:r1, c0 * N : c1 * N], in_=result[a, c0][:, r0:r1, :])
 
-        def multiply_and_store_slot(a, r):
-            for c in range(N_CHUNKS):
-                multiply(a, c, (r,))
-            store_result(a, r, r + 1)
-
-        def store_codes(a):
-            nc.sync.dma_start(out=out_1[a].rearrange("p t i -> p (t i)").bitcast(I32), in_=out_codes[a][:])
+        def store_codes(a0, a1):
+            words = out_1.rearrange("a p t i -> p a (t i)").bitcast(I32)
+            nc.sync.dma_start(out=words[:, a0:a1, :], in_=out_codes[:, a0:a1, :])
 
         def store_scales():
             for q in range(P // QUADRANT):
@@ -200,115 +200,110 @@ def tile_mix_dyq_fm_pl_none_kernel(tc, dy, w8_words, w8_scales, w4_words, w4_sca
                     in_=out_scales[QUADRANT * q + 4 : QUADRANT * q + 16, :].bitcast(I32),
                 )
 
-        nc.vector.memset(ws_raw[1][:].bitcast(I32), 0)
         nc.vector.memset(ws_raw[0][:].bitcast(I32), 0)
+        nc.vector.memset(ws_raw[1][:].bitcast(I32), 0)
 
-        load_w4(0)
         load_w8(0)
-        load_scales(1)
+        load_scales(0)
         load_dy(0, 0)
-        load_scales(0, 0, 1)
-        for part in range(len(DY_CUTS[1]) - 1):
-            load_dy(1, part)
-        load_scales(0, 1, 3)
-        load_w8(1)
-        load_w4(1)
+        load_scales(1)
+        load_w4(0)
+        load_dy(1, 0)
+        load_dy(1, 1)
+        load_dy(0, 1)
+        load_dy(1, 2)
 
-        deal_w4(0)
-        deal_w8(0)
         for a in range(N_SPANS):
-            deal_scales(1, a)
-
-        group_dy(0, 0, on_vector)
+            deal_w8(a)
+        for a in range(N_SPANS):
+            deal_scales(0, a)
+        group_dy(0, 0, on_vector, 0, HALF)
+        group_dy(0, 0, on_vector, HALF, SHARE_HALF_1)
+        group_dy(0, 0, on_scalar, SHARE_HALF_1, N)
         group_dy(0, 1, on_scalar)
-        deal_scales(0, 0)
-        quant_dy(0, 0)
-        group_dy(0, 2, on_vector, 0, SHARE_HALF_0)
-        group_dy(0, 2, on_scalar, SHARE_HALF_0, N)
+        quant_dy(0, 0, 0, HALF)
+        quant_dy(0, 0, HALF, N)
+        deal_scales(1, 0)
+        deal_w4(0)
+        deal_scales(1, 1)
         quant_dy(0, 1)
-        for c, r in EARLY_BANKS[:OPEN_AHEAD]:
-            open_banks(0, c, (r,))
+        open_banks(0, 0, range(PACK))
+        open_banks(1, 0, (0, 1))
+        open_banks(1, 1, (0, 1))
 
         group_dy(1, 0, on_vector, 0, HALF)
         group_dy(1, 0, on_vector, HALF, SHARE_HALF_1)
         group_dy(1, 0, on_scalar, SHARE_HALF_1, N)
-        group_dy(1, 1, on_scalar, 0, HALF)
         quant_dy(1, 0, 0, HALF)
         quant_dy(1, 0, HALF, N)
-        quant_dy(0, 2)
-        second_end = DY_CUTS[1][2] - 2 * N
+        deal_w4(1)
+        group_dy(1, 1, on_vector, 0, HALF)
         group_dy(1, 1, on_vector, HALF, N)
         quant_dy(1, 1, 0, HALF)
         quant_dy(1, 1, HALF, N)
-        group_dy(1, 2, on_vector, 0, second_end)
-
         end_sums(0, 0, range(PACK))
-        for c, r in EARLY_BANKS[OPEN_AHEAD:-1]:
-            open_banks(0, c, (r,))
-        end_sums(0, 1, (2,))
-        open_banks(0, 1, (1,))
-        end_sums(0, 1, (3, 0, 1))
-        for r in (0, 1):
-            drain(0, 0, (r,))
-            store_result(0, r, r + 1, 0, 1)
-        drain(0, 0, (2,), on_vector)
-        group_dy(1, 2, on_vector, second_end, HALF)
+        end_sums(1, 0, (0, 1))
+        drain(0, 0, (0, 1))
+        store_result(0, 0, 0, 2)
+        drain(0, 0, (2,))
+        drain(0, 0, (3,), on_vector)
+        store_result(0, 0, 2, 4)
+        drain(1, 0, (0, 1))
+        open_banks(1, 0, (2,))
+        end_sums(1, 0, (2,))
+        end_sums(1, 1, (0, 1))
+        drain(1, 1, (0, 1))
+        store_result(1, 0, 0, 2)
+        group_dy(0, 2, on_vector)
+        deal_scales(1, 2)
+        quant_dy(0, 2)
+        drain(1, 0, (2,))
+        multiply(1, 0, (3,))
+        multiply(1, 1, (2, 3))
+        store_result(1, 0, 2, 4)
+
+        group_dy(1, 2, on_vector, 0, HALF)
         group_dy(1, 2, on_vector, HALF, N)
         quant_dy(1, 2, 0, HALF)
         quant_dy(1, 2, HALF, N)
-        deal_scales(0, 1)
-        deal_w8(1)
-        deal_w4(1)
-        drain(0, 0, (3,))
-        for r in (2, 3):
-            drain(0, 1, (r,))
-            store_result(0, r, r + 1, 0, 2)
-        drain(0, 1, (0, 1))
-
-        open_banks(0, 2, (0, 1, 2))
-        close_banks(0, 2, (0,))
-        store_result(0, 0, 1, 1, 3)
-        open_banks(0, 2, (3,))
-        close_banks(0, 2, (1,))
-        store_result(0, 1, 2, 1, 3)
+        deal_w4(2)
+        multiply(0, 1, (0, 1))
+        open_banks(0, 2, range(PACK))
+        end_sums(0, 2, (0, 1))
+        drain(0, 2, (0, 1))
+        store_result(0, 1, 0, 2)
         close_banks(0, 2, (2, 3))
-        store_result(0, 2, 4, 2, 3)
-
-        multiply_and_store_slot(1, 0)
-        multiply_and_store_slot(1, 1)
-        group_out(0, 0, on_vector, False)
-        deal_scales(0, 2)
+        multiply(0, 1, (2, 3))
+        store_result(0, 1, 2, 4)
+        group_out(0, 0, on_vector, True)
+        group_out(1, 0, on_vector, True)
         quant_out(0, 0)
+        quant_out(1, 0)
         group_out(0, 1, on_vector, True)
         group_out(0, 2, on_vector, True)
         quant_out(0, 1)
         quant_out(0, 2)
-        deal_w8(2)
-        deal_w4(2)
-        store_codes(0)
-        multiply(1, 0, (2, 3))
-        group_out(1, 0, on_vector, False)
-        multiply(1, 1, (2, 3))
-        multiply(1, 2, (2, 3))
-        store_result(1, 2, 4)
-
         group_out(1, 1, on_vector, True)
-        quant_out(1, 0)
+        multiply(1, 2, range(PACK))
+        store_result(1, 1, 0, 4)
+        store_codes(0, 1)
         group_out(1, 2, on_vector, True)
         quant_out(1, 1)
         quant_out(1, 2)
-        multiply_and_store_slot(2, 0)
-        store_codes(1)
-        multiply(2, 0, (1, 2, 3))
+        for r in (0, 1):
+            for c in range(N_CHUNKS):
+                multiply(2, c, (r,))
+        store_result(2, 0, 0, 2)
+        multiply(2, 0, (2, 3))
         group_out(2, 0, on_vector, False)
-        multiply(2, 1, (1, 2, 3))
+        multiply(2, 1, (2, 3))
         group_out(2, 1, on_vector, False)
         quant_out(2, 0)
         quant_out(2, 1)
-        multiply(2, 2, (1, 2, 3))
-        store_result(2, 1, 4)
+        multiply(2, 2, (2, 3))
+        store_result(2, 0, 2, 4)
         group_out(2, 2, on_vector, True, 0, SHARE_LAST)
         group_out(2, 2, on_scalar, True, SHARE_LAST, N)
         quant_out(2, 2)
-        store_codes(2)
+        store_codes(1, 3)
         store_scales()

@@ -30,7 +30,7 @@ DY_CUTS = ((0, 2 * N, T), (0, N, 2 * N, T))
 OUT_CUTS = ((0, 1, 3), (0, 2, 3), (0, 3))
 W_LOADS = ((0, 3),)
 SHARE_HALF_1 = 344
-SHARE_LAST = 192
+SHARE_LAST = 128
 
 
 def tile_mix_dyq_fm_pl_none_kernel(tc, dy, w8_words, w8_scales, w4_words, w4_scales, out_0, out_1, out_2):
@@ -270,20 +270,22 @@ def tile_mix_dyq_fm_pl_none_kernel(tc, dy, w8_words, w8_scales, w4_words, w4_sca
         multiply(0, 1, (0, 1))
         open_banks(0, 2, range(PACK))
         end_sums(0, 2, (0, 1))
-        drain(0, 2, (0, 1))
+        drain(0, 2, (0,))
+        group_out(0, 0, on_vector, True, 0, HALF)
+        drain(0, 2, (1,), on_vector)
         store_result(0, 1, 0, 2)
         close_banks(0, 2, (2, 3))
         multiply(0, 1, (2, 3))
         store_result(0, 1, 2, 4)
-        group_out(0, 0, on_vector, True)
+        group_out(0, 0, on_vector, True, HALF, N)
         group_out(1, 0, on_vector, True)
         quant_out(0, 0)
-        quant_out(1, 0)
         group_out(0, 1, on_vector, True)
         group_out(0, 2, on_vector, True)
         quant_out(0, 1)
         quant_out(0, 2)
         group_out(1, 1, on_vector, True)
+        quant_out(1, 0)
         multiply(1, 2, range(PACK))
         store_result(1, 1, 0, 4)
         store_codes(0, 1)
@@ -294,6 +296,7 @@ def tile_mix_dyq_fm_pl_none_kernel(tc, dy, w8_words, w8_scales, w4_words, w4_sca
             for c in range(N_CHUNKS):
                 multiply(2, c, (r,))
         store_result(2, 0, 0, 2)
+        store_codes(1, 2)
         multiply(2, 0, (2, 3))
         group_out(2, 0, on_vector, False)
         multiply(2, 1, (2, 3))
@@ -305,5 +308,5 @@ def tile_mix_dyq_fm_pl_none_kernel(tc, dy, w8_words, w8_scales, w4_words, w4_sca
         group_out(2, 2, on_vector, True, 0, SHARE_LAST)
         group_out(2, 2, on_scalar, True, SHARE_LAST, N)
         quant_out(2, 2)
-        store_codes(1, 3)
+        store_codes(2, 3)
         store_scales()

@@ -8,6 +8,7 @@ FLOPS = 2 * K * D * T
 F32 = mybir.dt.float32
 BF16 = mybir.dt.bfloat16
 I32 = mybir.dt.int32
+U32 = mybir.dt.uint32
 U16 = mybir.dt.uint16
 U8 = mybir.dt.uint8
 E4M3 = mybir.dt.float8_e4m3fn_x4
@@ -17,20 +18,15 @@ E2M1 = mybir.dt.float4_e2m1fn_x4
 P = 128
 PACK = 4
 SPAN = P * PACK
-N = 512
 N_SPANS = D // SPAN
-N_CHUNKS = T // N
+BANK = 512
 ALIGN = 256
 QUADRANT = 32
 LINE = 16
 RUN = 4
 STAGED = 6
-HALF = N // 2
-DY_CUTS = ((0, 2 * N, T), (0, N, 2 * N, T))
-OUT_CUTS = ((0, 1, 3), (0, 2, 3), (0, 3))
-W_LOADS = ((0, 3),)
-SHARE_HALF_1 = 344
-SHARE_LAST = 128
+DY_CUTS = ((0, 640, T), (0, 640, T))
+OUT_CUTS = ((0, 640, T),) * 3
 
 
 def tile_mix_dyq_fm_pl_none_kernel(tc, dy, w8_words, w8_scales, w4_words, w4_scales, out_0, out_1, out_2):
@@ -40,154 +36,153 @@ def tile_mix_dyq_fm_pl_none_kernel(tc, dy, w8_words, w8_scales, w4_words, w4_sca
         stage = ctx.enter_context(tc.tile_pool(name="stage", bufs=STAGED))
         psum = ctx.enter_context(tc.psum_pool(name="psum", bufs=8))
         ctx.enter_context(tc.manual_schedule())
+        on_vector, on_scalar = nc.vector.tensor_copy, nc.scalar.copy
 
-        ws_raw = [keep.tile([P, D], U8, name="ws_raw_%d" % g, align_bytes=ALIGN) for g in range(2)]
-        w8_raw, w4_raw, w8, w4, ws = {}, {}, {}, {}, {}
-        for a0, a1 in W_LOADS:
-            w8_raw[a0] = keep.tile([P, (a1 - a0) * SPAN], I32, name="w8_raw_%d" % a0, align_bytes=ALIGN)
-            w4_raw[a0] = keep.tile([P, 2 * (a1 - a0) * SPAN], U8, name="w4_raw_%d" % a0, align_bytes=ALIGN)
+        def kept(name, shape, dtype):
+            return keep.tile(shape, dtype, name=name, align_bytes=ALIGN)
+
+        w8_raw = kept("w8_raw", [P, D], U32)
+        w4_raw = kept("w4_raw", [P, D], U16)
+        ws_raw = [kept("ws_raw_%d" % g, [P, D], U8) for g in range(2)]
+        w8 = [kept("w8_%d" % a, [P, SPAN], U32) for a in range(N_SPANS)]
+        w4 = [kept("w4_%d" % a, [P, 2 * SPAN], U8) for a in range(N_SPANS)]
+        ws = [[kept("ws_%d_%d" % (g, a), [P, SPAN], U8) for a in range(N_SPANS)] for g in range(2)]
         dy_raw, dy_codes, dy_scales, result = {}, {}, {}, {}
         for g in range(2):
             for t0, t1 in zip(DY_CUTS[g], DY_CUTS[g][1:]):
-                dy_raw[g, t0] = keep.tile([P, PACK, t1 - t0], F32, name="dy_raw_%d_%d" % (g, t0), align_bytes=ALIGN)
-            for c in range(N_CHUNKS):
-                dy_codes[c, g] = keep.tile([P, N], I32, name="dy_codes_%d_%d" % (c, g), align_bytes=ALIGN)
-                dy_scales[c, g] = keep.tile([P, N], U8, name="dy_scales_%d_%d" % (c, g), align_bytes=ALIGN)
+                dy_raw[g, t0] = kept("dy_raw_%d_%d" % (g, t0), [P, PACK, t1 - t0], F32)
+            for c in range(T // BANK):
+                dy_codes[g, c] = kept("dy_codes_%d_%d" % (g, c), [P, BANK], I32)
+                dy_scales[g, c] = kept("dy_scales_%d_%d" % (g, c), [P, BANK], U8)
         for a in range(N_SPANS):
-            w8[a] = keep.tile([P, SPAN], I32, name="w8_%d" % a, align_bytes=ALIGN)
-            w4[a] = keep.tile([P, 2 * SPAN], U8, name="w4_%d" % a, align_bytes=ALIGN)
-            for g in range(2):
-                ws[g, a] = keep.tile([P, SPAN], U8, name="ws_%d_%d" % (g, a), align_bytes=ALIGN)
-            for c0, c1 in zip(OUT_CUTS[a], OUT_CUTS[a][1:]):
-                result[a, c0] = keep.tile([P, PACK, (c1 - c0) * N], F32, name="result_%d_%d" % (a, c0), align_bytes=ALIGN)
-        out_codes = keep.tile([P, N_SPANS, T], I32, name="out_codes", align_bytes=ALIGN)
-        out_scales = keep.tile([P, T], U8, name="out_scales", align_bytes=ALIGN)
+            for t0, t1 in zip(OUT_CUTS[a], OUT_CUTS[a][1:]):
+                result[a, t0] = kept("result_%d_%d" % (a, t0), [P, PACK, t1 - t0], F32)
+        out_codes = kept("out_codes", [P, N_SPANS, T], I32)
+        out_scales = kept("out_scales", [P, T], U8)
 
-        def chunk_of_result(a, c):
-            c0 = max(cut for cut in OUT_CUTS[a] if cut <= c)
-            return result[a, c0][:, :, (c - c0) * N : (c - c0 + 1) * N]
-
-        def first_of(ranges, index):
-            return max(lo for lo, hi in ranges if lo <= index)
+        def columns(tiles, index, cuts, t0, t1):
+            first = max(cut for cut in cuts[index] if cut <= t0)
+            return tiles[index, first][:, :, t0 - first : t1 - first]
 
         def load_dy(g, part):
             t0, t1 = DY_CUTS[g][part : part + 2]
             rows = dy[g * SPAN : (g + 1) * SPAN, t0:t1]
             nc.sync.dma_start(out=dy_raw[g, t0][:], in_=rows.rearrange("(p j) t -> p j t", j=PACK))
 
-        def load_scales(g, a0=0, a1=N_SPANS):
+        def load_scales(g):
             scales = (w8_scales, w4_scales)[g]
             for r in range(4):
-                cols = slice(a0 * SPAN, a1 * SPAN)
-                nc.sync.dma_start(out=ws_raw[g][r:P:QUADRANT, cols].bitcast(I32), in_=scales[0, r:16:4, cols].bitcast(I32))
+                nc.sync.dma_start(out=ws_raw[g][r:P:QUADRANT, :].bitcast(I32), in_=scales[0, r:16:4, :].bitcast(I32))
 
-        def load_w8(part):
-            a0, a1 = W_LOADS[part]
-            words = w8_words[0].rearrange("p d i -> p (d i)").bitcast(I32)
-            nc.sync.dma_start(out=w8_raw[a0][:], in_=words[:, a0 * SPAN : a1 * SPAN])
+        def load_w8():
+            nc.sync.dma_start(out=w8_raw[:].bitcast(I32), in_=w8_words[0].rearrange("p d i -> p (d i)").bitcast(I32))
 
-        def load_w4(part):
-            a0, a1 = W_LOADS[part]
-            nc.sync.dma_start(out=w4_raw[a0][:].bitcast(I32), in_=w4_words[0][:, 2 * a0 * SPAN : 2 * a1 * SPAN].bitcast(I32))
+        def load_w4():
+            nc.sync.dma_start(out=w4_raw[:].bitcast(I32), in_=w4_words[0].bitcast(I32))
 
-        def deal(out, in_, per_line):
-            nc.vector.tensor_copy(
-                out=out.rearrange("p (r c i) -> p c r i", r=PACK, i=per_line),
-                in_=in_.rearrange("p (c i r) -> p c r i", r=PACK, i=per_line),
+        def deal(copy, out, raw, a, per_line, r0=0, r1=PACK):
+            copy(
+                out=out.rearrange("p (r c i) -> p c r i", r=PACK, i=per_line)[:, :, r0:r1, :],
+                in_=raw[:, a * SPAN : (a + 1) * SPAN].rearrange("p (c i r) -> p c r i", r=PACK, i=per_line)[:, :, r0:r1, :],
             )
 
-        def deal_w8(a):
-            a0 = first_of(W_LOADS, a)
-            deal(w8[a][:], w8_raw[a0][:, (a - a0) * SPAN : (a - a0 + 1) * SPAN], LINE // 4)
+        def deal_w8(a, copy):
+            deal(copy, w8[a][:], w8_raw, a, LINE // 4)
 
-        def deal_w4(a):
-            a0 = first_of(W_LOADS, a)
-            deal(w4[a][:].bitcast(U16), w4_raw[a0][:, 2 * (a - a0) * SPAN : 2 * (a - a0 + 1) * SPAN].bitcast(U16), LINE // 2)
+        def deal_w4(a, copy, r0=0, r1=PACK):
+            deal(copy, w4[a][:].bitcast(U16), w4_raw, a, LINE // 2, r0, r1)
 
         def deal_scales(g, a):
-            deal(ws[g, a][:], ws_raw[g][:, a * SPAN : (a + 1) * SPAN], LINE)
+            deal(on_vector, ws[g][a][:], ws_raw[g], a, LINE)
 
-        grouped = {}
-        on_vector, on_scalar = nc.vector.tensor_copy, nc.scalar.copy
+        staged = {}
 
-        def interleave(key, src, copy, lo, hi, in_runs):
-            if key not in grouped:
-                grouped[key] = stage.tile([P, N, PACK], BF16, name="grouped", align_bytes=ALIGN)
-            out = grouped[key][:, lo:hi, :]
-            if in_runs:
-                copy(
-                    out=out.rearrange("p (c i) j -> p c j i", i=RUN),
-                    in_=src.rearrange("p j (c i) -> p c j i", i=RUN),
-                )
-            else:
-                copy(out=out, in_=src.rearrange("p j t -> p t j"))
-
-        def group_dy(g, c, copy, lo=0, hi=N):
-            t0 = max(t for t in DY_CUTS[g] if t <= c * N + lo)
-            interleave(("dy", g, c), dy_raw[g, t0][:, :, c * N + lo - t0 : c * N + hi - t0], copy, lo, hi, True)
-
-        def quant_dy(g, c, lo=0, hi=N):
-            nc.vector.quantize_mx(
-                out=dy_codes[c, g][:, lo:hi].bitcast(E5M2),
-                scales=dy_scales[c, g][:, lo:hi],
-                in_=grouped["dy", g, c][:, lo:hi, :].rearrange("p t j -> p (t j)"),
+        def interleave(key, src, copy, t0, t1):
+            c = t0 // BANK
+            if (key, c) not in staged:
+                staged[key, c] = stage.tile([P, BANK, PACK], BF16, name="staged", align_bytes=ALIGN)
+            copy(
+                out=staged[key, c][:, t0 - c * BANK : t1 - c * BANK, :].rearrange("p (c i) j -> p c j i", i=RUN),
+                in_=src.rearrange("p j (c i) -> p c j i", i=RUN),
             )
+
+        def staged_columns(key, t0, t1):
+            c = t0 // BANK
+            return staged[key, c][:, t0 - c * BANK : t1 - c * BANK, :].rearrange("p t j -> p (t j)")
+
+        def group_dy(g, t0, t1, copy=on_vector):
+            interleave(("dy", g), columns(dy_raw, g, DY_CUTS, t0, t1), copy, t0, t1)
+
+        def codes_of(g, t0, t1):
+            c = t0 // BANK
+            cols = slice(t0 - c * BANK, t1 - c * BANK)
+            return dy_codes[g, c][:, cols].bitcast(E5M2), dy_scales[g, c][:, cols]
+
+        def quant_dy(g, t0, t1):
+            codes, scales = codes_of(g, t0, t1)
+            nc.vector.quantize_mx(out=codes, scales=scales, in_=staged_columns(("dy", g), t0, t1))
 
         banks = {}
 
-        def open_banks(a, c, slots):
-            for r in slots:
-                banks[a, c, r] = psum.tile([P, N], F32, name="acc")
+        def slots_of(r0, t0, t1):
+            return range(r0, r0 + BANK // (t1 - t0))
+
+        def open_bank(a, t0, t1, r0):
+            bank = psum.tile([P, BANK // (t1 - t0), t1 - t0], F32, name="acc")
+            banks[a, t0, r0] = bank
+            codes, scales = codes_of(0, t0, t1)
+            for r in slots_of(r0, t0, t1):
                 nc.tensor.matmul_mx(
-                    out=banks[a, c, r][:],
+                    out=bank[:, r - r0, :],
                     lhsT=w8[a][:, r * P : (r + 1) * P].bitcast(E4M3),
-                    lhsT_scale=ws[0, a][:, r * P : (r + 1) * P],
-                    rhs=dy_codes[c, 0][:].bitcast(E5M2),
-                    rhs_scale=dy_scales[c, 0][:],
-                    start=True,
+                    lhsT_scale=ws[0][a][:, r * P : (r + 1) * P],
+                    rhs=codes,
+                    rhs_scale=scales,
+                    start=r == r0,
                     stop=False,
                 )
 
-        def end_sums(a, c, slots):
+        def close_bank(a, t0, t1, r0):
+            codes, scales = codes_of(1, t0, t1)
+            slots = slots_of(r0, t0, t1)
             for r in slots:
                 nc.tensor.matmul_mx(
-                    out=banks[a, c, r][:],
+                    out=banks[a, t0, r0][:, r - r0, :],
                     lhsT=w4[a][:, 2 * r * P : 2 * (r + 1) * P].bitcast(E2M1),
-                    lhsT_scale=ws[1, a][:, r * P : (r + 1) * P],
-                    rhs=dy_codes[c, 1][:].bitcast(E5M2),
-                    rhs_scale=dy_scales[c, 1][:],
+                    lhsT_scale=ws[1][a][:, r * P : (r + 1) * P],
+                    rhs=codes,
+                    rhs_scale=scales,
                     start=False,
-                    stop=True,
+                    stop=r == slots[-1],
                 )
 
-        def drain(a, c, slots, copy=on_scalar):
-            for r in slots:
-                copy(out=chunk_of_result(a, c)[:, r, :], in_=banks[a, c, r][:])
+        def drain(a, t0, t1, r0, copy=on_scalar):
+            slots = slots_of(r0, t0, t1)
+            copy(out=columns(result, a, OUT_CUTS, t0, t1)[:, slots[0] : slots[-1] + 1, :], in_=banks[a, t0, r0][:])
 
-        def close_banks(a, c, slots):
-            for r in slots:
-                end_sums(a, c, (r,))
-                drain(a, c, (r,))
+        def firsts(t0, t1):
+            return range(0, PACK, BANK // (t1 - t0))
 
-        def multiply(a, c, slots):
-            for r in slots:
-                open_banks(a, c, (r,))
-                close_banks(a, c, (r,))
+        def multiply(a, t0, t1):
+            for r0 in firsts(t0, t1):
+                open_bank(a, t0, t1, r0)
+                close_bank(a, t0, t1, r0)
+                drain(a, t0, t1, r0)
 
-        def group_out(a, c, copy, in_runs, lo=0, hi=N):
-            interleave(("out", a, c), chunk_of_result(a, c)[:, :, lo:hi], copy, lo, hi, in_runs)
+        def group_out(a, t0, t1, copy=on_vector):
+            interleave(("out", a), columns(result, a, OUT_CUTS, t0, t1), copy, t0, t1)
 
-        def quant_out(a, c):
+        def quant_out(a, t0, t1):
             nc.vector.quantize_mx(
-                out=out_codes[:, a, c * N : (c + 1) * N].bitcast(E4M3),
-                scales=out_scales[4 * (a + 1) : P, c * N : (c + 1) * N],
-                in_=grouped["out", a, c][:].rearrange("p t j -> p (t j)"),
+                out=out_codes[:, a, t0:t1].bitcast(E4M3),
+                scales=out_scales[4 * (a + 1) : P, t0:t1],
+                in_=staged_columns(("out", a), t0, t1),
             )
 
-        def store_result(a, part, r0, r1):
-            c0, c1 = OUT_CUTS[a][part : part + 2]
+        def store_result(a, part, r0=0, r1=PACK):
+            t0, t1 = OUT_CUTS[a][part : part + 2]
             rows = out_0[a * SPAN : (a + 1) * SPAN, :].rearrange("(p r) t -> p r t", r=PACK)
-            nc.sync.dma_start(out=rows[:, r0:r1, c0 * N : c1 * N], in_=result[a, c0][:, r0:r1, :])
+            nc.sync.dma_start(out=rows[:, r0:r1, t0:t1], in_=result[a, t0][:, r0:r1, :])
 
         def store_codes(a0, a1):
             words = out_1.rearrange("a p t i -> p a (t i)").bitcast(I32)
@@ -202,111 +197,118 @@ def tile_mix_dyq_fm_pl_none_kernel(tc, dy, w8_words, w8_scales, w4_words, w4_sca
 
         nc.vector.memset(ws_raw[0][:].bitcast(I32), 0)
         nc.vector.memset(ws_raw[1][:].bitcast(I32), 0)
-
-        load_w8(0)
+        load_w8()
         load_scales(0)
         load_dy(0, 0)
         load_scales(1)
-        load_w4(0)
         load_dy(1, 0)
-        load_dy(1, 1)
+        load_w4()
         load_dy(0, 1)
-        load_dy(1, 2)
+        load_dy(1, 1)
+
+        def first_bank(g):
+            group_dy(g, 0, 256)
+            group_dy(g, 256, 344)
+            group_dy(g, 344, 512, on_scalar)
+            quant_dy(g, 0, 256)
+            quant_dy(g, 256, 512)
 
         for a in range(N_SPANS):
-            deal_w8(a)
-        for a in range(N_SPANS):
+            deal_w8(a, on_scalar)
             deal_scales(0, a)
-        group_dy(0, 0, on_vector, 0, HALF)
-        group_dy(0, 0, on_vector, HALF, SHARE_HALF_1)
-        group_dy(0, 0, on_scalar, SHARE_HALF_1, N)
-        group_dy(0, 1, on_scalar)
-        quant_dy(0, 0, 0, HALF)
-        quant_dy(0, 0, HALF, N)
+        first_bank(0)
+        group_dy(0, 512, 640, on_scalar)
         deal_scales(1, 0)
-        deal_w4(0)
+        quant_dy(0, 512, 640)
         deal_scales(1, 1)
-        quant_dy(0, 1)
-        open_banks(0, 0, range(PACK))
-        open_banks(1, 0, (0, 1))
-        open_banks(1, 1, (0, 1))
-
-        group_dy(1, 0, on_vector, 0, HALF)
-        group_dy(1, 0, on_vector, HALF, SHARE_HALF_1)
-        group_dy(1, 0, on_scalar, SHARE_HALF_1, N)
-        quant_dy(1, 0, 0, HALF)
-        quant_dy(1, 0, HALF, N)
-        deal_w4(1)
-        group_dy(1, 1, on_vector, 0, HALF)
-        group_dy(1, 1, on_vector, HALF, N)
-        quant_dy(1, 1, 0, HALF)
-        quant_dy(1, 1, HALF, N)
-        end_sums(0, 0, range(PACK))
-        end_sums(1, 0, (0, 1))
-        drain(0, 0, (0, 1))
-        store_result(0, 0, 0, 2)
-        drain(0, 0, (2,))
-        drain(0, 0, (3,), on_vector)
-        store_result(0, 0, 2, 4)
-        drain(1, 0, (0, 1))
-        open_banks(1, 0, (2,))
-        end_sums(1, 0, (2,))
-        end_sums(1, 1, (0, 1))
-        drain(1, 1, (0, 1))
-        store_result(1, 0, 0, 2)
-        group_dy(0, 2, on_vector)
         deal_scales(1, 2)
-        quant_dy(0, 2)
-        drain(1, 0, (2,))
-        multiply(1, 0, (3,))
-        multiply(1, 1, (2, 3))
-        store_result(1, 0, 2, 4)
-
-        group_dy(1, 2, on_vector, 0, HALF)
-        group_dy(1, 2, on_vector, HALF, N)
-        quant_dy(1, 2, 0, HALF)
-        quant_dy(1, 2, HALF, N)
-        deal_w4(2)
-        multiply(0, 1, (0, 1))
-        open_banks(0, 2, range(PACK))
-        end_sums(0, 2, (0, 1))
-        drain(0, 2, (0,))
-        group_out(0, 0, on_vector, True, 0, HALF)
-        drain(0, 2, (1,), on_vector)
-        store_result(0, 1, 0, 2)
-        close_banks(0, 2, (2, 3))
-        multiply(0, 1, (2, 3))
-        store_result(0, 1, 2, 4)
-        group_out(0, 0, on_vector, True, HALF, N)
-        group_out(1, 0, on_vector, True)
-        quant_out(0, 0)
-        group_out(0, 1, on_vector, True)
-        group_out(0, 2, on_vector, True)
-        quant_out(0, 1)
-        quant_out(0, 2)
-        group_out(1, 1, on_vector, True)
-        quant_out(1, 0)
-        multiply(1, 2, range(PACK))
-        store_result(1, 1, 0, 4)
-        store_codes(0, 1)
-        group_out(1, 2, on_vector, True)
-        quant_out(1, 1)
-        quant_out(1, 2)
-        for r in (0, 1):
-            for c in range(N_CHUNKS):
-                multiply(2, c, (r,))
-        store_result(2, 0, 0, 2)
-        store_codes(1, 2)
-        multiply(2, 0, (2, 3))
-        group_out(2, 0, on_vector, False)
-        multiply(2, 1, (2, 3))
-        group_out(2, 1, on_vector, False)
-        quant_out(2, 0)
-        quant_out(2, 1)
-        multiply(2, 2, (2, 3))
-        store_result(2, 0, 2, 4)
-        group_out(2, 2, on_vector, True, 0, SHARE_LAST)
-        group_out(2, 2, on_scalar, True, SHARE_LAST, N)
-        quant_out(2, 2)
+        for r in range(PACK):
+            open_bank(0, 0, 512, r)
+        open_bank(0, 512, 640, 0)
+        for r in (0, 1, 2):
+            open_bank(1, 0, 512, r)
+        first_bank(1)
+        deal_w4(0, on_scalar, 0, 2)
+        deal_w4(0, on_scalar, 2, 4)
+        group_dy(1, 512, 640)
+        deal_w4(1, on_vector)
+        quant_dy(1, 512, 640)
+        deal_w4(2, on_vector)
+        for r in range(PACK):
+            close_bank(0, 0, 512, r)
+            drain(0, 0, 512, r)
+        close_bank(0, 512, 640, 0)
+        drain(0, 512, 640, 0, on_vector)
+        store_result(0, 0)
+        for r in range(PACK):
+            if r > 2:
+                open_bank(1, 0, 512, r)
+            close_bank(1, 0, 512, r)
+            drain(1, 0, 512, r, on_vector if r == 0 else on_scalar)
+        group_dy(0, 640, 768)
+        group_dy(0, 768, 1024)
+        quant_dy(0, 640, 768)
+        group_dy(0, 1024, 1536)
+        quant_dy(0, 768, 1024)
+        quant_dy(0, 1024, 1536)
+        multiply(1, 512, 640)
+        store_result(1, 0)
+        multiply(2, 0, 512)
+        multiply(2, 512, 640)
+        store_result(2, 0)
+        group_out(0, 0, 256)
+        right = ((640, 768), (768, 1024), (1024, 1536))
+        for t0, t1 in right:
+            for r in firsts(t0, t1):
+                open_bank(0, t0, t1, r)
+        group_dy(1, 640, 768)
+        group_dy(1, 768, 1024)
+        quant_dy(1, 640, 768)
+        quant_dy(1, 768, 1024)
+        group_dy(1, 1024, 1304)
+        group_dy(1, 1304, 1536, on_scalar)
+        quant_dy(1, 1024, 1280)
+        quant_dy(1, 1280, 1536)
+        group_out(0, 256, 512)
+        group_out(1, 0, 256)
+        for t0, t1 in right[:2]:
+            for r in firsts(t0, t1):
+                close_bank(0, t0, t1, r)
+                drain(0, t0, t1, r)
+        open_bank(1, 640, 768, 0)
+        close_bank(1, 640, 768, 0)
+        for r in range(PACK):
+            close_bank(0, 1024, 1536, r)
+            drain(0, 1024, 1536, r, on_vector if r % 2 else on_scalar)
+        store_result(0, 1)
+        drain(1, 640, 768, 0)
+        for a in (1, 2):
+            for t0, t1 in right:
+                if (a, t0) != (1, 640):
+                    multiply(a, t0, t1)
+            store_result(a, 1)
+        quant_out(0, 0, 512)
+        group_out(1, 256, 512)
+        for a in range(N_SPANS):
+            last = a == N_SPANS - 1
+            group_out(a, 512, 640)
+            if a == 0:
+                quant_out(1, 0, 512)
+            if last:
+                quant_out(a, 0, 512)
+            if last:
+                group_out(a, 640, 768)
+                group_out(a, 768, 1024, on_scalar)
+                group_out(a, 1024, 1536, on_scalar)
+            else:
+                group_out(a, 640, 1024)
+                group_out(a, 1024, 1536)
+            quant_out(a, 512, 1024)
+            if a == 1:
+                group_out(2, 0, 256)
+            quant_out(a, 1024, 1536)
+            if a == 1:
+                store_codes(0, 2)
+                group_out(2, 256, 512)
         store_codes(2, 3)
         store_scales()

@@ -25,8 +25,8 @@ QUADRANT = 32
 LINE = 16
 RUN = 4
 STAGED = 6
-DY_CUTS = ((0, 640, T), (0, 640, T))
-OUT_CUTS = ((0, 640, T),) * 3
+DY_CUTS = ((0, 768, T),) * 2
+OUT_CUTS = ((0, 768, T), (0, 768, T), (0, 512, T))
 
 
 def tile_mix_dyq_fm_pl_none_kernel(tc, dy, w8_words, w8_scales, w4_words, w4_scales, out_0, out_1, out_2):
@@ -86,8 +86,8 @@ def tile_mix_dyq_fm_pl_none_kernel(tc, dy, w8_words, w8_scales, w4_words, w4_sca
                 in_=raw[:, a * SPAN : (a + 1) * SPAN].rearrange("p (c i r) -> p c r i", r=PACK, i=per_line)[:, :, r0:r1, :],
             )
 
-        def deal_w8(a, copy):
-            deal(copy, w8[a][:], w8_raw, a, LINE // 4)
+        def deal_w8(a, copy, r0=0, r1=PACK):
+            deal(copy, w8[a][:], w8_raw, a, LINE // 4, r0, r1)
 
         def deal_w4(a, copy, r0=0, r1=PACK):
             deal(copy, w4[a][:].bitcast(U16), w4_raw, a, LINE // 2, r0, r1)
@@ -213,102 +213,80 @@ def tile_mix_dyq_fm_pl_none_kernel(tc, dy, w8_words, w8_scales, w4_words, w4_sca
             quant_dy(g, 0, 256)
             quant_dy(g, 256, 512)
 
-        for a in range(N_SPANS):
-            deal_w8(a, on_scalar)
+        deal_w8(2, on_scalar)
+        deal_w8(0, on_scalar)
+        for a in (2, 0, 1):
             deal_scales(0, a)
+        deal_w8(1, on_vector)
         first_bank(0)
-        group_dy(0, 512, 640, on_scalar)
-        deal_scales(1, 0)
-        quant_dy(0, 512, 640)
-        deal_scales(1, 1)
+        group_dy(0, 512, 768, on_scalar)
         deal_scales(1, 2)
-        for r in range(PACK):
-            open_bank(0, 0, 512, r)
-        open_bank(0, 512, 640, 0)
-        for r in (0, 1, 2):
-            open_bank(1, 0, 512, r)
+        deal_scales(1, 0)
+        quant_dy(0, 512, 768)
+        deal_scales(1, 1)
+        for a in (2, 0):
+            for r in range(PACK):
+                open_bank(a, 0, 512, r)
         first_bank(1)
-        deal_w4(0, on_scalar, 0, 2)
-        deal_w4(0, on_scalar, 2, 4)
-        group_dy(1, 512, 640)
+        deal_w4(2, on_scalar, 0, 1)
+        group_dy(1, 512, 768, on_scalar)
+        deal_w4(2, on_vector, 1, 4)
+        deal_w4(0, on_vector)
         deal_w4(1, on_vector)
-        quant_dy(1, 512, 640)
-        deal_w4(2, on_vector)
+        quant_dy(1, 512, 768)
+        for r in range(PACK):
+            close_bank(2, 0, 512, r)
+            drain(2, 0, 512, r, on_vector if r > 1 else on_scalar)
+        store_result(2, 0)
         for r in range(PACK):
             close_bank(0, 0, 512, r)
             drain(0, 0, 512, r)
-        close_bank(0, 512, 640, 0)
-        drain(0, 512, 640, 0, on_vector)
-        store_result(0, 0)
-        for r in range(PACK):
-            if r > 2:
-                open_bank(1, 0, 512, r)
-            close_bank(1, 0, 512, r)
-            drain(1, 0, 512, r, on_vector if r == 0 else on_scalar)
-        group_dy(0, 640, 768)
         group_dy(0, 768, 1024)
-        quant_dy(0, 640, 768)
         group_dy(0, 1024, 1536)
         quant_dy(0, 768, 1024)
         quant_dy(0, 1024, 1536)
-        multiply(1, 512, 640)
+        multiply(0, 512, 768)
+        store_result(0, 0)
+        for r in range(PACK):
+            open_bank(1, 0, 512, r)
+            close_bank(1, 0, 512, r)
+            drain(1, 0, 512, r, on_scalar if r else on_vector)
+        multiply(1, 512, 768)
         store_result(1, 0)
-        multiply(2, 0, 512)
-        multiply(2, 512, 640)
-        store_result(2, 0)
-        group_out(0, 0, 256)
-        right = ((640, 768), (768, 1024), (1024, 1536))
-        for t0, t1 in right:
-            for r in firsts(t0, t1):
-                open_bank(0, t0, t1, r)
-        group_dy(1, 640, 768)
         group_dy(1, 768, 1024)
-        quant_dy(1, 640, 768)
+        group_dy(1, 1024, 1280)
         quant_dy(1, 768, 1024)
-        group_dy(1, 1024, 1304)
-        group_dy(1, 1304, 1536, on_scalar)
+        group_dy(1, 1280, 1536)
         quant_dy(1, 1024, 1280)
         quant_dy(1, 1280, 1536)
-        group_out(0, 256, 512)
-        group_out(1, 0, 256)
-        for t0, t1 in right[:2]:
-            for r in firsts(t0, t1):
-                close_bank(0, t0, t1, r)
-                drain(0, t0, t1, r)
-        open_bank(1, 640, 768, 0)
-        close_bank(1, 640, 768, 0)
-        for r in range(PACK):
-            close_bank(0, 1024, 1536, r)
-            drain(0, 1024, 1536, r, on_vector if r % 2 else on_scalar)
-        store_result(0, 1)
-        drain(1, 640, 768, 0)
-        for a in (1, 2):
-            for t0, t1 in right:
-                if (a, t0) != (1, 640):
-                    multiply(a, t0, t1)
+        for a in (0, 1):
+            multiply(a, 768, 1024)
+            multiply(a, 1024, 1536)
             store_result(a, 1)
+        multiply(2, 512, 1024)
+        multiply(2, 1024, 1536)
+        group_out(0, 0, 512)
+        group_out(0, 512, 768)
         quant_out(0, 0, 512)
-        group_out(1, 256, 512)
-        for a in range(N_SPANS):
-            last = a == N_SPANS - 1
-            group_out(a, 512, 640)
-            if a == 0:
-                quant_out(1, 0, 512)
-            if last:
-                quant_out(a, 0, 512)
-            if last:
-                group_out(a, 640, 768)
-                group_out(a, 768, 1024, on_scalar)
-                group_out(a, 1024, 1536, on_scalar)
-            else:
-                group_out(a, 640, 1024)
-                group_out(a, 1024, 1536)
-            quant_out(a, 512, 1024)
-            if a == 1:
-                group_out(2, 0, 256)
-            quant_out(a, 1024, 1536)
-            if a == 1:
-                store_codes(0, 2)
-                group_out(2, 256, 512)
-        store_codes(2, 3)
+        group_out(2, 0, 512)
+        group_out(0, 768, 1024)
+        quant_out(2, 0, 512)
+        group_out(0, 1024, 1536)
+        quant_out(0, 512, 1024)
+        group_out(1, 0, 512)
+        quant_out(0, 1024, 1536)
+        store_codes(0, 1)
+        store_result(2, 1)
+        group_out(1, 512, 768)
+        quant_out(1, 0, 512)
+        group_out(1, 768, 1024)
+        group_out(1, 1024, 1536)
+        quant_out(1, 512, 1024)
+        group_out(2, 512, 1024)
+        quant_out(1, 1024, 1536)
+        group_out(2, 1024, 1152)
+        group_out(2, 1152, 1536, on_scalar)
+        quant_out(2, 512, 1024)
+        quant_out(2, 1024, 1536)
+        store_codes(1, 3)
         store_scales()

@@ -26,7 +26,9 @@ LINE = 16
 RUN = 4
 STAGED = 6
 DY_CUTS = ((0, 768, T),) * 2
-OUT_CUTS = ((0, 768, T), (0, 768, T), (0, 512, T))
+W8_CUTS = (0, 3)
+W4_CUTS = (0, 3)
+OUT_CUTS = ((0, 768, T), (0, 768, T), (0, T))
 
 
 def tile_mix_dyq_fm_pl_none_kernel(tc, dy, w8_words, w8_scales, w4_words, w4_scales, out_0, out_1, out_2):
@@ -41,8 +43,8 @@ def tile_mix_dyq_fm_pl_none_kernel(tc, dy, w8_words, w8_scales, w4_words, w4_sca
         def kept(name, shape, dtype):
             return keep.tile(shape, dtype, name=name, align_bytes=ALIGN)
 
-        w8_raw = kept("w8_raw", [P, D], U32)
-        w4_raw = kept("w4_raw", [P, D], U16)
+        w8_raw = {a0: kept("w8_raw_%d" % a0, [P, (a1 - a0) * SPAN], U32) for a0, a1 in zip(W8_CUTS, W8_CUTS[1:])}
+        w4_raw = {a0: kept("w4_raw_%d" % a0, [P, (a1 - a0) * SPAN], U16) for a0, a1 in zip(W4_CUTS, W4_CUTS[1:])}
         ws_raw = [kept("ws_raw_%d" % g, [P, D], U8) for g in range(2)]
         w8 = [kept("w8_%d" % a, [P, SPAN], U32) for a in range(N_SPANS)]
         w4 = [kept("w4_%d" % a, [P, 2 * SPAN], U8) for a in range(N_SPANS)]
@@ -69,16 +71,20 @@ def tile_mix_dyq_fm_pl_none_kernel(tc, dy, w8_words, w8_scales, w4_words, w4_sca
             rows = dy[g * SPAN : (g + 1) * SPAN, t0:t1]
             nc.sync.dma_start(out=dy_raw[g, t0][:], in_=rows.rearrange("(p j) t -> p j t", j=PACK))
 
-        def load_scales(g):
+        def load_scales(g, into, r0=0, r1=4):
             scales = (w8_scales, w4_scales)[g]
-            for r in range(4):
-                nc.sync.dma_start(out=ws_raw[g][r:P:QUADRANT, :].bitcast(I32), in_=scales[0, r:16:4, :].bitcast(I32))
+            for r in range(r0, r1):
+                nc.sync.dma_start(out=into[r:P:QUADRANT, :].bitcast(I32), in_=scales[0, r:16:4, :].bitcast(I32))
 
-        def load_w8():
-            nc.sync.dma_start(out=w8_raw[:].bitcast(I32), in_=w8_words[0].rearrange("p d i -> p (d i)").bitcast(I32))
+        def load_w8(part):
+            a0, a1 = W8_CUTS[part : part + 2]
+            words = w8_words[0].rearrange("p d i -> p (d i)").bitcast(I32)
+            nc.sync.dma_start(out=w8_raw[a0][:].bitcast(I32), in_=words[:, a0 * SPAN : a1 * SPAN])
 
-        def load_w4():
-            nc.sync.dma_start(out=w4_raw[:].bitcast(I32), in_=w4_words[0].bitcast(I32))
+        def load_w4(part):
+            a0, a1 = W4_CUTS[part : part + 2]
+            words = w4_words[0].bitcast(I32)
+            nc.sync.dma_start(out=w4_raw[a0][:].bitcast(I32), in_=words[:, a0 * SPAN // 2 : a1 * SPAN // 2])
 
         def deal(copy, out, raw, a, per_line, r0=0, r1=PACK):
             copy(
@@ -86,11 +92,13 @@ def tile_mix_dyq_fm_pl_none_kernel(tc, dy, w8_words, w8_scales, w4_words, w4_sca
                 in_=raw[:, a * SPAN : (a + 1) * SPAN].rearrange("p (c i r) -> p c r i", r=PACK, i=per_line)[:, :, r0:r1, :],
             )
 
-        def deal_w8(a, copy, r0=0, r1=PACK):
-            deal(copy, w8[a][:], w8_raw, a, LINE // 4, r0, r1)
+        def deal_w8(a, copy=on_vector, r0=0, r1=PACK):
+            first = max(cut for cut in W8_CUTS if cut <= a)
+            deal(copy, w8[a][:], w8_raw[first], a - first, LINE // 4, r0, r1)
 
-        def deal_w4(a, copy, r0=0, r1=PACK):
-            deal(copy, w4[a][:].bitcast(U16), w4_raw, a, LINE // 2, r0, r1)
+        def deal_w4(a, copy=on_vector, r0=0, r1=PACK):
+            first = max(cut for cut in W4_CUTS if cut <= a)
+            deal(copy, w4[a][:].bitcast(U16), w4_raw[first], a - first, LINE // 2, r0, r1)
 
         def deal_scales(g, a):
             deal(on_vector, ws[g][a][:], ws_raw[g], a, LINE)
@@ -124,50 +132,39 @@ def tile_mix_dyq_fm_pl_none_kernel(tc, dy, w8_words, w8_scales, w4_words, w4_sca
 
         banks = {}
 
+        def stationary(g, a, r):
+            if g == 0:
+                return w8[a][:, r * P : (r + 1) * P].bitcast(E4M3)
+            return w4[a][:, 2 * r * P : 2 * (r + 1) * P].bitcast(E2M1)
+
         def slots_of(r0, t0, t1):
             return range(r0, r0 + BANK // (t1 - t0))
 
-        def open_bank(a, t0, t1, r0):
-            bank = psum.tile([P, BANK // (t1 - t0), t1 - t0], F32, name="acc")
-            banks[a, t0, r0] = bank
-            codes, scales = codes_of(0, t0, t1)
-            for r in slots_of(r0, t0, t1):
-                nc.tensor.matmul_mx(
-                    out=bank[:, r - r0, :],
-                    lhsT=w8[a][:, r * P : (r + 1) * P].bitcast(E4M3),
-                    lhsT_scale=ws[0][a][:, r * P : (r + 1) * P],
-                    rhs=codes,
-                    rhs_scale=scales,
-                    start=r == r0,
-                    stop=False,
-                )
-
-        def close_bank(a, t0, t1, r0):
-            codes, scales = codes_of(1, t0, t1)
+        def passes(g, a, t0, t1, r0):
+            opens = (a, t0, r0) not in banks
             slots = slots_of(r0, t0, t1)
+            if opens:
+                banks[a, t0, r0] = psum.tile([P, len(slots), t1 - t0], F32, name="acc")
+            codes, scales = codes_of(g, t0, t1)
             for r in slots:
                 nc.tensor.matmul_mx(
                     out=banks[a, t0, r0][:, r - r0, :],
-                    lhsT=w4[a][:, 2 * r * P : 2 * (r + 1) * P].bitcast(E2M1),
-                    lhsT_scale=ws[1][a][:, r * P : (r + 1) * P],
+                    lhsT=stationary(g, a, r),
+                    lhsT_scale=ws[g][a][:, r * P : (r + 1) * P],
                     rhs=codes,
                     rhs_scale=scales,
-                    start=False,
-                    stop=r == slots[-1],
+                    start=opens and r == r0,
+                    stop=not opens and r == slots[-1],
                 )
 
         def drain(a, t0, t1, r0, copy=on_scalar):
             slots = slots_of(r0, t0, t1)
             copy(out=columns(result, a, OUT_CUTS, t0, t1)[:, slots[0] : slots[-1] + 1, :], in_=banks[a, t0, r0][:])
 
-        def firsts(t0, t1):
-            return range(0, PACK, BANK // (t1 - t0))
-
-        def multiply(a, t0, t1):
-            for r0 in firsts(t0, t1):
-                open_bank(a, t0, t1, r0)
-                close_bank(a, t0, t1, r0)
-                drain(a, t0, t1, r0)
+        def multiply(a, t0, t1, r0, copy=on_scalar):
+            passes(1, a, t0, t1, r0)
+            passes(0, a, t0, t1, r0)
+            drain(a, t0, t1, r0, copy)
 
         def group_out(a, t0, t1, copy=on_vector):
             interleave(("out", a), columns(result, a, OUT_CUTS, t0, t1), copy, t0, t1)
@@ -195,97 +192,102 @@ def tile_mix_dyq_fm_pl_none_kernel(tc, dy, w8_words, w8_scales, w4_words, w4_sca
                     in_=out_scales[QUADRANT * q + 4 : QUADRANT * q + 16, :].bitcast(I32),
                 )
 
-        nc.vector.memset(ws_raw[0][:].bitcast(I32), 0)
+
         nc.vector.memset(ws_raw[1][:].bitcast(I32), 0)
-        load_w8()
-        load_scales(0)
-        load_dy(0, 0)
-        load_scales(1)
+        nc.vector.memset(ws_raw[0][:].bitcast(I32), 0)
+        load_w4(0)
         load_dy(1, 0)
-        load_w4()
-        load_dy(0, 1)
+        load_scales(1, ws_raw[1])
+        load_dy(0, 0)
+        load_scales(0, ws_raw[0])
+        load_w8(0)
         load_dy(1, 1)
+        load_dy(0, 1)
 
-        def first_bank(g):
-            group_dy(g, 0, 256)
-            group_dy(g, 256, 344)
-            group_dy(g, 344, 512, on_scalar)
-            quant_dy(g, 0, 256)
-            quant_dy(g, 256, 512)
-
-        deal_w8(2, on_scalar)
-        deal_w8(0, on_scalar)
-        for a in (2, 0, 1):
-            deal_scales(0, a)
-        deal_w8(1, on_vector)
-        first_bank(0)
-        group_dy(0, 512, 768, on_scalar)
-        deal_scales(1, 2)
-        deal_scales(1, 0)
-        quant_dy(0, 512, 768)
-        deal_scales(1, 1)
-        for a in (2, 0):
-            for r in range(PACK):
-                open_bank(a, 0, 512, r)
-        first_bank(1)
-        deal_w4(2, on_scalar, 0, 1)
+        for a in range(N_SPANS):
+            deal_w4(a)
+        group_dy(1, 0, 512)
         group_dy(1, 512, 768, on_scalar)
-        deal_w4(2, on_vector, 1, 4)
-        deal_w4(0, on_vector)
-        deal_w4(1, on_vector)
+        deal_scales(1, 0)
+        quant_dy(1, 0, 512)
+        deal_scales(1, 1)
         quant_dy(1, 512, 768)
-        for r in range(PACK):
-            close_bank(2, 0, 512, r)
-            drain(2, 0, 512, r, on_vector if r > 1 else on_scalar)
-        store_result(2, 0)
-        for r in range(PACK):
-            close_bank(0, 0, 512, r)
-            drain(0, 0, 512, r)
+        deal_scales(1, 2)
+        left = [(0, 512, r) for r in range(4)] + [(512, 768, 0), (512, 768, 2)]
+        right = [(768, 1024, 0), (768, 1024, 2)] + [(1024, 1536, r) for r in range(4)]
+        for piece in left:
+            passes(1, 0, *piece)
+        passes(1, 1, 0, 512, 0)
+        passes(1, 1, 0, 512, 1)
+
+        group_dy(0, 0, 512)
+        group_dy(0, 512, 768, on_scalar)
+        deal_scales(0, 0)
+        quant_dy(0, 0, 512)
+        deal_w8(0)
+        quant_dy(0, 512, 768)
+        deal_scales(0, 1)
+        deal_w8(1)
+        deal_scales(0, 2)
+        deal_w8(2)
+        for n, piece in enumerate(left):
+            passes(0, 0, *piece)
+            drain(0, *piece, on_vector if n in (2, 4) else on_scalar)
+        store_result(0, 0)
+        group_dy(1, 768, 1024)
+        group_dy(1, 1024, 1536)
+        quant_dy(1, 768, 1024)
+        quant_dy(1, 1024, 1536)
+        for n, piece in enumerate(left):
+            if n > 1:
+                passes(1, 1, *piece)
+            passes(0, 1, *piece)
+            drain(1, *piece, on_vector if n in (4,) else on_scalar)
+        store_result(1, 0)
+        multiply(2, 0, 512, 0)
+        passes(1, 2, 0, 512, 1)
+        passes(0, 2, 0, 512, 1)
+        for piece in right:
+            passes(1, 0, *piece)
         group_dy(0, 768, 1024)
-        group_dy(0, 1024, 1536)
+        group_dy(0, 1024, 1280)
+        group_dy(0, 1280, 1536, on_scalar)
         quant_dy(0, 768, 1024)
         quant_dy(0, 1024, 1536)
-        multiply(0, 512, 768)
-        store_result(0, 0)
-        for r in range(PACK):
-            open_bank(1, 0, 512, r)
-            close_bank(1, 0, 512, r)
-            drain(1, 0, 512, r, on_scalar if r else on_vector)
-        multiply(1, 512, 768)
-        store_result(1, 0)
-        group_dy(1, 768, 1024)
-        group_dy(1, 1024, 1280)
-        quant_dy(1, 768, 1024)
-        group_dy(1, 1280, 1536)
-        quant_dy(1, 1024, 1280)
-        quant_dy(1, 1280, 1536)
-        for a in (0, 1):
-            multiply(a, 768, 1024)
-            multiply(a, 1024, 1536)
-            store_result(a, 1)
-        multiply(2, 512, 1024)
-        multiply(2, 1024, 1536)
+        drain(2, 0, 512, 1)
+        multiply(2, 0, 512, 2)
+        for n, piece in enumerate(right):
+            passes(0, 0, *piece)
+            drain(0, *piece, on_vector if n in (0, 2, 4) else on_scalar)
+        store_result(0, 1)
+        for piece in right:
+            multiply(1, *piece)
+        store_result(1, 1)
+        multiply(2, 0, 512, 3)
+        for t0 in (512, 1024):
+            for r in range(4):
+                multiply(2, t0, t0 + BANK, r)
         group_out(0, 0, 512)
         group_out(0, 512, 768)
         quant_out(0, 0, 512)
-        group_out(2, 0, 512)
         group_out(0, 768, 1024)
-        quant_out(2, 0, 512)
         group_out(0, 1024, 1536)
         quant_out(0, 512, 1024)
         group_out(1, 0, 512)
         quant_out(0, 1024, 1536)
         store_codes(0, 1)
-        store_result(2, 1)
+        store_result(2, 0)
         group_out(1, 512, 768)
         quant_out(1, 0, 512)
         group_out(1, 768, 1024)
         group_out(1, 1024, 1536)
         quant_out(1, 512, 1024)
-        group_out(2, 512, 1024)
+        group_out(2, 0, 512)
         quant_out(1, 1024, 1536)
-        group_out(2, 1024, 1152)
-        group_out(2, 1152, 1536, on_scalar)
+        group_out(2, 512, 768)
+        group_out(2, 768, 1024, on_scalar)
+        group_out(2, 1024, 1536, on_scalar)
+        quant_out(2, 0, 512)
         quant_out(2, 512, 1024)
         quant_out(2, 1024, 1536)
         store_codes(1, 3)

@@ -45,6 +45,7 @@ def tile_mix_dyq_fm_pl_none_kernel(tc, dy, w8_words, w8_scales, w4_words, w4_sca
 
         w8_raw = {a0: kept("w8_raw_%d" % a0, [P, (a1 - a0) * SPAN], U32) for a0, a1 in zip(W8_CUTS, W8_CUTS[1:])}
         w4_raw = {a0: kept("w4_raw_%d" % a0, [P, (a1 - a0) * SPAN], U16) for a0, a1 in zip(W4_CUTS, W4_CUTS[1:])}
+        ws_rows = kept("ws_rows", [P, D], U8)
         ws_raw = [kept("ws_raw_%d" % g, [P, D], U8) for g in range(2)]
         w8 = [kept("w8_%d" % a, [P, SPAN], U32) for a in range(N_SPANS)]
         w4 = [kept("w4_%d" % a, [P, 2 * SPAN], U8) for a in range(N_SPANS)]
@@ -75,6 +76,10 @@ def tile_mix_dyq_fm_pl_none_kernel(tc, dy, w8_words, w8_scales, w4_words, w4_sca
             scales = (w8_scales, w4_scales)[g]
             for r in range(r0, r1):
                 nc.sync.dma_start(out=into[r:P:QUADRANT, :].bitcast(I32), in_=scales[0, r:16:4, :].bitcast(I32))
+
+        def settle_scales():
+            for q in range(0, P, QUADRANT):
+                on_vector(out=ws_raw[1][q : q + 4, :].bitcast(I32), in_=ws_rows[q : q + 4, :].bitcast(I32))
 
         def load_w8(part):
             a0, a1 = W8_CUTS[part : part + 2]
@@ -193,81 +198,88 @@ def tile_mix_dyq_fm_pl_none_kernel(tc, dy, w8_words, w8_scales, w4_words, w4_sca
                 )
 
 
-        nc.vector.memset(ws_raw[1][:].bitcast(I32), 0)
         nc.vector.memset(ws_raw[0][:].bitcast(I32), 0)
+        nc.vector.memset(ws_raw[1][:].bitcast(I32), 0)
         load_w4(0)
+        load_scales(1, ws_rows)
         load_dy(1, 0)
-        load_scales(1, ws_raw[1])
-        load_dy(0, 0)
         load_scales(0, ws_raw[0])
+        load_dy(0, 0)
         load_w8(0)
         load_dy(1, 1)
         load_dy(0, 1)
 
         for a in range(N_SPANS):
             deal_w4(a)
+        settle_scales()
+        for a in range(N_SPANS):
+            deal_scales(1, a)
         group_dy(1, 0, 512)
         group_dy(1, 512, 768, on_scalar)
-        deal_scales(1, 0)
+        deal_scales(0, 0)
         quant_dy(1, 0, 512)
-        deal_scales(1, 1)
+        deal_scales(0, 1)
         quant_dy(1, 512, 768)
-        deal_scales(1, 2)
+        deal_scales(0, 2)
         left = [(0, 512, r) for r in range(4)] + [(512, 768, 0), (512, 768, 2)]
         right = [(768, 1024, 0), (768, 1024, 2)] + [(1024, 1536, r) for r in range(4)]
+        narrow = [(t0, t0 + 256, r0) for r0 in (0, 2) for t0 in (768, 1024, 1280)]
         for piece in left:
             passes(1, 0, *piece)
         passes(1, 1, 0, 512, 0)
         passes(1, 1, 0, 512, 1)
 
-        group_dy(0, 0, 512)
+        group_dy(0, 0, 256)
+        group_dy(0, 256, 448)
+        group_dy(0, 448, 512, on_scalar)
         group_dy(0, 512, 768, on_scalar)
-        deal_scales(0, 0)
-        quant_dy(0, 0, 512)
+        quant_dy(0, 0, 256)
+        quant_dy(0, 256, 512)
         deal_w8(0)
         quant_dy(0, 512, 768)
-        deal_scales(0, 1)
         deal_w8(1)
-        deal_scales(0, 2)
-        deal_w8(2)
         for n, piece in enumerate(left):
             passes(0, 0, *piece)
-            drain(0, *piece, on_vector if n in (2, 4) else on_scalar)
+            drain(0, *piece, on_vector if n in (1, 3) else on_scalar)
         store_result(0, 0)
-        group_dy(1, 768, 1024)
-        group_dy(1, 1024, 1536)
-        quant_dy(1, 768, 1024)
-        quant_dy(1, 1024, 1536)
+        deal_w8(2)
         for n, piece in enumerate(left):
             if n > 1:
                 passes(1, 1, *piece)
             passes(0, 1, *piece)
-            drain(1, *piece, on_vector if n in (4,) else on_scalar)
+            drain(1, *piece, on_scalar)
         store_result(1, 0)
-        multiply(2, 0, 512, 0)
-        passes(1, 2, 0, 512, 1)
-        passes(0, 2, 0, 512, 1)
-        for piece in right:
+        group_dy(1, 768, 1024)
+        group_dy(1, 1024, 1536)
+        quant_dy(1, 768, 1024)
+        quant_dy(1, 1024, 1536)
+        for piece in narrow:
             passes(1, 0, *piece)
+        for piece in right[:2]:
+            passes(1, 1, *piece)
+        group_out(0, 0, 256)
         group_dy(0, 768, 1024)
         group_dy(0, 1024, 1280)
         group_dy(0, 1280, 1536, on_scalar)
+        group_out(0, 256, 448, on_scalar)
         quant_dy(0, 768, 1024)
-        quant_dy(0, 1024, 1536)
-        drain(2, 0, 512, 1)
-        multiply(2, 0, 512, 2)
-        for n, piece in enumerate(right):
+        quant_dy(0, 1024, 1280)
+        quant_dy(0, 1280, 1536)
+        for n, piece in enumerate(narrow):
             passes(0, 0, *piece)
-            drain(0, *piece, on_vector if n in (0, 2, 4) else on_scalar)
-        store_result(0, 1)
-        for piece in right:
-            multiply(1, *piece)
+            drain(0, *piece, on_vector if n in (2, 4) else on_scalar)
+            if n % 3 == 2:
+                store_result(0, 1, piece[2], piece[2] + 2)
+        for n, piece in enumerate(right):
+            if n > 1:
+                passes(1, 1, *piece)
+            passes(0, 1, *piece)
+            drain(1, *piece, on_vector if n == 1 else on_scalar)
         store_result(1, 1)
-        multiply(2, 0, 512, 3)
-        for t0 in (512, 1024):
-            for r in range(4):
+        for r in range(4):
+            for t0 in range(0, T, BANK):
                 multiply(2, t0, t0 + BANK, r)
-        group_out(0, 0, 512)
+        group_out(0, 448, 512)
         group_out(0, 512, 768)
         quant_out(0, 0, 512)
         group_out(0, 768, 1024)
@@ -276,7 +288,8 @@ def tile_mix_dyq_fm_pl_none_kernel(tc, dy, w8_words, w8_scales, w4_words, w4_sca
         group_out(1, 0, 512)
         quant_out(0, 1024, 1536)
         store_codes(0, 1)
-        store_result(2, 0)
+        store_result(2, 0, 0, 2)
+        store_result(2, 0, 2, 4)
         group_out(1, 512, 768)
         quant_out(1, 0, 512)
         group_out(1, 768, 1024)
@@ -284,8 +297,8 @@ def tile_mix_dyq_fm_pl_none_kernel(tc, dy, w8_words, w8_scales, w4_words, w4_sca
         quant_out(1, 512, 1024)
         group_out(2, 0, 512)
         quant_out(1, 1024, 1536)
-        group_out(2, 512, 768)
-        group_out(2, 768, 1024, on_scalar)
+        group_out(2, 512, 896)
+        group_out(2, 896, 1024, on_scalar)
         group_out(2, 1024, 1536, on_scalar)
         quant_out(2, 0, 512)
         quant_out(2, 512, 1024)

@@ -25,10 +25,10 @@ QUADRANT = 32
 LINE = 16
 RUN = 4
 STAGED = 6
-DY_CUTS = ((0, 768, T),) * 2
+CUT = 768
+DY_CUTS = ((0, CUT, T),) * 2
 W8_CUTS = (0, 3)
 W4_CUTS = (0, 3)
-OUT_CUTS = ((0, 768, T), (0, 768, T), (0, T))
 
 
 def tile_mix_dyq_fm_pl_none_kernel(tc, dy, w8_words, w8_scales, w4_words, w4_scales, out_0, out_1, out_2):
@@ -50,16 +50,14 @@ def tile_mix_dyq_fm_pl_none_kernel(tc, dy, w8_words, w8_scales, w4_words, w4_sca
         w8 = [kept("w8_%d" % a, [P, SPAN], U32) for a in range(N_SPANS)]
         w4 = [kept("w4_%d" % a, [P, 2 * SPAN], U8) for a in range(N_SPANS)]
         ws = [[kept("ws_%d_%d" % (g, a), [P, SPAN], U8) for a in range(N_SPANS)] for g in range(2)]
-        dy_raw, dy_codes, dy_scales, result = {}, {}, {}, {}
+        dy_raw, dy_codes, dy_scales = {}, {}, {}
         for g in range(2):
             for t0, t1 in zip(DY_CUTS[g], DY_CUTS[g][1:]):
                 dy_raw[g, t0] = kept("dy_raw_%d_%d" % (g, t0), [P, PACK, t1 - t0], F32)
             for c in range(T // BANK):
                 dy_codes[g, c] = kept("dy_codes_%d_%d" % (g, c), [P, BANK], I32)
                 dy_scales[g, c] = kept("dy_scales_%d_%d" % (g, c), [P, BANK], U8)
-        for a in range(N_SPANS):
-            for t0, t1 in zip(OUT_CUTS[a], OUT_CUTS[a][1:]):
-                result[a, t0] = kept("result_%d_%d" % (a, t0), [P, PACK, t1 - t0], F32)
+        result = kept("result", [P, N_SPANS, PACK, T], F32)
         out_codes = kept("out_codes", [P, N_SPANS, T], I32)
         out_scales = kept("out_scales", [P, T], U8)
 
@@ -142,37 +140,44 @@ def tile_mix_dyq_fm_pl_none_kernel(tc, dy, w8_words, w8_scales, w4_words, w4_sca
                 return w8[a][:, r * P : (r + 1) * P].bitcast(E4M3)
             return w4[a][:, 2 * r * P : 2 * (r + 1) * P].bitcast(E2M1)
 
-        def slots_of(r0, t0, t1):
-            return range(r0, r0 + BANK // (t1 - t0))
+        def widths(t0, t1):
+            cuts = [t0]
+            while cuts[-1] < t1:
+                cuts.append(cuts[-1] + max(n for n in (512, 256, 128) if cuts[-1] % n == 0 and cuts[-1] + n <= t1))
+            return list(zip(cuts, cuts[1:]))
 
-        def passes(g, a, t0, t1, r0):
-            opens = (a, t0, r0) not in banks
-            slots = slots_of(r0, t0, t1)
+        def passes(g, a, rows, t0, t1):
+            key = (a, rows, t0)
+            opens = key not in banks
             if opens:
-                banks[a, t0, r0] = psum.tile([P, len(slots), t1 - t0], F32, name="acc")
-            codes, scales = codes_of(g, t0, t1)
-            for r in slots:
+                banks[key] = psum.tile([P, len(rows), t1 - t0], F32, name="acc")
+            todo = [(n, r, u0, u1) for n, r in enumerate(rows) for u0, u1 in widths(t0, t1)]
+            for step in todo:
+                n, r, u0, u1 = step
+                codes, scales = codes_of(g, u0, u1)
                 nc.tensor.matmul_mx(
-                    out=banks[a, t0, r0][:, r - r0, :],
+                    out=banks[key][:, n, u0 - t0 : u1 - t0],
                     lhsT=stationary(g, a, r),
                     lhsT_scale=ws[g][a][:, r * P : (r + 1) * P],
                     rhs=codes,
                     rhs_scale=scales,
-                    start=opens and r == r0,
-                    stop=not opens and r == slots[-1],
+                    start=opens and step == todo[0],
+                    stop=not opens and step == todo[-1],
                 )
 
-        def drain(a, t0, t1, r0, copy=on_scalar):
-            slots = slots_of(r0, t0, t1)
-            copy(out=columns(result, a, OUT_CUTS, t0, t1)[:, slots[0] : slots[-1] + 1, :], in_=banks[a, t0, r0][:])
+        def drain(a, rows, t0, t1, copy=on_scalar):
+            copy(out=result[:, a, rows.start : rows.stop : rows.step, t0:t1], in_=banks[a, rows, t0][:])
 
-        def multiply(a, t0, t1, r0, copy=on_scalar):
-            passes(1, a, t0, t1, r0)
-            passes(0, a, t0, t1, r0)
-            drain(a, t0, t1, r0, copy)
+        def multiply(a, rows, t0, t1, copy=on_scalar):
+            passes(1, a, rows, t0, t1)
+            passes(0, a, rows, t0, t1)
+            drain(a, rows, t0, t1, copy)
+
+        def row(r):
+            return range(r, r + 1)
 
         def group_out(a, t0, t1, copy=on_vector):
-            interleave(("out", a), columns(result, a, OUT_CUTS, t0, t1), copy, t0, t1)
+            interleave(("out", a), result[:, a, :, t0:t1], copy, t0, t1)
 
         def quant_out(a, t0, t1):
             nc.vector.quantize_mx(
@@ -181,10 +186,18 @@ def tile_mix_dyq_fm_pl_none_kernel(tc, dy, w8_words, w8_scales, w4_words, w4_sca
                 in_=staged_columns(("out", a), t0, t1),
             )
 
-        def store_result(a, part, r0=0, r1=PACK):
-            t0, t1 = OUT_CUTS[a][part : part + 2]
+        def store_early(r):
+            rows = out_0.rearrange("(a p r) t -> p a r t", a=N_SPANS, r=PACK)
+            nc.sync.dma_start(out=rows[:, :, r, 0:CUT], in_=result[:, :, r, 0:CUT])
+
+        def store_rows(a, r0, r1, t0, t1):
             rows = out_0[a * SPAN : (a + 1) * SPAN, :].rearrange("(p r) t -> p r t", r=PACK)
-            nc.sync.dma_start(out=rows[:, r0:r1, t0:t1], in_=result[a, t0][:, r0:r1, :])
+            nc.sync.dma_start(out=rows[:, r0:r1, t0:t1], in_=result[:, a, r0:r1, t0:t1])
+
+        def store_rest(a, h0, h1):
+            pairs = out_0[a * SPAN : (a + 1) * SPAN, :].rearrange("(p h e) t -> p h (e t)", h=2, e=2)
+            held = result[:, a, :, :].rearrange("p (h e) t -> p h (e t)", h=2)
+            nc.sync.dma_start(out=pairs[:, h0:h1, CUT : 2 * T], in_=held[:, h0:h1, CUT : 2 * T])
 
         def store_codes(a0, a1):
             words = out_1.rearrange("a p t i -> p a (t i)").bitcast(I32)
@@ -215,84 +228,95 @@ def tile_mix_dyq_fm_pl_none_kernel(tc, dy, w8_words, w8_scales, w4_words, w4_sca
         for a in range(N_SPANS):
             deal_scales(1, a)
         group_dy(1, 0, 512)
-        group_dy(1, 512, 768, on_scalar)
+        group_dy(1, 512, CUT, on_scalar)
         deal_scales(0, 0)
         quant_dy(1, 0, 512)
         deal_scales(0, 1)
-        quant_dy(1, 512, 768)
+        quant_dy(1, 512, CUT)
         deal_scales(0, 2)
-        left = [(0, 512, r) for r in range(4)] + [(512, 768, 0), (512, 768, 2)]
-        right = [(768, 1024, 0), (768, 1024, 2)] + [(1024, 1536, r) for r in range(4)]
-        narrow = [(t0, t0 + 256, r0) for r0 in (0, 2) for t0 in (768, 1024, 1280)]
-        for piece in left:
-            passes(1, 0, *piece)
-        passes(1, 1, 0, 512, 0)
-        passes(1, 1, 0, 512, 1)
+        even, odd = range(0, 4, 2), range(1, 4, 2)
+        early = [(a, rows, t0, t1) for a in range(N_SPANS) for rows, t0, t1 in ((row(0), 0, 512), (even, 512, CUT))]
+        early += [(0, row(2), 0, 512), (0, row(1), 0, 512), (0, odd, 512, CUT), (0, row(3), 0, 512)]
+        early += [(a, row(2), 0, 512) for a in (1, 2)]
+        for piece in early[:8]:
+            passes(1, *piece)
 
         group_dy(0, 0, 256)
         group_dy(0, 256, 448)
         group_dy(0, 448, 512, on_scalar)
-        group_dy(0, 512, 768, on_scalar)
+        group_dy(0, 512, CUT, on_scalar)
         quant_dy(0, 0, 256)
         quant_dy(0, 256, 512)
         deal_w8(0)
-        quant_dy(0, 512, 768)
+        quant_dy(0, 512, CUT)
         deal_w8(1)
-        for n, piece in enumerate(left):
-            passes(0, 0, *piece)
-            drain(0, *piece, on_vector if n in (1, 3) else on_scalar)
-        store_result(0, 0)
         deal_w8(2)
-        for n, piece in enumerate(left):
-            if n > 1:
-                passes(1, 1, *piece)
-            passes(0, 1, *piece)
-            drain(1, *piece, on_scalar)
-        store_result(1, 0)
-        group_dy(1, 768, 1024)
+        for n, piece in enumerate(early):
+            if n >= 8:
+                passes(1, *piece)
+            passes(0, *piece)
+            drain(*piece, on_vector if n in (2, 4) else on_scalar)
+            if n == 5:
+                store_early(0)
+            if n == 8:
+                store_rows(0, 1, 2, 0, CUT)
+        store_early(2)
+        passes(1, 2, row(1), 0, 512)
+        passes(0, 2, row(1), 0, 512)
+        group_dy(1, CUT, 1024)
         group_dy(1, 1024, 1536)
-        quant_dy(1, 768, 1024)
+        quant_dy(1, CUT, 1024)
         quant_dy(1, 1024, 1536)
-        for piece in narrow:
-            passes(1, 0, *piece)
-        for piece in right[:2]:
-            passes(1, 1, *piece)
-        group_out(0, 0, 256)
+        drain(2, row(1), 0, 512, on_vector)
+        upper = [(0, range(0, 2), t0, t1) for t0, t1 in ((768, 1024), (1024, 1280), (1280, 1408), (1408, 1536))]
+        lower = [(0, range(2, 4), t0, t0 + 256) for t0 in (768, 1024, 1280)]
+        for piece in upper + lower:
+            passes(1, *piece)
+        passes(1, 1, even, CUT, 1024)
         group_dy(0, 768, 1024)
-        group_dy(0, 1024, 1280)
-        group_dy(0, 1280, 1536, on_scalar)
-        group_out(0, 256, 448, on_scalar)
+        group_dy(0, 1024, 1216)
+        group_dy(0, 1216, 1280, on_scalar)
+        group_dy(0, 1280, 1408, on_scalar)
+        group_dy(0, 1408, 1536, on_scalar)
+        group_out(0, 0, 128, on_scalar)
         quant_dy(0, 768, 1024)
         quant_dy(0, 1024, 1280)
-        quant_dy(0, 1280, 1536)
-        for n, piece in enumerate(narrow):
-            passes(0, 0, *piece)
-            drain(0, *piece, on_vector if n in (2, 4) else on_scalar)
-            if n % 3 == 2:
-                store_result(0, 1, piece[2], piece[2] + 2)
-        for n, piece in enumerate(right):
-            if n > 1:
-                passes(1, 1, *piece)
-            passes(0, 1, *piece)
-            drain(1, *piece, on_vector if n == 1 else on_scalar)
-        store_result(1, 1)
-        for r in range(4):
-            for t0 in range(0, T, BANK):
-                multiply(2, t0, t0 + BANK, r)
-        group_out(0, 448, 512)
-        group_out(0, 512, 768)
+        quant_dy(0, 1280, 1408)
+        quant_dy(0, 1408, 1536)
+        for n, piece in enumerate(upper):
+            passes(0, *piece)
+            drain(*piece, on_vector if n % 2 else on_scalar)
+        store_rows(0, 0, 2, CUT, T)
+        for n, piece in enumerate(lower):
+            passes(0, *piece)
+            drain(*piece, on_vector if n == 1 else on_scalar)
+        store_rest(0, 1, 2)
+
+        def rest_of(a, r, first=0):
+            multiply(a, row(r), 1024, 1536)
+            for t0 in range(first, T, BANK):
+                multiply(a, row(r + 1), t0, t0 + BANK)
+
+        passes(0, 1, even, CUT, 1024)
+        drain(1, even, CUT, 1024)
+        rest_of(1, 0)
+        store_rest(1, 0, 1)
+        rest_of(1, 2)
+        store_rest(1, 1, 2)
+        multiply(2, even, CUT, 1024)
+        rest_of(2, 0, BANK)
+        rest_of(2, 2)
+        group_out(0, 128, 512)
+        group_out(0, 512, 1024)
         quant_out(0, 0, 512)
-        group_out(0, 768, 1024)
         group_out(0, 1024, 1536)
         quant_out(0, 512, 1024)
         group_out(1, 0, 512)
         quant_out(0, 1024, 1536)
         store_codes(0, 1)
-        store_result(2, 0, 0, 2)
-        store_result(2, 0, 2, 4)
-        group_out(1, 512, 768)
+        store_rest(2, 0, 2)
+        group_out(1, 512, 1024)
         quant_out(1, 0, 512)
-        group_out(1, 768, 1024)
         group_out(1, 1024, 1536)
         quant_out(1, 512, 1024)
         group_out(2, 0, 512)

from contextlib import ExitStack

import concourse.mybir as mybir

K, D, T = 1024, 1536, 1536
FLOPS = 2 * K * D * T

F32 = mybir.dt.float32
BF16 = mybir.dt.bfloat16
I32 = mybir.dt.int32
U32 = mybir.dt.uint32
U16 = mybir.dt.uint16
U8 = mybir.dt.uint8
E4M3 = mybir.dt.float8_e4m3fn_x4
E5M2 = mybir.dt.float8_e5m2_x4
E2M1 = mybir.dt.float4_e2m1fn_x4

P = 128
PACK = 4
SPAN = P * PACK
N_SPANS = D // SPAN
BANK = 512
ALIGN = 256
QUADRANT = 32
LINE = 16
RUN = 4
STAGED = 6
CUT = 768
DY_CUTS = ((0, CUT, T),) * 2
W8_CUTS = (0, 3)
W4_CUTS = (0, 3)


def tile_mix_dyq_fm_pl_none_kernel(tc, dy, w8_words, w8_scales, w4_words, w4_scales, out_0, out_1, out_2):
    nc = tc.nc
    with ExitStack() as ctx:
        keep = ctx.enter_context(tc.tile_pool(name="keep", bufs=1))
        stage = ctx.enter_context(tc.tile_pool(name="stage", bufs=STAGED))
        psum = ctx.enter_context(tc.psum_pool(name="psum", bufs=8))
        ctx.enter_context(tc.manual_schedule())
        on_vector, on_scalar = nc.vector.tensor_copy, nc.scalar.copy

        def kept(name, shape, dtype):
            return keep.tile(shape, dtype, name=name, align_bytes=ALIGN)

        w8_raw = {a0: kept("w8_raw_%d" % a0, [P, (a1 - a0) * SPAN], U32) for a0, a1 in zip(W8_CUTS, W8_CUTS[1:])}
        w4_raw = {a0: kept("w4_raw_%d" % a0, [P, (a1 - a0) * SPAN], U16) for a0, a1 in zip(W4_CUTS, W4_CUTS[1:])}
        ws_rows = kept("ws_rows", [P, D], U8)
        ws_raw = [kept("ws_raw_%d" % g, [P, D], U8) for g in range(2)]
        w8 = [kept("w8_%d" % a, [P, SPAN], U32) for a in range(N_SPANS)]
        w4 = [kept("w4_%d" % a, [P, 2 * SPAN], U8) for a in range(N_SPANS)]
        ws = [[kept("ws_%d_%d" % (g, a), [P, SPAN], U8) for a in range(N_SPANS)] for g in range(2)]
        dy_raw, dy_codes, dy_scales = {}, {}, {}
        for g in range(2):
            for t0, t1 in zip(DY_CUTS[g], DY_CUTS[g][1:]):
                dy_raw[g, t0] = kept("dy_raw_%d_%d" % (g, t0), [P, PACK, t1 - t0], F32)
            for c in range(T // BANK):
                dy_codes[g, c] = kept("dy_codes_%d_%d" % (g, c), [P, BANK], I32)
                dy_scales[g, c] = kept("dy_scales_%d_%d" % (g, c), [P, BANK], U8)
        result = kept("result", [P, N_SPANS, PACK, T], F32)
        out_codes = kept("out_codes", [P, N_SPANS, T], I32)
        out_scales = kept("out_scales", [P, T], U8)

        def columns(tiles, index, cuts, t0, t1):
            first = max(cut for cut in cuts[index] if cut <= t0)
            return tiles[index, first][:, :, t0 - first : t1 - first]

        def load_dy(g, part):
            t0, t1 = DY_CUTS[g][part : part + 2]
            rows = dy[g * SPAN : (g + 1) * SPAN, t0:t1]
            nc.sync.dma_start(out=dy_raw[g, t0][:], in_=rows.rearrange("(p j) t -> p j t", j=PACK))

        def load_scales(g, into, r0=0, r1=4):
            scales = (w8_scales, w4_scales)[g]
            for r in range(r0, r1):
                nc.sync.dma_start(out=into[r:P:QUADRANT, :].bitcast(I32), in_=scales[0, r:16:4, :].bitcast(I32))

        def settle_scales():
            for q in range(0, P, QUADRANT):
                on_vector(out=ws_raw[1][q : q + 4, :].bitcast(I32), in_=ws_rows[q : q + 4, :].bitcast(I32))

        def load_w8(part):
            a0, a1 = W8_CUTS[part : part + 2]
            words = w8_words[0].rearrange("p d i -> p (d i)").bitcast(I32)
            nc.sync.dma_start(out=w8_raw[a0][:].bitcast(I32), in_=words[:, a0 * SPAN : a1 * SPAN])

        def load_w4(part):
            a0, a1 = W4_CUTS[part : part + 2]
            words = w4_words[0].bitcast(I32)
            nc.sync.dma_start(out=w4_raw[a0][:].bitcast(I32), in_=words[:, a0 * SPAN // 2 : a1 * SPAN // 2])

        def deal(copy, out, raw, a, per_line, r0=0, r1=PACK):
            copy(
                out=out.rearrange("p (r c i) -> p c r i", r=PACK, i=per_line)[:, :, r0:r1, :],
                in_=raw[:, a * SPAN : (a + 1) * SPAN].rearrange("p (c i r) -> p c r i", r=PACK, i=per_line)[:, :, r0:r1, :],
            )

        def deal_w8(a, copy=on_vector, r0=0, r1=PACK):
            first = max(cut for cut in W8_CUTS if cut <= a)
            deal(copy, w8[a][:], w8_raw[first], a - first, LINE // 4, r0, r1)

        def deal_w4(a, copy=on_vector, r0=0, r1=PACK):
            first = max(cut for cut in W4_CUTS if cut <= a)
            deal(copy, w4[a][:].bitcast(U16), w4_raw[first], a - first, LINE // 2, r0, r1)

        def deal_scales(g, a):
            deal(on_vector, ws[g][a][:], ws_raw[g], a, LINE)

        staged = {}

        def interleave(key, src, copy, t0, t1):
            c = t0 // BANK
            if (key, c) not in staged:
                staged[key, c] = stage.tile([P, BANK, PACK], BF16, name="staged", align_bytes=ALIGN)
            copy(
                out=staged[key, c][:, t0 - c * BANK : t1 - c * BANK, :].rearrange("p (c i) j -> p c j i", i=RUN),
                in_=src.rearrange("p j (c i) -> p c j i", i=RUN),
            )

        def staged_columns(key, t0, t1):
            c = t0 // BANK
            return staged[key, c][:, t0 - c * BANK : t1 - c * BANK, :].rearrange("p t j -> p (t j)")

        def group_dy(g, t0, t1, copy=on_vector):
            interleave(("dy", g), columns(dy_raw, g, DY_CUTS, t0, t1), copy, t0, t1)

        def codes_of(g, t0, t1):
            c = t0 // BANK
            cols = slice(t0 - c * BANK, t1 - c * BANK)
            return dy_codes[g, c][:, cols].bitcast(E5M2), dy_scales[g, c][:, cols]

        def quant_dy(g, t0, t1):
            codes, scales = codes_of(g, t0, t1)
            nc.vector.quantize_mx(out=codes, scales=scales, in_=staged_columns(("dy", g), t0, t1))

        banks = {}

        def stationary(g, a, r):
            if g == 0:
                return w8[a][:, r * P : (r + 1) * P].bitcast(E4M3)
            return w4[a][:, 2 * r * P : 2 * (r + 1) * P].bitcast(E2M1)

        def widths(t0, t1):
            cuts = [t0]
            while cuts[-1] < t1:
                cuts.append(cuts[-1] + max(n for n in (512, 256, 128) if cuts[-1] % n == 0 and cuts[-1] + n <= t1))
            return list(zip(cuts, cuts[1:]))

        def passes(g, a, rows, t0, t1):
            key = (a, rows, t0)
            opens = key not in banks
            if opens:
                banks[key] = psum.tile([P, len(rows), t1 - t0], F32, name="acc")
            todo = [(n, r, u0, u1) for n, r in enumerate(rows) for u0, u1 in widths(t0, t1)]
            for step in todo:
                n, r, u0, u1 = step
                codes, scales = codes_of(g, u0, u1)
                nc.tensor.matmul_mx(
                    out=banks[key][:, n, u0 - t0 : u1 - t0],
                    lhsT=stationary(g, a, r),
                    lhsT_scale=ws[g][a][:, r * P : (r + 1) * P],
                    rhs=codes,
                    rhs_scale=scales,
                    start=opens and step == todo[0],
                    stop=not opens and step == todo[-1],
                )

        def drain(a, rows, t0, t1, copy=on_scalar):
            copy(out=result[:, a, rows.start : rows.stop : rows.step, t0:t1], in_=banks[a, rows, t0][:])

        def multiply(a, rows, t0, t1, copy=on_scalar):
            passes(1, a, rows, t0, t1)
            passes(0, a, rows, t0, t1)
            drain(a, rows, t0, t1, copy)

        def row(r):
            return range(r, r + 1)

        def group_out(a, t0, t1, copy=on_vector):
            interleave(("out", a), result[:, a, :, t0:t1], copy, t0, t1)

        def quant_out(a, t0, t1):
            nc.vector.quantize_mx(
                out=out_codes[:, a, t0:t1].bitcast(E4M3),
                scales=out_scales[4 * (a + 1) : P, t0:t1],
                in_=staged_columns(("out", a), t0, t1),
            )

        def store_early(r):
            rows = out_0.rearrange("(a p r) t -> p a r t", a=N_SPANS, r=PACK)
            nc.sync.dma_start(out=rows[:, :, r, 0:CUT], in_=result[:, :, r, 0:CUT])

        def store_rows(a, r0, r1, t0, t1):
            rows = out_0[a * SPAN : (a + 1) * SPAN, :].rearrange("(p r) t -> p r t", r=PACK)
            nc.sync.dma_start(out=rows[:, r0:r1, t0:t1], in_=result[:, a, r0:r1, t0:t1])

        def store_rest(a, h0, h1):
            pairs = out_0[a * SPAN : (a + 1) * SPAN, :].rearrange("(p h e) t -> p h (e t)", h=2, e=2)
            held = result[:, a, :, :].rearrange("p (h e) t -> p h (e t)", h=2)
            nc.sync.dma_start(out=pairs[:, h0:h1, CUT : 2 * T], in_=held[:, h0:h1, CUT : 2 * T])

        def store_codes(a0, a1):
            words = out_1.rearrange("a p t i -> p a (t i)").bitcast(I32)
            nc.sync.dma_start(out=words[:, a0:a1, :], in_=out_codes[:, a0:a1, :])

        def store_scales():
            for q in range(P // QUADRANT):
                nc.sync.dma_start(
                    out=out_2[:, 4 * q : 4 * q + 4, :].bitcast(I32),
                    in_=out_scales[QUADRANT * q + 4 : QUADRANT * q + 16, :].bitcast(I32),
                )


        nc.vector.memset(ws_raw[0][:].bitcast(I32), 0)
        nc.vector.memset(ws_raw[1][:].bitcast(I32), 0)
        load_w4(0)
        load_scales(1, ws_rows)
        load_dy(1, 0)
        load_scales(0, ws_raw[0])
        load_dy(0, 0)
        load_w8(0)
        load_dy(1, 1)
        load_dy(0, 1)

        for a in range(N_SPANS):
            deal_w4(a)
        settle_scales()
        for a in range(N_SPANS):
            deal_scales(1, a)
        group_dy(1, 0, 512)
        group_dy(1, 512, CUT, on_scalar)
        deal_scales(0, 0)
        quant_dy(1, 0, 512)
        deal_scales(0, 1)
        quant_dy(1, 512, CUT)
        deal_scales(0, 2)
        even, odd = range(0, 4, 2), range(1, 4, 2)
        early = [(a, rows, t0, t1) for a in range(N_SPANS) for rows, t0, t1 in ((row(0), 0, 512), (even, 512, CUT))]
        early += [(0, row(2), 0, 512), (0, row(1), 0, 512), (0, odd, 512, CUT), (0, row(3), 0, 512)]
        early += [(a, row(2), 0, 512) for a in (1, 2)]
        for piece in early[:8]:
            passes(1, *piece)

        group_dy(0, 0, 256)
        group_dy(0, 256, 448)
        group_dy(0, 448, 512, on_scalar)
        group_dy(0, 512, CUT, on_scalar)
        quant_dy(0, 0, 256)
        quant_dy(0, 256, 512)
        deal_w8(0)
        quant_dy(0, 512, CUT)
        deal_w8(1)
        deal_w8(2)
        for n, piece in enumerate(early):
            if n >= 8:
                passes(1, *piece)
            passes(0, *piece)
            drain(*piece, on_vector if n in (2, 4) else on_scalar)
            if n == 5:
                store_early(0)
            if n == 8:
                store_rows(0, 1, 2, 0, CUT)
        store_early(2)
        passes(1, 2, row(1), 0, 512)
        passes(0, 2, row(1), 0, 512)
        group_dy(1, CUT, 1024)
        group_dy(1, 1024, 1536)
        quant_dy(1, CUT, 1024)
        quant_dy(1, 1024, 1536)
        drain(2, row(1), 0, 512, on_vector)
        upper = [(0, range(0, 2), t0, t1) for t0, t1 in ((768, 1024), (1024, 1280), (1280, 1408), (1408, 1536))]
        lower = [(0, range(2, 4), t0, t0 + 256) for t0 in (768, 1024, 1280)]
        for piece in upper + lower:
            passes(1, *piece)
        passes(1, 1, even, CUT, 1024)
        group_dy(0, 768, 1024)
        group_dy(0, 1024, 1216)
        group_dy(0, 1216, 1280, on_scalar)
        group_dy(0, 1280, 1408, on_scalar)
        group_dy(0, 1408, 1536, on_scalar)
        group_out(0, 0, 128, on_scalar)
        quant_dy(0, 768, 1024)
        quant_dy(0, 1024, 1280)
        quant_dy(0, 1280, 1408)
        quant_dy(0, 1408, 1536)
        for n, piece in enumerate(upper):
            passes(0, *piece)
            drain(*piece, on_vector if n % 2 else on_scalar)
        store_rows(0, 0, 2, CUT, T)
        for n, piece in enumerate(lower):
            passes(0, *piece)
            drain(*piece, on_vector if n == 1 else on_scalar)
        store_rest(0, 1, 2)

        def rest_of(a, r, first=0):
            multiply(a, row(r), 1024, 1536)
            for t0 in range(first, T, BANK):
                multiply(a, row(r + 1), t0, t0 + BANK)

        passes(0, 1, even, CUT, 1024)
        drain(1, even, CUT, 1024)
        rest_of(1, 0)
        store_rest(1, 0, 1)
        rest_of(1, 2)
        store_rest(1, 1, 2)
        multiply(2, even, CUT, 1024)
        rest_of(2, 0, BANK)
        rest_of(2, 2)
        group_out(0, 128, 512)
        group_out(0, 512, 1024)
        quant_out(0, 0, 512)
        group_out(0, 1024, 1536)
        quant_out(0, 512, 1024)
        group_out(1, 0, 512)
        quant_out(0, 1024, 1536)
        store_codes(0, 1)
        store_rest(2, 0, 2)
        group_out(1, 512, 1024)
        quant_out(1, 0, 512)
        group_out(1, 1024, 1536)
        quant_out(1, 512, 1024)
        group_out(2, 0, 512)
        quant_out(1, 1024, 1536)
        group_out(2, 512, 896)
        group_out(2, 896, 1024, on_scalar)
        group_out(2, 1024, 1536, on_scalar)
        quant_out(2, 0, 512)
        quant_out(2, 512, 1024)
        quant_out(2, 1024, 1536)
        store_codes(1, 3)
        store_scales()
